import numpy as np
import ml_dtypes


def mxq(x, axis, fmt="e4m3"):
    dtype, down = {"e4m3": (ml_dtypes.float8_e4m3fn, 7), "e5m2": (ml_dtypes.float8_e5m2, 14)}[fmt]
    v = np.moveaxis(np.asarray(x, np.float32).astype(ml_dtypes.bfloat16).astype(np.float64), axis, -1)
    blocks = v.reshape(v.shape[:-1] + (-1, 32))
    amax = np.abs(blocks).max(-1, keepdims=True)
    byte = np.maximum(np.where(amax > 0, np.frexp(amax)[1] - 1 + 127, 0) - down, 1)
    scale = np.exp2(byte - 127.0)
    codes = (blocks / scale).astype(np.float32).astype(dtype).astype(np.float64)
    return np.moveaxis((codes * scale).reshape(v.shape), -1, axis)


WIDE = False


def mx_kscale(k):
    if not WIDE:
        return np.ones(k)
    levels = np.array([10, -10, 5, -5, 0])
    if k % 512:
        return np.exp2(np.random.permutation(np.resize(levels, k // 32))).repeat(32)
    a = np.empty((k // 512, 16))
    for p in range(k // 512):
        a[p, :8] = np.random.permutation(np.resize(levels, 8))
        for g in range(8):
            far = levels[np.abs(levels - a[p, g]) >= 10]
            a[p, g + 8] = far[np.random.randint(len(far))]
    return np.exp2(a.ravel()).repeat(32)


def f64(x):
    return np.asarray(x).astype(np.float64)


def striped(idx):
    return np.tile(idx.reshape(-1, 16).T, (8, 1)).astype(np.uint16)


def unstriped(offs):
    return offs[:16].T.reshape(-1).astype(np.int64)


E2M1 = np.array([0.0, 0.5, 1.0, 1.5, 2.0, 3.0, 4.0, 6.0, -0.0, -0.5, -1.0, -1.5, -2.0, -3.0, -4.0, -6.0])


def pack_weight(w, fmt):
    k, n = w.shape
    w = f64(np.asarray(w, np.float32).astype(ml_dtypes.bfloat16)).reshape(k // 32, 32, n)
    amax = np.abs(w).max(1)
    if fmt == "e4m3":
        byte = np.frexp(amax)[1] - 1 + 127 - 7
    else:
        mant, ex = np.frexp(amax / 6.0)
        byte = np.where(mant > 0.5, ex, ex - 1) + 127
    byte = np.clip(np.where(amax > 0, byte, 1), 1, 254)
    scaled = (w * np.exp2(127.0 - byte)[:, None, :]).reshape(k, n).astype(np.float32)
    by_word = np.ascontiguousarray(scaled.reshape(k // 512, 128, 4, n).transpose(0, 1, 3, 2))
    if fmt == "e4m3":
        words = by_word.astype(ml_dtypes.float8_e4m3fn).view(np.uint8)
    else:
        c = by_word.astype(ml_dtypes.float4_e2m1fn).view(np.uint8) & 0xF
        words = (c[..., 0::2] | (c[..., 1::2] << 4)).reshape(k // 512, 128, 2 * n)
    return np.ascontiguousarray(words), np.ascontiguousarray(byte.astype(np.uint8).reshape(k // 512, 16, n))


def unpack_weight(words, scales, fmt):
    g, _, n = scales.shape
    words = np.ascontiguousarray(words).reshape(g, 128, n, -1)
    if fmt == "e4m3":
        vals = words.view(ml_dtypes.float8_e4m3fn).astype(np.float64)
    else:
        nib = np.empty((g, 128, n, 4), np.uint8)
        nib[..., 0::2] = words & 0xF
        nib[..., 1::2] = words >> 4
        vals = E2M1[nib]
    vals = vals * np.repeat(np.exp2(scales.astype(np.float64) - 127.0), 8, axis=1)[..., None]
    return vals.transpose(0, 1, 3, 2).reshape(g * 512, n)


def gelu(v):
    return 0.5 * v * (1.0 + np.tanh(np.sqrt(2.0 / np.pi) * (v + 0.044715 * v**3)))


def often(T, S):
    return np.random.permutation(T)[(T * np.random.uniform(0, 1, S) ** 4).astype(np.int64)]


def bf(x):
    return np.asarray(x, np.float32).astype(ml_dtypes.bfloat16)


def planes(Y):
    n, m = Y.shape
    b = f64(bf(Y)).reshape(n // 32, 32, m)
    amax = np.abs(b).max(1)
    byte = np.clip(np.where(amax > 0, np.frexp(amax)[1] - 1 + 127 - 7, 1), 1, 254)
    codes = (b * np.exp2(127.0 - byte)[:, None, :]).reshape(n, m).astype(np.float32).astype(ml_dtypes.float8_e4m3fn).view(np.uint8)
    words = codes.reshape(n // 512, 128, 4, m).transpose(0, 1, 3, 2)
    return np.ascontiguousarray(words), np.ascontiguousarray(byte.astype(np.uint8).reshape(n // 512, 16, m))


K, T, S, T2, P, H, N = 1024, 2048, 1024, 2048, 512, 1024, 512

def setup_inputs():
    n = np.random.standard_normal
    s = mx_kscale(K)[:, None]
    u = mx_kscale(H)[:, None]
    tab_words, tab_scales = pack_weight(n((K, T)) * s, "e4m3")
    tab2_words, tab2_scales = pack_weight(n((K, T2)) * s, "e4m3")
    wg_words, wg_scales = pack_weight(1.5 * n((K, H)) / np.sqrt(K) / s, "e2m1")
    wc_words, wc_scales = pack_weight(n((K, H)) / np.sqrt(K) / s * u.T, "e4m3")
    wa = n((K, H)) / np.sqrt(K) / s * u.T
    wo = n((H, N)) / np.sqrt(H) * np.exp(0.8 * n((1, N))) / u
    return {
        "tab_words": tab_words, "tab_scales": tab_scales,
        "offs": striped(np.random.permutation(T)[:S]),
        "pos1": striped(often(S, P)),
        "tab2_words": tab2_words, "tab2_scales": tab2_scales,
        "offs2": striped(np.random.permutation(T2)[:P]),
        "wa": wa.astype(np.float32),
        "wg_words": wg_words, "wg_scales": wg_scales,
        "wc_words": wc_words, "wc_scales": wc_scales,
        "wo": wo.astype(np.float32),
    }

def reference(tab_words, tab_scales, offs, pos1, tab2_words, tab2_scales, offs2,
              wa, wg_words, wg_scales, wc_words, wc_scales, wo):
    v = unpack_weight(tab_words, tab_scales, "e4m3")[:, unstriped(offs)]
    v2 = unpack_weight(tab2_words, tab2_scales, "e4m3")[:, unstriped(offs2)]
    a = mxq(f64(wa), 0, "e4m3").T @ v
    g = unpack_weight(wg_words, wg_scales, "e2m1").T @ v2
    c = unpack_weight(wc_words, wc_scales, "e4m3").T @ v2
    z = g / (1.0 + np.exp(-g)) * c - a[:, unstriped(pos1)]
    y = mxq(f64(wo), 0, "e4m3").T @ mxq(z, 0, "e4m3")
    words, scales = planes(y)
    return y, words, scales

@@ -1,0 +1,293 @@
+from contextlib import ExitStack
+
+import concourse.mybir as mybir
+
+K, T, S, M, H, N = 1024, 2048, 1024, 512, 1024, 512
+FLOPS = 2 * K * H * S + 2 * 2 * K * H * M + 2 * H * N * M
+
+F32 = mybir.dt.float32
+BF16 = mybir.dt.bfloat16
+I32 = mybir.dt.int32
+U32 = mybir.dt.uint32
+U16 = mybir.dt.uint16
+U8 = mybir.dt.uint8
+FP8X4 = mybir.dt.float8_e4m3fn_x4
+FP4X4 = mybir.dt.float4_e2m1fn_x4
+MULT = mybir.AluOpType.mult
+SUB = mybir.AluOpType.subtract
+SILU = mybir.ActivationFunctionType.Silu
+
+P = 128
+PACK = 4
+PASS = P * PACK
+BANK = 512
+PIECE = 128
+
+
+def tile_list_expense_overspend_signals_kernel(
+    tc, tab_words, tab_scales, offs, pos1, tab2_words, tab2_scales, offs2,
+    wa, wg_words, wg_scales, wc_words, wc_scales, wo, out_0, out_1, out_2,
+):
+    nc = tc.nc
+    with ExitStack() as ctx:
+        lists = ctx.enter_context(tc.tile_pool(name="lists", bufs=1))
+        keep = ctx.enter_context(tc.tile_pool(name="keep", bufs=1))
+        raws = ctx.enter_context(tc.tile_pool(name="raws", bufs=4))
+        rounded = ctx.enter_context(tc.tile_pool(name="rounded", bufs=3))
+        a_rows = ctx.enter_context(tc.tile_pool(name="a_rows", bufs=4))
+        gates = ctx.enter_context(tc.tile_pool(name="gates", bufs=3))
+        psum = ctx.enter_context(tc.psum_pool(name="psum", bufs=8))
+
+        def kept(name, shape, dtype):
+            return keep.tile(shape, dtype, name=name, align_bytes=64)
+
+        idx = lists.tile([P, S // 16], U16, name="idx")
+        idx2 = lists.tile([P, M // 16], U16, name="idx2")
+        heads = lists.tile([P, M // 16], U16, name="heads")
+        tab_s = kept("tab_s", [P, T], U8)
+        tab2_s = kept("tab2_s", [P, T], U8)
+        gc_s_raw = kept("gc_s_raw", [P, 2 * H], U8)
+        v2_s_up = kept("v2_s_up", [P, M], U8)
+        nc.vector.memset(tab_s[:].bitcast(I32), 0)
+        nc.gpsimd.memset(tab2_s[:].bitcast(I32), 0)
+        nc.gpsimd.memset(gc_s_raw[:].bitcast(I32), 0)
+        nc.gpsimd.memset(v2_s_up[:].bitcast(I32), 0)
+
+        nc.sync.dma_start(idx[:], offs)
+        for q in range(4):
+            nc.scalar.dma_start(tab_s[32 * q : 32 * q + 8, :].bitcast(I32), tab_scales[:, 4 * q : 4 * q + 4, :].bitcast(I32))
+
+        def load_tab2_scales():
+            for q in range(4):
+                nc.sync.dma_start(tab2_s[32 * q : 32 * q + 8, :].bitcast(I32), tab2_scales[:, 4 * q : 4 * q + 4, :].bitcast(I32))
+
+        def load_weight_scales(first, scales):
+            for q in range(4):
+                rows = gc_s_raw[32 * q + first : 32 * q + first + 4, :].bitcast(I32)
+                nc.sync.dma_start(
+                    rows.rearrange("r (a e) -> r a e", a=2),
+                    scales[:, 4 * q : 4 * q + 4, :].bitcast(I32).rearrange("a r e -> r a e"),
+                )
+
+        def load_table(words, a, name):
+            tile = kept(name, [P, T], U32)
+            nc.sync.dma_start(tile[:].bitcast(I32), words[a].rearrange("p t i -> p (t i)").bitcast(I32))
+            return tile
+
+        def load_wa(a, b):
+            raw = raws.tile([P, PACK, PASS], F32, name="raw")
+            rows = wa[a * PASS : (a + 1) * PASS, b * PASS : (b + 1) * PASS]
+            nc.sync.dma_start(raw[:], rows.rearrange("(p i) r -> p i r", i=PACK))
+            return raw
+
+        def load_wo(b):
+            raw = raws.tile([P, PACK, N], F32, name="raw")
+            rows = wo[b * PASS : (b + 1) * PASS, :].rearrange("(g t j) n -> t g j n", t=4, j=4)
+            for t in range(4):
+                nc.sync.dma_start(raw[:, t, :], rows[t])
+            return raw
+
+        def load_gc(b):
+            g_raw = kept("g_raw%d" % b, [P, 2, PASS // 2], I32)
+            c_raw = kept("c_raw%d" % b, [P, 2, PASS], I32)
+            g_src = wg_words.bitcast(I32)[:, :, b * PASS // 2 : (b + 1) * PASS // 2]
+            c_src = wc_words.rearrange("a p e i -> a p (e i)").bitcast(I32)[:, :, b * PASS : (b + 1) * PASS]
+            nc.sync.dma_start(g_raw[:], g_src.rearrange("a p e -> p a e"))
+            nc.sync.dma_start(c_raw[:], c_src.rearrange("a p e -> p a e"))
+            return g_raw, c_raw
+
+        tab_w, tab2_w, wa_raw, gc_raw = {}, {}, {}, {}
+        tab_w[0] = load_table(tab_words, 0, "tab_w0")
+        nc.sync.dma_start(idx2[:], offs2)
+        wa_raw[0, 0] = load_wa(0, 0)
+        tab_w[1] = load_table(tab_words, 1, "tab_w1")
+        wa_raw[1, 0] = load_wa(1, 0)
+        nc.sync.dma_start(heads[:], pos1)
+        tab2_w[0] = load_table(tab2_words, 0, "tab2_w0")
+        load_tab2_scales()
+        wa_raw[0, 1] = load_wa(0, 1)
+        load_weight_scales(0, wg_scales)
+        wa_raw[1, 1] = load_wa(1, 1)
+        load_weight_scales(4, wc_scales)
+        tab2_w[1] = load_table(tab2_words, 1, "tab2_w1")
+        gc_raw[0] = load_gc(0)
+        gc_raw[1] = load_gc(1)
+
+        def gather(name, width, dtype, window, offsets):
+            picked = kept(name, [P, width], dtype)
+            nc.vector.tensor_copy(picked[:], window[:].indirect(offsets[:]))
+            return picked
+
+        def quantise(name, src):
+            codes = kept(name + "_w", [P, PASS], U32)
+            scales = kept(name + "_s", [P, PASS], U8)
+            nc.vector.quantize_mx(out=codes[:].bitcast(FP8X4), scales=scales[:], in_=src[:])
+            return codes, scales
+
+        def round_wa(a, b, vector_share):
+            bf = rounded.tile([P, PACK * PASS], BF16, name="bf", align_bytes=64)
+            dst = bf[:].rearrange("p (t g j i) -> p t g i j", t=4, j=4, i=PACK)
+            src = wa_raw[a, b][:].rearrange("p i (g t j) -> p t g i j", t=4, j=4)
+            cut = 4 - vector_share
+            nc.scalar.copy(dst[:, :cut], src[:, :cut])
+            if vector_share:
+                nc.vector.tensor_copy(dst[:, cut:], src[:, cut:])
+            return bf
+
+        def round_wo(raw):
+            bf = rounded.tile([P, PACK * N], BF16, name="bf", align_bytes=64)
+            nc.scalar.copy(
+                bf[:].rearrange("p (u c t) -> p c t u", u=4, t=4),
+                raw[:].rearrange("p t (c u) -> p c t u", u=4),
+            )
+            return bf
+
+        def deal_gc(b):
+            g_raw, c_raw = gc_raw[b]
+            g_w = kept("g_w%d" % b, [P, 2, PASS // 2], I32)
+            c_w = kept("c_w%d" % b, [P, 2, PASS], I32)
+            nc.vector.tensor_copy(
+                g_w[:].rearrange("p a (t g j) -> p a g t j", t=4, j=2),
+                g_raw[:].rearrange("p a (g t j) -> p a g t j", t=4, j=2),
+            )
+            nc.vector.tensor_copy(
+                c_w[:].rearrange("p a (t g j) -> p a g t j", t=4, j=4),
+                c_raw[:].rearrange("p a (g t j) -> p a g t j", t=4, j=4),
+            )
+            return g_w, c_w
+
+        def a_pass(acc, a, t, h):
+            codes, scales = wa_q[a]
+            cols, picked = slice(t * P, (t + 1) * P), slice(h * BANK, (h + 1) * BANK)
+            nc.tensor.matmul_mx(
+                out=acc[:], lhsT=codes[:, cols].bitcast(FP8X4), lhsT_scale=scales[:, cols],
+                rhs=v_w[a][:, picked].bitcast(FP8X4), rhs_scale=v_s[4 * a :, picked],
+                start=(a == 0), stop=(a == 1),
+            )
+
+        def pick_heads(accs, a_picked, t):
+            row = a_rows.tile([P, S], F32, name="row")
+            for h in range(2):
+                nc.scalar.copy(row[:, h * BANK : (h + 1) * BANK], accs[h][:])
+            nc.vector.tensor_copy(a_picked[:, t, :], row[:].indirect(heads[:]))
+
+        def gated(b, t, g_w, c_w, sc):
+            g_acc = psum.tile([P, BANK], F32, name="acc")
+            c_acc = psum.tile([P, BANK], F32, name="acc")
+            for a in range(2):
+                cols = slice(a * H + b * PASS + t * P, a * H + b * PASS + (t + 1) * P)
+                nc.tensor.matmul_mx(
+                    out=g_acc[:], lhsT=g_w[:, a, t * P // 2 : (t + 1) * P // 2].bitcast(FP4X4), lhsT_scale=gc_s[:, cols],
+                    rhs=v2_w[a][:].bitcast(FP8X4), rhs_scale=(v2_s, v2_s_up)[a][:],
+                    start=(a == 0), stop=(a == 1),
+                )
+            for a in range(2):
+                cols = slice(a * H + b * PASS + t * P, a * H + b * PASS + (t + 1) * P)
+                nc.tensor.matmul_mx(
+                    out=c_acc[:], lhsT=c_w[:, a, t * P : (t + 1) * P].bitcast(FP8X4), lhsT_scale=gc_s[4:, cols],
+                    rhs=v2_w[a][:].bitcast(FP8X4), rhs_scale=v2_s[4 * a :, :],
+                    start=(a == 0), stop=(a == 1),
+                )
+            gate = gates.tile([P, M], F32, name="gate")
+            nc.scalar.activation(gate[:], g_acc[:], SILU)
+            nc.vector.tensor_tensor(sc[:, t, :], c_acc[:], gate[:], MULT)
+
+        def in_fours(planes, lo, hi):
+            return planes[:, :, lo:hi].rearrange("p t (c i) -> p c t i", i=4)
+
+        def woven(bf, lo, hi):
+            return bf[:, PACK * lo : PACK * hi].rearrange("p (c i t) -> p c t i", i=4, t=PACK)
+
+        def quantise_cols(codes, scales, bf, lo, hi):
+            nc.vector.quantize_mx(out=codes[:, lo:hi].bitcast(FP8X4), scales=scales[:, lo:hi], in_=bf[:, PACK * lo : PACK * hi])
+
+        v_w, v2_w, wa_q = {}, {}, {}
+        v_s = gather("v_s", S, U8, tab_s, idx)
+        v_w[0] = gather("v_w0", S, U32, tab_w[0], idx)
+        wa_q[0] = quantise("wa00", round_wa(0, 0, 0))
+        accs = [[psum.tile([P, BANK], F32, name="acc") for h in range(2)] for t in range(4)]
+        for t in range(4):
+            for h in range(2):
+                a_pass(accs[t][h], 0, t, h)
+        v_w[1] = gather("v_w1", S, U32, tab_w[1], idx)
+        wa_q[1] = quantise("wa10", round_wa(1, 0, 2))
+        wo_raw = [load_wo(0), load_wo(1)]
+        a_picked = [kept("a_picked%d" % b, [P, 4, M], F32) for b in range(2)]
+        v2_w[0] = gather("v2_w0", M, U32, tab2_w[0], idx2)
+        v2_s = gather("v2_s", M, U8, tab2_s, idx2)
+        nc.gpsimd.dma_start(v2_s_up[: P - 4, :].bitcast(I32), v2_s[4:, :].bitcast(I32))
+        for t in range(4):
+            for h in range(2):
+                a_pass(accs[t][h], 1, t, h)
+            pick_heads(accs[t], a_picked[0], t)
+
+        for a in range(2):
+            wa_q[a] = quantise("wa%d1" % a, round_wa(a, 1, 0))
+        v2_w[1] = gather("v2_w1", M, U32, tab2_w[1], idx2)
+        gc_s = kept("gc_s", [P, 2 * H], U8)
+        nc.vector.tensor_copy(
+            gc_s[:].bitcast(I32).rearrange("p (ab t g) -> p ab g t", ab=4, t=4),
+            gc_s_raw[:].bitcast(I32).rearrange("p (ab g t) -> p ab g t", ab=4, t=4),
+        )
+        g_w, c_w = deal_gc(0)
+        sc = [kept("sc%d" % b, [P, 4, M], F32) for b in range(2)]
+        for t in range(4):
+            pair = [psum.tile([P, BANK], F32, name="acc") for h in range(2)]
+            for h in range(2):
+                for a in range(2):
+                    a_pass(pair[h], a, t, h)
+            pick_heads(pair, a_picked[1], t)
+            gated(0, t, g_w, c_w, sc[0])
+
+        g_w, c_w = deal_gc(1)
+        z_bf = [kept("z_bf%d" % b, [P, PACK * M], BF16) for b in range(2)]
+        z_w = [kept("z_w%d" % b, [P, M], U32) for b in range(2)]
+        z_s = [kept("z_s%d" % b, [P, M], U8) for b in range(2)]
+        nc.vector.tensor_tensor(woven(z_bf[0], 0, M), in_fours(sc[0], 0, M), in_fours(a_picked[0], 0, M), SUB)
+        for t in range(4):
+            gated(1, t, g_w, c_w, sc[1])
+        quantise_cols(z_w[0], z_s[0], z_bf[0], 0, M)
+        wo_q = [quantise("wo%d" % b, round_wo(wo_raw[b])) for b in range(2)]
+
+        y = kept("y", [P, 4, M], F32)
+        y_bf = kept("y_bf", [P, PACK * M], BF16)
+        y_w = kept("y_w", [P, M], U32)
+        y_s = kept("y_s", [P, M], U8)
+        y_rows = out_0.rearrange("(p u) m -> p u m", u=4)
+        y_words = out_1[0].rearrange("p m t -> p (m t)").bitcast(I32)
+
+        def z_piece(lo):
+            hi = lo + PIECE
+            nc.vector.tensor_tensor(woven(z_bf[1], lo, hi), in_fours(sc[1], lo, hi), in_fours(a_picked[1], lo, hi), SUB)
+
+        def y_product(lo):
+            hi = lo + PIECE
+            quantise_cols(z_w[1], z_s[1], z_bf[1], lo, hi)
+            acc = psum.tile([P, 4, PIECE], F32, name="acc")
+            for u in range(4):
+                cols = slice(u * P, (u + 1) * P)
+                for b in range(2):
+                    nc.tensor.matmul_mx(
+                        out=acc[:, u, :], lhsT=wo_q[b][0][:, cols].bitcast(FP8X4), lhsT_scale=wo_q[b][1][:, cols],
+                        rhs=z_w[b][:, lo:hi].bitcast(FP8X4), rhs_scale=z_s[b][:, lo:hi],
+                        start=(b == 0), stop=(b == 1),
+                    )
+            nc.scalar.copy(y[:, :, lo:hi], acc[:])
+            nc.sync.dma_start(y_rows[:, :, lo:hi], y[:, :, lo:hi])
+
+        def y_round(lo):
+            nc.vector.tensor_copy(woven(y_bf, lo, lo + PIECE), in_fours(y, lo, lo + PIECE))
+
+        def y_planes(lo):
+            hi = lo + PIECE
+            quantise_cols(y_w, y_s, y_bf, lo, hi)
+            nc.sync.dma_start(y_words[:, lo:hi], y_w[:, lo:hi].bitcast(I32))
+
+        stages = (z_piece, y_product, y_round, y_planes)
+        pieces = M // PIECE
+        for step in range(pieces + len(stages) - 1):
+            for lag, stage in enumerate(stages):
+                if 0 <= step - lag < pieces:
+                    stage((step - lag) * PIECE)
+        for q in range(4):
+            nc.sync.dma_start(out_2[0, 4 * q : 4 * q + 4, :].bitcast(I32), y_s[32 * q : 32 * q + 4, :].bitcast(I32))

@@ -49,13 +49,18 @@ def tile_list_expense_overspend_signals_kernel(
         gc_s_raw = kept("gc_s_raw", [P, 2 * H], U8)
         v2_s_up = kept("v2_s_up", [P, M], U8)
         nc.vector.memset(tab_s[:].bitcast(I32), 0)
-        nc.gpsimd.memset(tab2_s[:].bitcast(I32), 0)
-        nc.gpsimd.memset(gc_s_raw[:].bitcast(I32), 0)
-        nc.gpsimd.memset(v2_s_up[:].bitcast(I32), 0)
+        nc.vector.memset(tab2_s[:].bitcast(I32), 0)
+        nc.vector.memset(gc_s_raw[:].bitcast(I32), 0)
+        nc.vector.memset(v2_s_up[:].bitcast(I32), 0)
 
+        warm = kept("warm", [P, 8], F32)
+        nc.vector.memset(warm[:, 0:1], 0.0)
+        nc.scalar.activation(warm[:, 4:5], warm[:, 0:1], SILU)
         nc.sync.dma_start(idx[:], offs)
+        nc.sync.dma_start(idx2[:], offs2)
+        nc.sync.dma_start(heads[:], pos1)
         for q in range(4):
-            nc.scalar.dma_start(tab_s[32 * q : 32 * q + 8, :].bitcast(I32), tab_scales[:, 4 * q : 4 * q + 4, :].bitcast(I32))
+            nc.sync.dma_start(tab_s[32 * q : 32 * q + 8, :].bitcast(I32), tab_scales[:, 4 * q : 4 * q + 4, :].bitcast(I32))
 
         def load_tab2_scales():
             for q in range(4):
@@ -89,7 +94,7 @@ def tile_list_expense_overspend_signals_kernel(
 
         def load_gc(b):
             g_raw = kept("g_raw%d" % b, [P, 2, PASS // 2], I32)
-            c_raw = kept("c_raw%d" % b, [P, 2, PASS], I32)
+            c_raw = keep.tile([P, 2, PASS], I32, name="c_raw%d" % b, tag="c_raw%d" % b, align_bytes=64)
             g_src = wg_words.bitcast(I32)[:, :, b * PASS // 2 : (b + 1) * PASS // 2]
             c_src = wc_words.rearrange("a p e i -> a p (e i)").bitcast(I32)[:, :, b * PASS : (b + 1) * PASS]
             nc.sync.dma_start(g_raw[:], g_src.rearrange("a p e -> p a e"))
@@ -98,18 +103,16 @@ def tile_list_expense_overspend_signals_kernel(
 
         tab_w, tab2_w, wa_raw, gc_raw = {}, {}, {}, {}
         tab_w[0] = load_table(tab_words, 0, "tab_w0")
-        nc.sync.dma_start(idx2[:], offs2)
         wa_raw[0, 0] = load_wa(0, 0)
+        load_tab2_scales()
         tab_w[1] = load_table(tab_words, 1, "tab_w1")
         wa_raw[1, 0] = load_wa(1, 0)
-        nc.sync.dma_start(heads[:], pos1)
-        tab2_w[0] = load_table(tab2_words, 0, "tab2_w0")
-        load_tab2_scales()
         wa_raw[0, 1] = load_wa(0, 1)
-        load_weight_scales(0, wg_scales)
+        tab2_w[0] = load_table(tab2_words, 0, "tab2_w0")
         wa_raw[1, 1] = load_wa(1, 1)
-        load_weight_scales(4, wc_scales)
+        load_weight_scales(0, wg_scales)
         tab2_w[1] = load_table(tab2_words, 1, "tab2_w1")
+        load_weight_scales(4, wc_scales)
         gc_raw[0] = load_gc(0)
         gc_raw[1] = load_gc(1)
 
@@ -142,22 +145,22 @@ def tile_list_expense_overspend_signals_kernel(
             )
             return bf
 
-        def deal_gc(b):
+        def deal_gc(b, engine):
             g_raw, c_raw = gc_raw[b]
             g_w = kept("g_w%d" % b, [P, 2, PASS // 2], I32)
             c_w = kept("c_w%d" % b, [P, 2, PASS], I32)
-            nc.vector.tensor_copy(
+            engine.tensor_copy(
                 g_w[:].rearrange("p a (t g j) -> p a g t j", t=4, j=2),
                 g_raw[:].rearrange("p a (g t j) -> p a g t j", t=4, j=2),
             )
-            nc.vector.tensor_copy(
+            engine.tensor_copy(
                 c_w[:].rearrange("p a (t g j) -> p a g t j", t=4, j=4),
                 c_raw[:].rearrange("p a (g t j) -> p a g t j", t=4, j=4),
             )
             return g_w, c_w
 
-        def a_pass(acc, a, t, h):
-            codes, scales = wa_q[a]
+        def a_pass(acc, weights, a, t, h):
+            codes, scales = weights[a]
             cols, picked = slice(t * P, (t + 1) * P), slice(h * BANK, (h + 1) * BANK)
             nc.tensor.matmul_mx(
                 out=acc[:], lhsT=codes[:, cols].bitcast(FP8X4), lhsT_scale=scales[:, cols],
@@ -204,50 +207,77 @@ def tile_list_expense_overspend_signals_kernel(
         v_w, v2_w, wa_q = {}, {}, {}
         v_s = gather("v_s", S, U8, tab_s, idx)
         v_w[0] = gather("v_w0", S, U32, tab_w[0], idx)
-        wa_q[0] = quantise("wa00", round_wa(0, 0, 0))
+        wa_q[0] = quantise("wa00", round_wa(0, 0, 2))
+        v2_s = gather("v2_s", M, U8, tab2_s, idx2)
+        nc.gpsimd.dma_start(v2_s_up[: P - 4, :].bitcast(I32), v2_s[4:, :].bitcast(I32))
         accs = [[psum.tile([P, BANK], F32, name="acc") for h in range(2)] for t in range(4)]
         for t in range(4):
             for h in range(2):
-                a_pass(accs[t][h], 0, t, h)
+                a_pass(accs[t][h], wa_q, 0, t, h)
         v_w[1] = gather("v_w1", S, U32, tab_w[1], idx)
         wa_q[1] = quantise("wa10", round_wa(1, 0, 2))
+        wa01_bf = round_wa(0, 1, 2)
+        wa11_bf = round_wa(1, 1, 0)
+        second_half = [quantise("wa01", wa01_bf), quantise("wa11", wa11_bf)]
         wo_raw = [load_wo(0), load_wo(1)]
-        a_picked = [kept("a_picked%d" % b, [P, 4, M], F32) for b in range(2)]
-        v2_w[0] = gather("v2_w0", M, U32, tab2_w[0], idx2)
-        v2_s = gather("v2_s", M, U8, tab2_s, idx2)
-        nc.gpsimd.dma_start(v2_s_up[: P - 4, :].bitcast(I32), v2_s[4:, :].bitcast(I32))
+        a_picked = [kept("a_picked0", [P, 4, M], F32), keep.tile([P, 4, M], F32, name="a_picked1", tag="c_raw0", align_bytes=64)]
         for t in range(4):
             for h in range(2):
-                a_pass(accs[t][h], 1, t, h)
+                a_pass(accs[t][h], wa_q, 1, t, h)
             pick_heads(accs[t], a_picked[0], t)
 
-        for a in range(2):
-            wa_q[a] = quantise("wa%d1" % a, round_wa(a, 1, 0))
+        v2_w[0] = gather("v2_w0", M, U32, tab2_w[0], idx2)
         v2_w[1] = gather("v2_w1", M, U32, tab2_w[1], idx2)
         gc_s = kept("gc_s", [P, 2 * H], U8)
         nc.vector.tensor_copy(
             gc_s[:].bitcast(I32).rearrange("p (ab t g) -> p ab g t", ab=4, t=4),
             gc_s_raw[:].bitcast(I32).rearrange("p (ab g t) -> p ab g t", ab=4, t=4),
         )
-        g_w, c_w = deal_gc(0)
+        gc_w = [deal_gc(0, nc.vector), deal_gc(1, nc.vector)]
         sc = [kept("sc%d" % b, [P, 4, M], F32) for b in range(2)]
-        for t in range(4):
-            pair = [psum.tile([P, BANK], F32, name="acc") for h in range(2)]
-            for h in range(2):
-                for a in range(2):
-                    a_pass(pair[h], a, t, h)
-            pick_heads(pair, a_picked[1], t)
-            gated(0, t, g_w, c_w, sc[0])
-
-        g_w, c_w = deal_gc(1)
         z_bf = [kept("z_bf%d" % b, [P, PACK * M], BF16) for b in range(2)]
         z_w = [kept("z_w%d" % b, [P, M], U32) for b in range(2)]
         z_s = [kept("z_s%d" % b, [P, M], U8) for b in range(2)]
-        nc.vector.tensor_tensor(woven(z_bf[0], 0, M), in_fours(sc[0], 0, M), in_fours(a_picked[0], 0, M), SUB)
-        for t in range(4):
-            gated(1, t, g_w, c_w, sc[1])
-        quantise_cols(z_w[0], z_s[0], z_bf[0], 0, M)
+
+        def second_a():
+            for t in range(4):
+                pair = [psum.tile([P, BANK], F32, name="acc") for h in range(2)]
+                for h in range(2):
+                    for a in range(2):
+                        a_pass(pair[h], second_half, a, t, h)
+                pick_heads(pair, a_picked[1], t)
+
+        def gated_half(b):
+            for t in range(4):
+                gated(b, t, *gc_w[b], sc[b])
+
+        def first_z():
+            for lo in range(0, M, M):
+                hi = lo + M
+                nc.vector.tensor_tensor(woven(z_bf[0], lo, hi), in_fours(sc[0], lo, hi), in_fours(a_picked[0], lo, hi), SUB)
+
+        second_a()
+        gated_half(0)
+        first_z()
+        gated_half(1)
+
         wo_q = [quantise("wo%d" % b, round_wo(wo_raw[b])) for b in range(2)]
+        quantise_cols(z_w[0], z_s[0], z_bf[0], 0, M)
+        pieces = M // PIECE
+        y_acc = [psum.tile([P, 4, PIECE], F32, name="acc") for piece in range(pieces)]
+
+        def y_pass(b, lo):
+            hi = lo + PIECE
+            for u in range(4):
+                cols = slice(u * P, (u + 1) * P)
+                nc.tensor.matmul_mx(
+                    out=y_acc[lo // PIECE][:, u, :], lhsT=wo_q[b][0][:, cols].bitcast(FP8X4), lhsT_scale=wo_q[b][1][:, cols],
+                    rhs=z_w[b][:, lo:hi].bitcast(FP8X4), rhs_scale=z_s[b][:, lo:hi],
+                    start=(b == 0 and u == 0), stop=(b == 1 and u == 3),
+                )
+
+        for lo in range(0, M, PIECE):
+            y_pass(0, lo)
 
         y = kept("y", [P, 4, M], F32)
         y_bf = kept("y_bf", [P, PACK * M], BF16)
@@ -263,16 +293,8 @@ def tile_list_expense_overspend_signals_kernel(
         def y_product(lo):
             hi = lo + PIECE
             quantise_cols(z_w[1], z_s[1], z_bf[1], lo, hi)
-            acc = psum.tile([P, 4, PIECE], F32, name="acc")
-            for u in range(4):
-                cols = slice(u * P, (u + 1) * P)
-                for b in range(2):
-                    nc.tensor.matmul_mx(
-                        out=acc[:, u, :], lhsT=wo_q[b][0][:, cols].bitcast(FP8X4), lhsT_scale=wo_q[b][1][:, cols],
-                        rhs=z_w[b][:, lo:hi].bitcast(FP8X4), rhs_scale=z_s[b][:, lo:hi],
-                        start=(b == 0), stop=(b == 1),
-                    )
-            nc.scalar.copy(y[:, :, lo:hi], acc[:])
+            y_pass(1, lo)
+            nc.scalar.copy(y[:, :, lo:hi], y_acc[lo // PIECE][:])
             nc.sync.dma_start(y_rows[:, :, lo:hi], y[:, :, lo:hi])
 
         def y_round(lo):
@@ -284,10 +306,9 @@ def tile_list_expense_overspend_signals_kernel(
             nc.sync.dma_start(y_words[:, lo:hi], y_w[:, lo:hi].bitcast(I32))
 
         stages = (z_piece, y_product, y_round, y_planes)
-        pieces = M // PIECE
         for step in range(pieces + len(stages) - 1):
             for lag, stage in enumerate(stages):
                 if 0 <= step - lag < pieces:
                     stage((step - lag) * PIECE)
         for q in range(4):
-            nc.sync.dma_start(out_2[0, 4 * q : 4 * q + 4, :].bitcast(I32), y_s[32 * q : 32 * q + 4, :].bitcast(I32))
+            nc.scalar.dma_start(out_2[0, 4 * q : 4 * q + 4, :].bitcast(I32), y_s[32 * q : 32 * q + 4, :].bitcast(I32))

@@ -33,12 +33,12 @@ def tile_list_expense_overspend_signals_kernel(
         lists = ctx.enter_context(tc.tile_pool(name="lists", bufs=1))
         keep = ctx.enter_context(tc.tile_pool(name="keep", bufs=1))
         raws = ctx.enter_context(tc.tile_pool(name="raws", bufs=4))
-        rounded = ctx.enter_context(tc.tile_pool(name="rounded", bufs=3))
-        a_rows = ctx.enter_context(tc.tile_pool(name="a_rows", bufs=4))
-        gates = ctx.enter_context(tc.tile_pool(name="gates", bufs=3))
+        staged = ctx.enter_context(tc.tile_pool(name="staged", bufs=10))
         psum = ctx.enter_context(tc.psum_pool(name="psum", bufs=8))
 
-        def kept(name, shape, dtype):
+        def kept(name, shape, dtype, tag=None):
+            if tag:
+                return keep.tile(shape, dtype, name=name, tag=tag, bufs=2, align_bytes=64)
             return keep.tile(shape, dtype, name=name, align_bytes=64)
 
         idx = lists.tile([P, S // 16], U16, name="idx")
@@ -57,10 +57,10 @@ def tile_list_expense_overspend_signals_kernel(
         nc.vector.memset(warm[:, 0:1], 0.0)
         nc.scalar.activation(warm[:, 4:5], warm[:, 0:1], SILU)
         nc.sync.dma_start(idx[:], offs)
-        nc.sync.dma_start(idx2[:], offs2)
-        nc.sync.dma_start(heads[:], pos1)
-        for q in range(4):
-            nc.sync.dma_start(tab_s[32 * q : 32 * q + 8, :].bitcast(I32), tab_scales[:, 4 * q : 4 * q + 4, :].bitcast(I32))
+
+        def load_tab_scales():
+            for q in range(4):
+                nc.sync.dma_start(tab_s[32 * q : 32 * q + 8, :].bitcast(I32), tab_scales[:, 4 * q : 4 * q + 4, :].bitcast(I32))
 
         def load_tab2_scales():
             for q in range(4):
@@ -103,32 +103,35 @@ def tile_list_expense_overspend_signals_kernel(
 
         tab_w, tab2_w, wa_raw, gc_raw = {}, {}, {}, {}
         tab_w[0] = load_table(tab_words, 0, "tab_w0")
+        load_tab_scales()
         wa_raw[0, 0] = load_wa(0, 0)
-        load_tab2_scales()
         tab_w[1] = load_table(tab_words, 1, "tab_w1")
         wa_raw[1, 0] = load_wa(1, 0)
+        nc.sync.dma_start(idx2[:], offs2)
+        load_tab2_scales()
+        nc.sync.dma_start(heads[:], pos1)
         wa_raw[0, 1] = load_wa(0, 1)
-        tab2_w[0] = load_table(tab2_words, 0, "tab2_w0")
         wa_raw[1, 1] = load_wa(1, 1)
+        tab2_w[0] = load_table(tab2_words, 0, "tab2_w0")
         load_weight_scales(0, wg_scales)
         tab2_w[1] = load_table(tab2_words, 1, "tab2_w1")
         load_weight_scales(4, wc_scales)
         gc_raw[0] = load_gc(0)
         gc_raw[1] = load_gc(1)
 
-        def gather(name, width, dtype, window, offsets):
-            picked = kept(name, [P, width], dtype)
+        def gather(name, width, dtype, window, offsets, tag=None):
+            picked = kept(name, [P, width], dtype, tag)
             nc.vector.tensor_copy(picked[:], window[:].indirect(offsets[:]))
             return picked
 
-        def quantise(name, src):
-            codes = kept(name + "_w", [P, PASS], U32)
+        def quantise(name, src, tag=None):
+            codes = kept(name + "_w", [P, PASS], U32, tag)
             scales = kept(name + "_s", [P, PASS], U8)
             nc.vector.quantize_mx(out=codes[:].bitcast(FP8X4), scales=scales[:], in_=src[:])
             return codes, scales
 
         def round_wa(a, b, vector_share):
-            bf = rounded.tile([P, PACK * PASS], BF16, name="bf", align_bytes=64)
+            bf = staged.tile([P, PACK * PASS], BF16, name="bf", tag="staged", align_bytes=64)
             dst = bf[:].rearrange("p (t g j i) -> p t g i j", t=4, j=4, i=PACK)
             src = wa_raw[a, b][:].rearrange("p i (g t j) -> p t g i j", t=4, j=4)
             cut = 4 - vector_share
@@ -138,7 +141,7 @@ def tile_list_expense_overspend_signals_kernel(
             return bf
 
         def round_wo(raw):
-            bf = rounded.tile([P, PACK * N], BF16, name="bf", align_bytes=64)
+            bf = staged.tile([P, PACK * N], BF16, name="bf", tag="staged", align_bytes=64)
             nc.scalar.copy(
                 bf[:].rearrange("p (u c t) -> p c t u", u=4, t=4),
                 raw[:].rearrange("p t (c u) -> p c t u", u=4),
@@ -169,7 +172,7 @@ def tile_list_expense_overspend_signals_kernel(
             )
 
         def pick_heads(accs, a_picked, t):
-            row = a_rows.tile([P, S], F32, name="row")
+            row = staged.tile([P, S], F32, name="row", tag="staged", align_bytes=64)
             for h in range(2):
                 nc.scalar.copy(row[:, h * BANK : (h + 1) * BANK], accs[h][:])
             nc.vector.tensor_copy(a_picked[:, t, :], row[:].indirect(heads[:]))
@@ -191,7 +194,7 @@ def tile_list_expense_overspend_signals_kernel(
                     rhs=v2_w[a][:].bitcast(FP8X4), rhs_scale=v2_s[4 * a :, :],
                     start=(a == 0), stop=(a == 1),
                 )
-            gate = gates.tile([P, M], F32, name="gate")
+            gate = staged.tile([P, M], F32, name="gate", tag="staged", align_bytes=64)
             nc.scalar.activation(gate[:], g_acc[:], SILU)
             nc.vector.tensor_tensor(sc[:, t, :], c_acc[:], gate[:], MULT)
 
@@ -204,27 +207,27 @@ def tile_list_expense_overspend_signals_kernel(
         def quantise_cols(codes, scales, bf, lo, hi):
             nc.vector.quantize_mx(out=codes[:, lo:hi].bitcast(FP8X4), scales=scales[:, lo:hi], in_=bf[:, PACK * lo : PACK * hi])
 
-        v_w, v2_w, wa_q = {}, {}, {}
-        v_s = gather("v_s", S, U8, tab_s, idx)
+        v_w, v2_w, wa_q, wo_q = {}, {}, {}, {}
         v_w[0] = gather("v_w0", S, U32, tab_w[0], idx)
-        wa_q[0] = quantise("wa00", round_wa(0, 0, 2))
-        v2_s = gather("v2_s", M, U8, tab2_s, idx2)
-        nc.gpsimd.dma_start(v2_s_up[: P - 4, :].bitcast(I32), v2_s[4:, :].bitcast(I32))
+        v_s = gather("v_s", S, U8, tab_s, idx)
+        wa_q[0] = quantise("wa00", round_wa(0, 0, 0), "early")
         accs = [[psum.tile([P, BANK], F32, name="acc") for h in range(2)] for t in range(4)]
         for t in range(4):
             for h in range(2):
                 a_pass(accs[t][h], wa_q, 0, t, h)
-        v_w[1] = gather("v_w1", S, U32, tab_w[1], idx)
+        v_w[1] = gather("v_w1", S, U32, tab_w[1], idx, "early")
         wa_q[1] = quantise("wa10", round_wa(1, 0, 2))
-        wa01_bf = round_wa(0, 1, 2)
-        wa11_bf = round_wa(1, 1, 0)
-        second_half = [quantise("wa01", wa01_bf), quantise("wa11", wa11_bf)]
-        wo_raw = [load_wo(0), load_wo(1)]
+        v2_s = gather("v2_s", M, U8, tab2_s, idx2)
+        nc.gpsimd.dma_start(v2_s_up[: P - 4, :].bitcast(I32), v2_s[4:, :].bitcast(I32))
+        second_half = [quantise("wa01", round_wa(0, 1, 2))]
         a_picked = [kept("a_picked0", [P, 4, M], F32), keep.tile([P, 4, M], F32, name="a_picked1", tag="c_raw0", align_bytes=64)]
         for t in range(4):
+            if t == 2:
+                second_half.append(quantise("wa11", round_wa(1, 1, 0)))
             for h in range(2):
                 a_pass(accs[t][h], wa_q, 1, t, h)
             pick_heads(accs[t], a_picked[0], t)
+        wo_raw = [load_wo(0), load_wo(1)]
 
         v2_w[0] = gather("v2_w0", M, U32, tab2_w[0], idx2)
         v2_w[1] = gather("v2_w1", M, U32, tab2_w[1], idx2)
@@ -238,30 +241,26 @@ def tile_list_expense_overspend_signals_kernel(
         z_bf = [kept("z_bf%d" % b, [P, PACK * M], BF16) for b in range(2)]
         z_w = [kept("z_w%d" % b, [P, M], U32) for b in range(2)]
         z_s = [kept("z_s%d" % b, [P, M], U8) for b in range(2)]
-
-        def second_a():
-            for t in range(4):
-                pair = [psum.tile([P, BANK], F32, name="acc") for h in range(2)]
-                for h in range(2):
-                    for a in range(2):
-                        a_pass(pair[h], second_half, a, t, h)
-                pick_heads(pair, a_picked[1], t)
-
-        def gated_half(b):
-            for t in range(4):
-                gated(b, t, *gc_w[b], sc[b])
-
-        def first_z():
-            for lo in range(0, M, M):
-                hi = lo + M
-                nc.vector.tensor_tensor(woven(z_bf[0], lo, hi), in_fours(sc[0], lo, hi), in_fours(a_picked[0], lo, hi), SUB)
-
-        second_a()
-        gated_half(0)
-        first_z()
-        gated_half(1)
-
-        wo_q = [quantise("wo%d" % b, round_wo(wo_raw[b])) for b in range(2)]
+        for t in range(4):
+            pair = [psum.tile([P, BANK], F32, name="acc") for h in range(2)]
+            for h in range(2):
+                for a in range(2):
+                    a_pass(pair[h], second_half, a, t, h)
+            pick_heads(pair, a_picked[1], t)
+        for t in range(4):
+            if t == 2:
+                wo_q[0] = quantise("wo0", round_wo(wo_raw[0]))
+            gated(0, t, *gc_w[0], sc[0])
+        for lo in range(0, M, M):
+            hi = lo + M
+            nc.vector.tensor_tensor(woven(z_bf[0], lo, hi), in_fours(sc[0], lo, hi), in_fours(a_picked[0], lo, hi), SUB)
+        for t in range(4):
+            if t == -2:
+                wo_q[0] = quantise("wo0", round_wo(wo_raw[0]))
+            if t == 4:
+                wo_q[1] = quantise("wo1", round_wo(wo_raw[1]))
+            gated(1, t, *gc_w[1], sc[1])
+        wo_q[1] = quantise("wo1", round_wo(wo_raw[1]))
         quantise_cols(z_w[0], z_s[0], z_bf[0], 0, M)
         pieces = M // PIECE
         y_acc = [psum.tile([P, 4, PIECE], F32, name="acc") for piece in range(pieces)]
@@ -303,7 +302,8 @@ def tile_list_expense_overspend_signals_kernel(
         def y_planes(lo):
             hi = lo + PIECE
             quantise_cols(y_w, y_s, y_bf, lo, hi)
-            nc.sync.dma_start(y_words[:, lo:hi], y_w[:, lo:hi].bitcast(I32))
+            if hi % (2 * PIECE) == 0:
+                nc.sync.dma_start(y_words[:, hi - 2 * PIECE : hi], y_w[:, hi - 2 * PIECE : hi].bitcast(I32))
 
         stages = (z_piece, y_product, y_round, y_planes)
         for step in range(pieces + len(stages) - 1):
@@ -311,4 +311,4 @@ def tile_list_expense_overspend_signals_kernel(
                 if 0 <= step - lag < pieces:
                     stage((step - lag) * PIECE)
         for q in range(4):
-            nc.scalar.dma_start(out_2[0, 4 * q : 4 * q + 4, :].bitcast(I32), y_s[32 * q : 32 * q + 4, :].bitcast(I32))
+            (nc.scalar, nc.sync)[q % 2].dma_start(out_2[0, 4 * q : 4 * q + 4, :].bitcast(I32), y_s[32 * q : 32 * q + 4, :].bitcast(I32))

@@ -102,14 +102,14 @@ def tile_list_expense_overspend_signals_kernel(
             return g_raw, c_raw
 
         tab_w, tab2_w, wa_raw, gc_raw = {}, {}, {}, {}
-        tab_w[0] = load_table(tab_words, 0, "tab_w0")
+        nc.sync.dma_start(idx2[:], offs2)
+        nc.sync.dma_start(heads[:], pos1)
         load_tab_scales()
+        tab_w[0] = load_table(tab_words, 0, "tab_w0")
         wa_raw[0, 0] = load_wa(0, 0)
+        load_tab2_scales()
         tab_w[1] = load_table(tab_words, 1, "tab_w1")
         wa_raw[1, 0] = load_wa(1, 0)
-        nc.sync.dma_start(idx2[:], offs2)
-        load_tab2_scales()
-        nc.sync.dma_start(heads[:], pos1)
         wa_raw[0, 1] = load_wa(0, 1)
         wa_raw[1, 1] = load_wa(1, 1)
         tab2_w[0] = load_table(tab2_words, 0, "tab2_w0")
@@ -156,10 +156,11 @@ def tile_list_expense_overspend_signals_kernel(
                 g_w[:].rearrange("p a (t g j) -> p a g t j", t=4, j=2),
                 g_raw[:].rearrange("p a (g t j) -> p a g t j", t=4, j=2),
             )
-            engine.tensor_copy(
-                c_w[:].rearrange("p a (t g j) -> p a g t j", t=4, j=4),
-                c_raw[:].rearrange("p a (g t j) -> p a g t j", t=4, j=4),
-            )
+            for a in range(2):
+                engine.tensor_copy(
+                    c_w[:, a, :].rearrange("p (t g j) -> p g t j", t=4, j=4),
+                    c_raw[:, a, :].rearrange("p (g t j) -> p g t j", t=4, j=4),
+                )
             return g_w, c_w
 
         def a_pass(acc, weights, a, t, h):
@@ -218,9 +219,9 @@ def tile_list_expense_overspend_signals_kernel(
         v_w[1] = gather("v_w1", S, U32, tab_w[1], idx, "early")
         wa_q[1] = quantise("wa10", round_wa(1, 0, 2))
         v2_s = gather("v2_s", M, U8, tab2_s, idx2)
-        nc.gpsimd.dma_start(v2_s_up[: P - 4, :].bitcast(I32), v2_s[4:, :].bitcast(I32))
+        nc.scalar.dma_start(v2_s_up[: P - 4, :].bitcast(I32), v2_s[4:, :].bitcast(I32))
         second_half = [quantise("wa01", round_wa(0, 1, 2))]
-        a_picked = [kept("a_picked0", [P, 4, M], F32), keep.tile([P, 4, M], F32, name="a_picked1", tag="c_raw0", align_bytes=64)]
+        a_picked = [kept("a_picked0", [P, 4, M], F32), keep.tile([P, 4, M], F32, name="a_picked1", tag="tab2_w1", align_bytes=64)]
         for t in range(4):
             if t == 2:
                 second_half.append(quantise("wa11", round_wa(1, 1, 0)))
@@ -232,11 +233,11 @@ def tile_list_expense_overspend_signals_kernel(
         v2_w[0] = gather("v2_w0", M, U32, tab2_w[0], idx2)
         v2_w[1] = gather("v2_w1", M, U32, tab2_w[1], idx2)
         gc_s = kept("gc_s", [P, 2 * H], U8)
-        nc.vector.tensor_copy(
+        nc.gpsimd.tensor_copy(
             gc_s[:].bitcast(I32).rearrange("p (ab t g) -> p ab g t", ab=4, t=4),
             gc_s_raw[:].bitcast(I32).rearrange("p (ab g t) -> p ab g t", ab=4, t=4),
         )
-        gc_w = [deal_gc(0, nc.vector), deal_gc(1, nc.vector)]
+        gc_w = [deal_gc(0, nc.gpsimd), deal_gc(1, nc.gpsimd)]
         sc = [kept("sc%d" % b, [P, 4, M], F32) for b in range(2)]
         z_bf = [kept("z_bf%d" % b, [P, PACK * M], BF16) for b in range(2)]
         z_w = [kept("z_w%d" % b, [P, M], U32) for b in range(2)]
@@ -254,14 +255,14 @@ def tile_list_expense_overspend_signals_kernel(
         for lo in range(0, M, M):
             hi = lo + M
             nc.vector.tensor_tensor(woven(z_bf[0], lo, hi), in_fours(sc[0], lo, hi), in_fours(a_picked[0], lo, hi), SUB)
+        quantise_cols(z_w[0], z_s[0], z_bf[0], 0, M)
         for t in range(4):
             if t == -2:
                 wo_q[0] = quantise("wo0", round_wo(wo_raw[0]))
-            if t == 4:
+            if t == 1:
                 wo_q[1] = quantise("wo1", round_wo(wo_raw[1]))
             gated(1, t, *gc_w[1], sc[1])
-        wo_q[1] = quantise("wo1", round_wo(wo_raw[1]))
-        quantise_cols(z_w[0], z_s[0], z_bf[0], 0, M)
+
         pieces = M // PIECE
         y_acc = [psum.tile([P, 4, PIECE], F32, name="acc") for piece in range(pieces)]
 

@@ -14,14 +14,18 @@ U8 = mybir.dt.uint8
 FP8X4 = mybir.dt.float8_e4m3fn_x4
 FP4X4 = mybir.dt.float4_e2m1fn_x4
 MULT = mybir.AluOpType.mult
+ADD = mybir.AluOpType.add
 SUB = mybir.AluOpType.subtract
 SILU = mybir.ActivationFunctionType.Silu
+COPY = mybir.ActivationFunctionType.Copy
 
 P = 128
 PACK = 4
 PASS = P * PACK
 BANK = 512
-PIECE = 128
+RUN = 8
+V_BUFS = 22
+S_BUFS = 12
 
 
 def tile_list_expense_overspend_signals_kernel(
@@ -32,14 +36,22 @@ def tile_list_expense_overspend_signals_kernel(
     with ExitStack() as ctx:
         lists = ctx.enter_context(tc.tile_pool(name="lists", bufs=1))
         keep = ctx.enter_context(tc.tile_pool(name="keep", bufs=1))
-        raws = ctx.enter_context(tc.tile_pool(name="raws", bufs=4))
-        staged = ctx.enter_context(tc.tile_pool(name="staged", bufs=10))
         psum = ctx.enter_context(tc.psum_pool(name="psum", bufs=8))
 
-        def kept(name, shape, dtype, tag=None):
-            if tag:
-                return keep.tile(shape, dtype, name=name, tag=tag, bufs=2, align_bytes=64)
+        def kept(name, shape, dtype):
             return keep.tile(shape, dtype, name=name, align_bytes=64)
+
+        def loaded(name, shape, dtype):
+            return keep.tile(shape, dtype, name=name, tag="loaded", bufs=7, align_bytes=64)
+
+        def by_vector(name, shape, dtype):
+            return keep.tile(shape, dtype, name=name, tag="by_vector", bufs=V_BUFS, align_bytes=64)
+
+        def by_scalar(name, shape, dtype):
+            return keep.tile(shape, dtype, name=name, tag="by_scalar", bufs=S_BUFS, align_bytes=64)
+
+        def bank(name, shape):
+            return psum.tile(shape, F32, name=name, tag="bank")
 
         idx = lists.tile([P, S // 16], U16, name="idx")
         idx2 = lists.tile([P, M // 16], U16, name="idx2")
@@ -48,268 +60,348 @@ def tile_list_expense_overspend_signals_kernel(
         tab2_s = kept("tab2_s", [P, T], U8)
         gc_s_raw = kept("gc_s_raw", [P, 2 * H], U8)
         v2_s_up = kept("v2_s_up", [P, M], U8)
-        nc.vector.memset(tab_s[:].bitcast(I32), 0)
-        nc.vector.memset(tab2_s[:].bitcast(I32), 0)
-        nc.vector.memset(gc_s_raw[:].bitcast(I32), 0)
-        nc.vector.memset(v2_s_up[:].bitcast(I32), 0)
 
-        warm = kept("warm", [P, 8], F32)
-        nc.vector.memset(warm[:, 0:1], 0.0)
-        nc.scalar.activation(warm[:, 4:5], warm[:, 0:1], SILU)
-        nc.sync.dma_start(idx[:], offs)
-
-        def load_tab_scales():
+        def load_table_scales(queue, tile, scales):
             for q in range(4):
-                nc.sync.dma_start(tab_s[32 * q : 32 * q + 8, :].bitcast(I32), tab_scales[:, 4 * q : 4 * q + 4, :].bitcast(I32))
+                queue.dma_start(tile[32 * q : 32 * q + 8, :].bitcast(I32), scales[:, 4 * q : 4 * q + 4, :].bitcast(I32))
 
-        def load_tab2_scales():
-            for q in range(4):
-                nc.sync.dma_start(tab2_s[32 * q : 32 * q + 8, :].bitcast(I32), tab2_scales[:, 4 * q : 4 * q + 4, :].bitcast(I32))
-
-        def load_weight_scales(first, scales):
+        def load_weight_scales(queue, first, scales):
             for q in range(4):
                 rows = gc_s_raw[32 * q + first : 32 * q + first + 4, :].bitcast(I32)
-                nc.sync.dma_start(
+                queue.dma_start(
                     rows.rearrange("r (a e) -> r a e", a=2),
                     scales[:, 4 * q : 4 * q + 4, :].bitcast(I32).rearrange("a r e -> r a e"),
                 )
 
-        def load_table(words, a, name):
-            tile = kept(name, [P, T], U32)
+        def load_table(words, a, name, shared=False):
+            tile = keep.tile([P, T], U32, name=name, tag="shared", align_bytes=64) if shared else loaded(name, [P, T], U32)
             nc.sync.dma_start(tile[:].bitcast(I32), words[a].rearrange("p t i -> p (t i)").bitcast(I32))
             return tile
 
         def load_wa(a, b):
-            raw = raws.tile([P, PACK, PASS], F32, name="raw")
+            raw = loaded("wa%d%d" % (a, b), [P, PACK, PASS], F32)
             rows = wa[a * PASS : (a + 1) * PASS, b * PASS : (b + 1) * PASS]
             nc.sync.dma_start(raw[:], rows.rearrange("(p i) r -> p i r", i=PACK))
             return raw
 
         def load_wo(b):
-            raw = raws.tile([P, PACK, N], F32, name="raw")
-            rows = wo[b * PASS : (b + 1) * PASS, :].rearrange("(g t j) n -> t g j n", t=4, j=4)
+            raw = loaded("wo%d" % b, [P, PACK, N], F32)
+            rows = wo[b * PASS : (b + 1) * PASS, :].rearrange("(g t j) n -> t g j n", t=4, j=RUN)
             for t in range(4):
                 nc.sync.dma_start(raw[:, t, :], rows[t])
             return raw
 
-        def load_gc(b):
-            g_raw = kept("g_raw%d" % b, [P, 2, PASS // 2], I32)
-            c_raw = keep.tile([P, 2, PASS], I32, name="c_raw%d" % b, tag="c_raw%d" % b, align_bytes=64)
-            g_src = wg_words.bitcast(I32)[:, :, b * PASS // 2 : (b + 1) * PASS // 2]
+        def load_g():
+            g_raw = kept("g_raw", [P, 2, H // 2], I32)
+            nc.sync.dma_start(g_raw[:], wg_words.bitcast(I32).rearrange("a p e -> p a e"))
+            return g_raw
+
+        def load_c(b):
+            c_raw = kept("c_raw%d" % b, [P, 2, PASS], I32)
             c_src = wc_words.rearrange("a p e i -> a p (e i)").bitcast(I32)[:, :, b * PASS : (b + 1) * PASS]
-            nc.sync.dma_start(g_raw[:], g_src.rearrange("a p e -> p a e"))
             nc.sync.dma_start(c_raw[:], c_src.rearrange("a p e -> p a e"))
-            return g_raw, c_raw
+            return c_raw
 
-        tab_w, tab2_w, wa_raw, gc_raw = {}, {}, {}, {}
-        nc.sync.dma_start(idx2[:], offs2)
-        nc.sync.dma_start(heads[:], pos1)
-        load_tab_scales()
-        tab_w[0] = load_table(tab_words, 0, "tab_w0")
-        wa_raw[0, 0] = load_wa(0, 0)
-        load_tab2_scales()
-        tab_w[1] = load_table(tab_words, 1, "tab_w1")
-        wa_raw[1, 0] = load_wa(1, 0)
-        wa_raw[0, 1] = load_wa(0, 1)
-        wa_raw[1, 1] = load_wa(1, 1)
-        tab2_w[0] = load_table(tab2_words, 0, "tab2_w0")
-        load_weight_scales(0, wg_scales)
-        tab2_w[1] = load_table(tab2_words, 1, "tab2_w1")
-        load_weight_scales(4, wc_scales)
-        gc_raw[0] = load_gc(0)
-        gc_raw[1] = load_gc(1)
-
-        def gather(name, width, dtype, window, offsets, tag=None):
-            picked = kept(name, [P, width], dtype, tag)
-            nc.vector.tensor_copy(picked[:], window[:].indirect(offsets[:]))
+        def gather(name, dtype, window, offsets, lo, hi):
+            picked = by_vector(name, [P, hi - lo], dtype)
+            nc.vector.tensor_copy(picked[:], window[:].indirect(offsets[:, lo // 16 : hi // 16]))
             return picked
 
-        def quantise(name, src, tag=None):
-            codes = kept(name + "_w", [P, PASS], U32, tag)
-            scales = kept(name + "_s", [P, PASS], U8)
+        def quantise(name, src):
+            width = src.shape[1] // PACK
+            codes = by_vector(name + "_w", [P, width], U32)
+            scales = kept(name + "_s", [P, width], U8)
             nc.vector.quantize_mx(out=codes[:].bitcast(FP8X4), scales=scales[:], in_=src[:])
             return codes, scales
 
-        def round_wa(a, b, vector_share):
-            bf = staged.tile([P, PACK * PASS], BF16, name="bf", tag="staged", align_bytes=64)
-            dst = bf[:].rearrange("p (t g j i) -> p t g i j", t=4, j=4, i=PACK)
-            src = wa_raw[a, b][:].rearrange("p i (g t j) -> p t g i j", t=4, j=4)
-            cut = 4 - vector_share
-            nc.scalar.copy(dst[:, :cut], src[:, :cut])
-            if vector_share:
-                nc.vector.tensor_copy(dst[:, cut:], src[:, cut:])
+        def rounded(name, plan):
+            if plan[0] == "s":
+                return by_scalar(name, [P, PACK * PASS], BF16)
+            return kept(name, [P, PACK * PASS], BF16)
+
+        def shares(plan):
+            return [(e, plan.index(e), plan.index(e) + plan.count(e)) for e in "svg" if e in plan]
+
+        def round_wa(raw, name, plan):
+            bf = rounded(name, plan)
+            for e, lo, hi in shares(plan):
+                if e == "g":
+                    dst = bf[:].rearrange("p (t g j i) -> p t g j i", t=4, j=RUN, i=PACK)
+                    src = raw[:].rearrange("p i (g t j) -> p t g j i", t=4, j=RUN)
+                    for t in range(lo, hi):
+                        nc.gpsimd.tensor_scalar(dst[:, t], src[:, t], 1.0, 0.0, MULT, ADD)
+                else:
+                    dst = bf[:].rearrange("p (t g j i) -> p t g i j", t=4, j=RUN, i=PACK)
+                    src = raw[:].rearrange("p i (g t j) -> p t g i j", t=4, j=RUN)
+                    if e == "s":
+                        nc.scalar.copy(dst[:, lo:hi], src[:, lo:hi])
+                    else:
+                        nc.vector.tensor_copy(dst[:, lo:hi], src[:, lo:hi])
             return bf
 
-        def round_wo(raw):
-            bf = staged.tile([P, PACK * N], BF16, name="bf", tag="staged", align_bytes=64)
-            nc.scalar.copy(
-                bf[:].rearrange("p (u c t) -> p c t u", u=4, t=4),
-                raw[:].rearrange("p t (c u) -> p c t u", u=4),
-            )
+        def round_wo(raw, name, plan):
+            bf = rounded(name, plan)
+            for e, lo, hi in shares(plan):
+                if e == "g":
+                    dst = bf[:].rearrange("p (u c t) -> p u c t", u=4, t=4)
+                    src = raw[:].rearrange("p t (c u) -> p u c t", u=4)
+                    for u in range(lo, hi):
+                        nc.gpsimd.tensor_scalar(dst[:, u], src[:, u], 1.0, 0.0, MULT, ADD)
+                else:
+                    dst = bf[:].rearrange("p (u c t) -> p c t u", u=4, t=4)
+                    src = raw[:].rearrange("p t (c u) -> p c t u", u=4)
+                    cols = slice(lo * 32, hi * 32)
+                    if e == "s":
+                        nc.scalar.copy(dst[:, cols], src[:, cols])
+                    else:
+                        nc.vector.tensor_copy(dst[:, cols], src[:, cols])
             return bf
 
-        def deal_gc(b, engine):
-            g_raw, c_raw = gc_raw[b]
-            g_w = kept("g_w%d" % b, [P, 2, PASS // 2], I32)
-            c_w = kept("c_w%d" % b, [P, 2, PASS], I32)
+        def deal_scales(engine):
+            gc_s = kept("gc_s", [P, 2 * H], U8)
             engine.tensor_copy(
-                g_w[:].rearrange("p a (t g j) -> p a g t j", t=4, j=2),
-                g_raw[:].rearrange("p a (g t j) -> p a g t j", t=4, j=2),
+                gc_s[:].bitcast(I32).rearrange("p (ab t g j) -> p ab t g j", ab=4, t=4, j=RUN // 4),
+                gc_s_raw[:].bitcast(I32).rearrange("p (ab g t j) -> p ab t g j", ab=4, t=4, j=RUN // 4),
             )
+            return gc_s
+
+        def deal_g(b, engine):
+            g_w = kept("g_w%d" % b, [P, 2, PASS // 2], I32)
+            engine.tensor_copy(
+                g_w[:].rearrange("p a (t g j) -> p a t g j", t=4, j=RUN // 2),
+                g_raw[:, :, b * PASS // 2 : (b + 1) * PASS // 2].rearrange("p a (g t j) -> p a t g j", t=4, j=RUN // 2),
+            )
+            return g_w
+
+        def deal_c(b, engine):
+            c_w = kept("c_w%d" % b, [P, 2, PASS], I32)
             for a in range(2):
                 engine.tensor_copy(
-                    c_w[:, a, :].rearrange("p (t g j) -> p g t j", t=4, j=4),
-                    c_raw[:, a, :].rearrange("p (g t j) -> p g t j", t=4, j=4),
+                    c_w[:, a, :].rearrange("p (t g j) -> p t g j", t=4, j=RUN),
+                    c_raw[b][:, a, :].rearrange("p (g t j) -> p t g j", t=4, j=RUN),
                 )
-            return g_w, c_w
+            return c_w
 
         def a_pass(acc, weights, a, t, h):
-            codes, scales = weights[a]
-            cols, picked = slice(t * P, (t + 1) * P), slice(h * BANK, (h + 1) * BANK)
+            codes, scales = weights
+            cols = slice(t * P, (t + 1) * P)
             nc.tensor.matmul_mx(
                 out=acc[:], lhsT=codes[:, cols].bitcast(FP8X4), lhsT_scale=scales[:, cols],
-                rhs=v_w[a][:, picked].bitcast(FP8X4), rhs_scale=v_s[4 * a :, picked],
+                rhs=v_w[a, h][:].bitcast(FP8X4), rhs_scale=v_s[4 * a :, h * BANK : (h + 1) * BANK],
                 start=(a == 0), stop=(a == 1),
             )
 
-        def pick_heads(accs, a_picked, t):
-            row = staged.tile([P, S], F32, name="row", tag="staged", align_bytes=64)
+        def a_row(b, t, accs):
+            row = by_scalar("row%d%d" % (b, t), [P, S], F32)
             for h in range(2):
                 nc.scalar.copy(row[:, h * BANK : (h + 1) * BANK], accs[h][:])
-            nc.vector.tensor_copy(a_picked[:, t, :], row[:].indirect(heads[:]))
+            return row
 
-        def gated(b, t, g_w, c_w, sc):
-            g_acc = psum.tile([P, BANK], F32, name="acc")
-            c_acc = psum.tile([P, BANK], F32, name="acc")
+        def a_tile(b, t):
+            accs = [bank("a%d%d" % (b, t), [P, BANK]) for h in range(2)]
+            for h in range(2):
+                for a in range(2):
+                    a_pass(accs[h], wa_q[a, b], a, t, h)
+            return a_row(b, t, accs)
+
+        def gate_tile(b, t):
+            g_acc = bank("g%d%d" % (b, t), [P, BANK])
             for a in range(2):
                 cols = slice(a * H + b * PASS + t * P, a * H + b * PASS + (t + 1) * P)
                 nc.tensor.matmul_mx(
-                    out=g_acc[:], lhsT=g_w[:, a, t * P // 2 : (t + 1) * P // 2].bitcast(FP4X4), lhsT_scale=gc_s[:, cols],
+                    out=g_acc[:], lhsT=g_w[b][:, a, t * P // 2 : (t + 1) * P // 2].bitcast(FP4X4), lhsT_scale=gc_s[:, cols],
                     rhs=v2_w[a][:].bitcast(FP8X4), rhs_scale=(v2_s, v2_s_up)[a][:],
                     start=(a == 0), stop=(a == 1),
                 )
+            gate = by_scalar("gate%d%d" % (b, t), [P, M], F32)
+            nc.scalar.activation(gate[:], g_acc[:], SILU)
+            return gate
+
+        def c_tile(b, t):
+            c_acc = bank("c%d%d" % (b, t), [P, BANK])
             for a in range(2):
                 cols = slice(a * H + b * PASS + t * P, a * H + b * PASS + (t + 1) * P)
                 nc.tensor.matmul_mx(
-                    out=c_acc[:], lhsT=c_w[:, a, t * P : (t + 1) * P].bitcast(FP8X4), lhsT_scale=gc_s[4:, cols],
+                    out=c_acc[:], lhsT=c_w[b][:, a, t * P : (t + 1) * P].bitcast(FP8X4), lhsT_scale=gc_s[4:, cols],
                     rhs=v2_w[a][:].bitcast(FP8X4), rhs_scale=v2_s[4 * a :, :],
                     start=(a == 0), stop=(a == 1),
                 )
-            gate = staged.tile([P, M], F32, name="gate", tag="staged", align_bytes=64)
-            nc.scalar.activation(gate[:], g_acc[:], SILU)
-            nc.vector.tensor_tensor(sc[:, t, :], c_acc[:], gate[:], MULT)
+            return c_acc
 
-        def in_fours(planes, lo, hi):
-            return planes[:, :, lo:hi].rearrange("p t (c i) -> p c t i", i=4)
+        def product(b, t, gate, c_acc):
+            sc = by_vector("sc%d%d" % (b, t), [P, M], F32)
+            nc.vector.tensor_tensor(sc[:], c_acc[:], gate[:], MULT)
+            return sc
 
-        def woven(bf, lo, hi):
-            return bf[:, PACK * lo : PACK * hi].rearrange("p (c i t) -> p c t i", i=4, t=PACK)
+        def pick_minus(dst, row, sc, lo, hi):
+            nc.vector.tensor_tensor(dst, row[:].indirect(heads[:, lo // 16 : hi // 16]), sc[:, lo:hi], SUB)
 
-        def quantise_cols(codes, scales, bf, lo, hi):
-            nc.vector.quantize_mx(out=codes[:, lo:hi].bitcast(FP8X4), scales=scales[:, lo:hi], in_=bf[:, PACK * lo : PACK * hi])
+        def pick(dst, row, lo, hi):
+            nc.vector.tensor_copy(dst, row[:].indirect(heads[:, lo // 16 : hi // 16]))
 
-        v_w, v2_w, wa_q, wo_q = {}, {}, {}, {}
-        v_w[0] = gather("v_w0", S, U32, tab_w[0], idx)
-        v_s = gather("v_s", S, U8, tab_s, idx)
-        wa_q[0] = quantise("wa00", round_wa(0, 0, 0), "early")
-        accs = [[psum.tile([P, BANK], F32, name="acc") for h in range(2)] for t in range(4)]
-        for t in range(4):
-            for h in range(2):
-                a_pass(accs[t][h], wa_q, 0, t, h)
-        v_w[1] = gather("v_w1", S, U32, tab_w[1], idx, "early")
-        wa_q[1] = quantise("wa10", round_wa(1, 0, 2))
-        v2_s = gather("v2_s", M, U8, tab2_s, idx2)
-        nc.scalar.dma_start(v2_s_up[: P - 4, :].bitcast(I32), v2_s[4:, :].bitcast(I32))
-        second_half = [quantise("wa01", round_wa(0, 1, 2))]
-        a_picked = [kept("a_picked0", [P, 4, M], F32), keep.tile([P, 4, M], F32, name="a_picked1", tag="tab2_w1", align_bytes=64)]
-        for t in range(4):
-            if t == 2:
-                second_half.append(quantise("wa11", round_wa(1, 1, 0)))
-            for h in range(2):
-                a_pass(accs[t][h], wa_q, 1, t, h)
-            pick_heads(accs[t], a_picked[0], t)
-        wo_raw = [load_wo(0), load_wo(1)]
+        def in_fours(planes):
+            return planes.rearrange("p t (c i) -> p c t i", i=4)
 
-        v2_w[0] = gather("v2_w0", M, U32, tab2_w[0], idx2)
-        v2_w[1] = gather("v2_w1", M, U32, tab2_w[1], idx2)
-        gc_s = kept("gc_s", [P, 2 * H], U8)
-        nc.gpsimd.tensor_copy(
-            gc_s[:].bitcast(I32).rearrange("p (ab t g) -> p ab g t", ab=4, t=4),
-            gc_s_raw[:].bitcast(I32).rearrange("p (ab g t) -> p ab g t", ab=4, t=4),
-        )
-        gc_w = [deal_gc(0, nc.gpsimd), deal_gc(1, nc.gpsimd)]
-        sc = [kept("sc%d" % b, [P, 4, M], F32) for b in range(2)]
-        z_bf = [kept("z_bf%d" % b, [P, PACK * M], BF16) for b in range(2)]
-        z_w = [kept("z_w%d" % b, [P, M], U32) for b in range(2)]
-        z_s = [kept("z_s%d" % b, [P, M], U8) for b in range(2)]
-        for t in range(4):
-            pair = [psum.tile([P, BANK], F32, name="acc") for h in range(2)]
-            for h in range(2):
-                for a in range(2):
-                    a_pass(pair[h], second_half, a, t, h)
-            pick_heads(pair, a_picked[1], t)
-        for t in range(4):
-            if t == 2:
-                wo_q[0] = quantise("wo0", round_wo(wo_raw[0]))
-            gated(0, t, *gc_w[0], sc[0])
-        for lo in range(0, M, M):
-            hi = lo + M
-            nc.vector.tensor_tensor(woven(z_bf[0], lo, hi), in_fours(sc[0], lo, hi), in_fours(a_picked[0], lo, hi), SUB)
-        quantise_cols(z_w[0], z_s[0], z_bf[0], 0, M)
-        for t in range(4):
-            if t == -2:
-                wo_q[0] = quantise("wo0", round_wo(wo_raw[0]))
-            if t == 1:
-                wo_q[1] = quantise("wo1", round_wo(wo_raw[1]))
-            gated(1, t, *gc_w[1], sc[1])
+        def woven(bf):
+            return bf.rearrange("p (c i t) -> p c t i", i=4, t=PACK)
 
-        pieces = M // PIECE
-        y_acc = [psum.tile([P, 4, PIECE], F32, name="acc") for piece in range(pieces)]
+        def round_z(name, minus_z, engine):
+            width = minus_z.shape[2]
+            if engine == "s":
+                bf = by_scalar(name, [P, PACK * width], BF16)
+                nc.scalar.activation(woven(bf[:]), in_fours(minus_z[:]), COPY, scale=-1.0)
+            elif engine == "v":
+                bf = by_vector(name, [P, PACK * width], BF16)
+                nc.vector.tensor_scalar(woven(bf[:]), in_fours(minus_z[:]), -1.0, None, MULT)
+            else:
+                bf = kept(name, [P, PACK * width], BF16)
+                nc.gpsimd.tensor_scalar(
+                    bf[:].rearrange("p (c t) -> p c t", t=PACK), minus_z[:].rearrange("p t c -> p c t"), -1.0, 0.0, MULT, ADD
+                )
+            return bf
 
-        def y_pass(b, lo):
-            hi = lo + PIECE
+        def y_pass(acc, b, z_q, lo, hi):
             for u in range(4):
                 cols = slice(u * P, (u + 1) * P)
                 nc.tensor.matmul_mx(
-                    out=y_acc[lo // PIECE][:, u, :], lhsT=wo_q[b][0][:, cols].bitcast(FP8X4), lhsT_scale=wo_q[b][1][:, cols],
-                    rhs=z_w[b][:, lo:hi].bitcast(FP8X4), rhs_scale=z_s[b][:, lo:hi],
+                    out=acc[:, u, :], lhsT=wo_q[b][0][:, cols].bitcast(FP8X4), lhsT_scale=wo_q[b][1][:, cols],
+                    rhs=z_q[0][:, lo:hi].bitcast(FP8X4), rhs_scale=z_q[1][:, lo:hi],
                     start=(b == 0 and u == 0), stop=(b == 1 and u == 3),
                 )
 
-        for lo in range(0, M, PIECE):
-            y_pass(0, lo)
-
-        y = kept("y", [P, 4, M], F32)
-        y_bf = kept("y_bf", [P, PACK * M], BF16)
-        y_w = kept("y_w", [P, M], U32)
-        y_s = kept("y_s", [P, M], U8)
+        v_w, v2_w, wa_raw, wa_q, wo_q, gc_raw, g_w, c_w, tab_w, tab2_w = {}, {}, {}, {}, {}, {}, {}, {}, {}, {}
         y_rows = out_0.rearrange("(p u) m -> p u m", u=4)
         y_words = out_1[0].rearrange("p m t -> p (m t)").bitcast(I32)
 
-        def z_piece(lo):
-            hi = lo + PIECE
-            nc.vector.tensor_tensor(woven(z_bf[1], lo, hi), in_fours(sc[1], lo, hi), in_fours(a_picked[1], lo, hi), SUB)
+        nc.vector.memset(tab_s[:].bitcast(I32), 0)
+        nc.vector.memset(tab2_s[:].bitcast(I32), 0)
+        nc.vector.memset(gc_s_raw[:].bitcast(I32), 0)
+        nc.vector.memset(v2_s_up[:].bitcast(I32), 0)
+        warm = kept("warm", [P, 8], F32)
+        nc.vector.memset(warm[:, 0:1], 0.0)
+        nc.scalar.activation(warm[:, 4:5], warm[:, 0:1], SILU)
+        nc.sync.dma_start(idx[:], offs)
+        tab_w[0] = load_table(tab_words, 0, "tab_w0")
+        load_table_scales(nc.gpsimd, tab_s, tab_scales)
+        wa_raw[0, 0] = load_wa(0, 0)
+        tab_w[1] = load_table(tab_words, 1, "tab_w1")
+        wa_raw[1, 0] = load_wa(1, 0)
+        nc.sync.dma_start(idx2[:], offs2)
+        nc.sync.dma_start(heads[:], pos1)
+        load_table_scales(nc.gpsimd, tab2_s, tab2_scales)
+        load_weight_scales(nc.gpsimd, 0, wg_scales)
+        load_weight_scales(nc.gpsimd, 4, wc_scales)
+        tab2_w[0] = load_table(tab2_words, 0, "tab2_w0")
+        tab2_w[1] = load_table(tab2_words, 1, "tab2_w1", shared=True)
+        g_raw = load_g()
+        c_raw = [load_c(0), load_c(1)]
+        wa_raw[0, 1] = load_wa(0, 1)
+        wa_raw[1, 1] = load_wa(1, 1)
+        wo_raw = [load_wo(0), load_wo(1)]
 
-        def y_product(lo):
-            hi = lo + PIECE
-            quantise_cols(z_w[1], z_s[1], z_bf[1], lo, hi)
-            y_pass(1, lo)
-            nc.scalar.copy(y[:, :, lo:hi], y_acc[lo // PIECE][:])
-            nc.sync.dma_start(y_rows[:, :, lo:hi], y[:, :, lo:hi])
+        for h in range(2):
+            v_w[0, h] = gather("v_w0%d" % h, U32, tab_w[0], idx, h * BANK, (h + 1) * BANK)
+        v_s = gather("v_s", U8, tab_s, idx, 0, S)
+        wa_q[0, 0] = quantise("wa00", round_wa(wa_raw[0, 0], "bf00", "ssss"))
+        accs = [[bank("a0%d" % t, [P, BANK]) for h in range(2)] for t in range(4)]
+        for t in range(4):
+            for h in range(2):
+                a_pass(accs[t][h], wa_q[0, 0], 0, t, h)
+        for h in range(2):
+            v_w[1, h] = gather("v_w1%d" % h, U32, tab_w[1], idx, h * BANK, (h + 1) * BANK)
+        wa_q[1, 0] = quantise("wa10", round_wa(wa_raw[1, 0], "bf10", "ssvv"))
+        rows = {}
+        for t in range(4):
+            for h in range(2):
+                a_pass(accs[t][h], wa_q[1, 0], 1, t, h)
+            rows[0, t] = a_row(0, t, accs[t])
+        v2_s = gather("v2_s", U8, tab2_s, idx2, 0, M)
+        nc.gpsimd.dma_start(v2_s_up[: P - 4, :].bitcast(I32), v2_s[4:, :].bitcast(I32))
+        gc_s = deal_scales(nc.gpsimd)
+        v2_w[0] = gather("v2_w0", U32, tab2_w[0], idx2, 0, M)
+        v2_w[1] = gather("v2_w1", U32, tab2_w[1], idx2, 0, M)
+        a_picked = keep.tile([P, 4, M], F32, name="a_picked", tag="shared", align_bytes=64)
+        g_w[0] = deal_g(0, nc.gpsimd)
+        g_w[1] = deal_g(1, nc.gpsimd)
+        c_w[0] = deal_c(0, nc.gpsimd)
+        c_w[1] = deal_c(1, nc.gpsimd)
+        sc0 = kept("sc0", [P, 4, M], F32)
+        for t in range(4):
+            pick(a_picked[:, t, :], rows[0, t], 0, M)
+        gates = {}
+        for t in range(4):
+            gates[0, t] = gate_tile(0, t)
+        for t in range(4):
+            nc.vector.tensor_tensor(sc0[:, t, :], c_tile(0, t)[:], gates[0, t][:], MULT)
+        sc1 = {}
+        bf01 = round_wa(wa_raw[0, 1], "bf01", "ssss")
+        z0_bf = kept("z0_bf", [P, PACK * M], BF16)
 
-        def y_round(lo):
-            nc.vector.tensor_copy(woven(y_bf, lo, lo + PIECE), in_fours(y, lo, lo + PIECE))
+        def subtract(lo, hi):
+            nc.vector.tensor_tensor(woven(z0_bf[:, PACK * lo : PACK * hi]), in_fours(sc0[:, :, lo:hi]), in_fours(a_picked[:, :, lo:hi]), SUB)
 
-        def y_planes(lo):
-            hi = lo + PIECE
-            quantise_cols(y_w, y_s, y_bf, lo, hi)
-            if hi % (2 * PIECE) == 0:
+        subtract(0, M // 2)
+        bf11 = round_wa(wa_raw[1, 1], "bf11", "ssvv")
+        for t in range(4):
+            gates[1, t] = gate_tile(1, t)
+        c_acc = [c_tile(1, t) for t in range(4)]
+        wa_q[0, 1] = quantise("wa01", bf01)
+        wa_q[1, 1] = quantise("wa11", bf11)
+        subtract(M // 2, M)
+        wo_bf0 = round_wo(wo_raw[0], "wo_bf0", "vvvv")
+        for t in range(4):
+            sc1[t] = product(1, t, gates[1, t], c_acc[t])
+        z0 = quantise("z0", z0_bf)
+        for t in range(4):
+            rows[1, t] = a_tile(1, t)
+            if t == 1:
+                wo_q[0] = quantise("wo0", wo_bf0)
+        wo_bf1 = round_wo(wo_raw[1], "wo_bf1", "ssss")
+        PIECE = 128
+        pieces = M // PIECE
+        y_acc = [bank("y%d" % piece, [P, 4, PIECE]) for piece in range(pieces)]
+        for piece in range(pieces):
+            y_pass(y_acc[piece], 0, z0, piece * PIECE, (piece + 1) * PIECE)
+
+        y_w = kept("y_w", [P, M], U32)
+        y_s = kept("y_s", [P, M], U8)
+        state = {}
+
+        def z_piece(n):
+            lo, hi = n * PIECE, (n + 1) * PIECE
+            minus_z = by_vector("minus_z1%d" % n, [P, 4, PIECE], F32)
+            for t in range(4):
+                pick_minus(minus_z[:, t, :], rows[1, t], sc1[t], lo, hi)
+            state[n] = minus_z
+
+        def z_round(n):
+            state[n] = round_z("z1_bf%d" % n, state[n], "s")
+
+        def y_product(n):
+            if n == 0:
+                wo_q[1] = quantise("wo1", wo_bf1)
+            z_q = quantise("z1%d" % n, state[n])
+            y_pass(y_acc[n], 1, z_q, 0, PIECE)
+            y = by_scalar("y%d" % n, [P, 4, PIECE], F32)
+            nc.scalar.copy(y[:], y_acc[n][:])
+            nc.sync.dma_start(y_rows[:, :, n * PIECE : (n + 1) * PIECE], y[:])
+            state[n] = y
+
+        def y_round(n):
+            y_bf = by_vector("y_bf%d" % n, [P, PACK * PIECE], BF16)
+            nc.vector.tensor_copy(woven(y_bf[:]), in_fours(state[n][:]))
+            state[n] = y_bf
+
+        def y_planes(n):
+            lo, hi = n * PIECE, (n + 1) * PIECE
+            nc.vector.quantize_mx(out=y_w[:, lo:hi].bitcast(FP8X4), scales=y_s[:, lo:hi], in_=state[n][:])
+            if n % 2 == 1:
                 nc.sync.dma_start(y_words[:, hi - 2 * PIECE : hi], y_w[:, hi - 2 * PIECE : hi].bitcast(I32))
 
-        stages = (z_piece, y_product, y_round, y_planes)
-        for step in range(pieces + len(stages) - 1):
-            for lag, stage in enumerate(stages):
+        stages = ((z_piece, 0), (z_round, 0), (y_round, 3), (y_product, 1), (y_planes, 3))
+        for step in range(pieces + 5):
+            for stage, lag in stages:
                 if 0 <= step - lag < pieces:
-                    stage((step - lag) * PIECE)
+                    stage(step - lag)
         for q in range(4):
             (nc.scalar, nc.sync)[q % 2].dma_start(out_2[0, 4 * q : 4 * q + 4, :].bitcast(I32), y_s[32 * q : 32 * q + 4, :].bitcast(I32))

@@ -282,22 +282,16 @@ def tile_list_expense_overspend_signals_kernel(
         nc.scalar.activation(warm[:, 4:5], warm[:, 0:1], SILU)
         nc.sync.dma_start(idx[:], offs)
         tab_w[0] = load_table(tab_words, 0, "tab_w0")
-        load_table_scales(nc.gpsimd, tab_s, tab_scales)
+        load_table_scales(nc.sync, tab_s, tab_scales)
         wa_raw[0, 0] = load_wa(0, 0)
         tab_w[1] = load_table(tab_words, 1, "tab_w1")
-        wa_raw[1, 0] = load_wa(1, 0)
         nc.sync.dma_start(idx2[:], offs2)
+        load_table_scales(nc.sync, tab2_s, tab2_scales)
+        wa_raw[1, 0] = load_wa(1, 0)
         nc.sync.dma_start(heads[:], pos1)
-        load_table_scales(nc.gpsimd, tab2_s, tab2_scales)
-        load_weight_scales(nc.gpsimd, 0, wg_scales)
-        load_weight_scales(nc.gpsimd, 4, wc_scales)
         tab2_w[0] = load_table(tab2_words, 0, "tab2_w0")
+        load_weight_scales(nc.sync, 0, wg_scales)
         tab2_w[1] = load_table(tab2_words, 1, "tab2_w1", shared=True)
-        g_raw = load_g()
-        c_raw = [load_c(0), load_c(1)]
-        wa_raw[0, 1] = load_wa(0, 1)
-        wa_raw[1, 1] = load_wa(1, 1)
-        wo_raw = [load_wo(0), load_wo(1)]
 
         for h in range(2):
             v_w[0, h] = gather("v_w0%d" % h, U32, tab_w[0], idx, h * BANK, (h + 1) * BANK)
@@ -309,14 +303,20 @@ def tile_list_expense_overspend_signals_kernel(
                 a_pass(accs[t][h], wa_q[0, 0], 0, t, h)
         for h in range(2):
             v_w[1, h] = gather("v_w1%d" % h, U32, tab_w[1], idx, h * BANK, (h + 1) * BANK)
+        v2_s = gather("v2_s", U8, tab2_s, idx2, 0, M)
+        nc.sync.dma_start(v2_s_up[:100, :].bitcast(I32), v2_s[4:104, :].bitcast(I32))
+        load_weight_scales(nc.sync, 4, wc_scales)
+        g_raw = load_g()
+        c_raw = [load_c(0), load_c(1)]
+        wa_raw[0, 1] = load_wa(0, 1)
+        wa_raw[1, 1] = load_wa(1, 1)
+        wo_raw = [load_wo(0), load_wo(1)]
         wa_q[1, 0] = quantise("wa10", round_wa(wa_raw[1, 0], "bf10", "ssvv"))
         rows = {}
         for t in range(4):
             for h in range(2):
                 a_pass(accs[t][h], wa_q[1, 0], 1, t, h)
             rows[0, t] = a_row(0, t, accs[t])
-        v2_s = gather("v2_s", U8, tab2_s, idx2, 0, M)
-        nc.gpsimd.dma_start(v2_s_up[: P - 4, :].bitcast(I32), v2_s[4:, :].bitcast(I32))
         gc_s = deal_scales(nc.gpsimd)
         v2_w[0] = gather("v2_w0", U32, tab2_w[0], idx2, 0, M)
         v2_w[1] = gather("v2_w1", U32, tab2_w[1], idx2, 0, M)

@@ -24,8 +24,10 @@ PACK = 4
 PASS = P * PACK
 BANK = 512
 RUN = 8
-V_BUFS = 22
+V_BUFS = 28
 S_BUFS = 12
+L_BUFS = 7
+SHARE = {"tab2_w1":"h0","a_picked00":"h0","c_raw0":"h1","a_picked01":"h1","z0_bf0":"by_vector","z0_bf1":"by_vector","gc_s":"by_vector","g_w0":"by_vector","g_w1":"by_vector","c_w10":"by_vector","c_w11":"by_vector"}
 
 
 def tile_list_expense_overspend_signals_kernel(
@@ -38,17 +40,23 @@ def tile_list_expense_overspend_signals_kernel(
         keep = ctx.enter_context(tc.tile_pool(name="keep", bufs=1))
         psum = ctx.enter_context(tc.psum_pool(name="psum", bufs=8))
 
+        def made(name, shape, dtype, tag, bufs):
+            if name in SHARE:
+                tag = SHARE[name]
+                bufs = {"by_vector": V_BUFS, "by_scalar": S_BUFS}.get(tag, 1)
+            return keep.tile(shape, dtype, name=name, tag=tag, bufs=bufs, align_bytes=64)
+
         def kept(name, shape, dtype):
-            return keep.tile(shape, dtype, name=name, align_bytes=64)
+            return made(name, shape, dtype, name, 1)
 
         def loaded(name, shape, dtype):
-            return keep.tile(shape, dtype, name=name, tag="loaded", bufs=7, align_bytes=64)
+            return made(name, shape, dtype, "loaded", L_BUFS)
 
         def by_vector(name, shape, dtype):
-            return keep.tile(shape, dtype, name=name, tag="by_vector", bufs=V_BUFS, align_bytes=64)
+            return made(name, shape, dtype, "by_vector", V_BUFS)
 
         def by_scalar(name, shape, dtype):
-            return keep.tile(shape, dtype, name=name, tag="by_scalar", bufs=S_BUFS, align_bytes=64)
+            return made(name, shape, dtype, "by_scalar", S_BUFS)
 
         def bank(name, shape):
             return psum.tile(shape, F32, name=name, tag="bank")
@@ -56,10 +64,11 @@ def tile_list_expense_overspend_signals_kernel(
         idx = lists.tile([P, S // 16], U16, name="idx")
         idx2 = lists.tile([P, M // 16], U16, name="idx2")
         heads = lists.tile([P, M // 16], U16, name="heads")
-        tab_s = kept("tab_s", [P, T], U8)
-        tab2_s = kept("tab2_s", [P, T], U8)
-        gc_s_raw = kept("gc_s_raw", [P, 2 * H], U8)
-        v2_s_up = kept("v2_s_up", [P, M], U8)
+
+        def zeroed(name, width):
+            tile = kept(name, [P, width], U8)
+            nc.vector.memset(tile[:].bitcast(I32), 0)
+            return tile
 
         def load_table_scales(queue, tile, scales):
             for q in range(4):
@@ -73,8 +82,8 @@ def tile_list_expense_overspend_signals_kernel(
                     scales[:, 4 * q : 4 * q + 4, :].bitcast(I32).rearrange("a r e -> r a e"),
                 )
 
-        def load_table(words, a, name, shared=False):
-            tile = keep.tile([P, T], U32, name=name, tag="shared", align_bytes=64) if shared else loaded(name, [P, T], U32)
+        def load_table(words, a, name):
+            tile = loaded(name, [P, T], U32)
             nc.sync.dma_start(tile[:].bitcast(I32), words[a].rearrange("p t i -> p (t i)").bitcast(I32))
             return tile
 
@@ -131,12 +140,13 @@ def tile_list_expense_overspend_signals_kernel(
                     for t in range(lo, hi):
                         nc.gpsimd.tensor_scalar(dst[:, t], src[:, t], 1.0, 0.0, MULT, ADD)
                 else:
-                    dst = bf[:].rearrange("p (t g j i) -> p t g i j", t=4, j=RUN, i=PACK)
-                    src = raw[:].rearrange("p i (g t j) -> p t g i j", t=4, j=RUN)
-                    if e == "s":
-                        nc.scalar.copy(dst[:, lo:hi], src[:, lo:hi])
-                    else:
-                        nc.vector.tensor_copy(dst[:, lo:hi], src[:, lo:hi])
+                    dst = bf[:].rearrange("p (t g h j i) -> p t g h i j", t=4, h=RUN // 4, j=4, i=PACK)
+                    src = raw[:].rearrange("p i (g t h j) -> p t g h i j", t=4, h=RUN // 4, j=4)
+                    for t in range(lo, hi):
+                        if e == "s":
+                            nc.scalar.copy(dst[:, t], src[:, t])
+                        else:
+                            nc.vector.tensor_copy(dst[:, t], src[:, t])
             return bf
 
         def round_wo(raw, name, plan):
@@ -173,13 +183,12 @@ def tile_list_expense_overspend_signals_kernel(
             )
             return g_w
 
-        def deal_c(b, engine):
-            c_w = kept("c_w%d" % b, [P, 2, PASS], I32)
-            for a in range(2):
-                engine.tensor_copy(
-                    c_w[:, a, :].rearrange("p (t g j) -> p t g j", t=4, j=RUN),
-                    c_raw[b][:, a, :].rearrange("p (g t j) -> p t g j", t=4, j=RUN),
-                )
+        def deal_c(b, a, engine):
+            c_w = kept("c_w%d%d" % (b, a), [P, PASS], I32)
+            engine.tensor_copy(
+                c_w[:].rearrange("p (t g j) -> p t g j", t=4, j=RUN),
+                c_raw[b][:, a, :].rearrange("p (g t j) -> p t g j", t=4, j=RUN),
+            )
             return c_w
 
         def a_pass(acc, weights, a, t, h):
@@ -222,7 +231,7 @@ def tile_list_expense_overspend_signals_kernel(
             for a in range(2):
                 cols = slice(a * H + b * PASS + t * P, a * H + b * PASS + (t + 1) * P)
                 nc.tensor.matmul_mx(
-                    out=c_acc[:], lhsT=c_w[b][:, a, t * P : (t + 1) * P].bitcast(FP8X4), lhsT_scale=gc_s[4:, cols],
+                    out=c_acc[:], lhsT=c_w[b, a][:, t * P : (t + 1) * P].bitcast(FP8X4), lhsT_scale=gc_s[4:, cols],
                     rhs=v2_w[a][:].bitcast(FP8X4), rhs_scale=v2_s[4 * a :, :],
                     start=(a == 0), stop=(a == 1),
                 )
@@ -272,96 +281,136 @@ def tile_list_expense_overspend_signals_kernel(
         v_w, v2_w, wa_raw, wa_q, wo_q, gc_raw, g_w, c_w, tab_w, tab2_w = {}, {}, {}, {}, {}, {}, {}, {}, {}, {}
         y_rows = out_0.rearrange("(p u) m -> p u m", u=4)
         y_words = out_1[0].rearrange("p m t -> p (m t)").bitcast(I32)
+        PIECE = 128
+        HALF = M // 2
+        pieces = M // PIECE
+        sc1 = {}
+        bf, wo_bf, wo_raw, c_raw, rows, gates, c_acc, a_picked, sc, z0_bf, z0 = {}, {}, {}, {}, {}, {}, {}, {}, {}, {}, {}
 
-        nc.vector.memset(tab_s[:].bitcast(I32), 0)
-        nc.vector.memset(tab2_s[:].bitcast(I32), 0)
-        nc.vector.memset(gc_s_raw[:].bitcast(I32), 0)
-        nc.vector.memset(v2_s_up[:].bitcast(I32), 0)
+        def subtract(half):
+            bf = kept("z0_bf%d" % half, [P, PACK * HALF], BF16)
+            nc.vector.tensor_tensor(woven(bf[:]), in_fours(sc[0][:, :, half * HALF : (half + 1) * HALF]), in_fours(a_picked[0, half]), SUB)
+            z0_bf[half] = bf
+
+        def y_first(acc, piece):
+            y_pass(acc, 0, z0[piece // 2], piece % 2 * PIECE, (piece % 2 + 1) * PIECE)
+
+        tab_s = zeroed("tab_s", T)
+        tab2_s = zeroed("tab2_s", T)
+        gc_s_raw = zeroed("gc_s_raw", 2 * H)
+        v2_s_up = zeroed("v2_s_up", M)
         warm = kept("warm", [P, 8], F32)
         nc.vector.memset(warm[:, 0:1], 0.0)
         nc.scalar.activation(warm[:, 4:5], warm[:, 0:1], SILU)
         nc.sync.dma_start(idx[:], offs)
         tab_w[0] = load_table(tab_words, 0, "tab_w0")
         load_table_scales(nc.sync, tab_s, tab_scales)
-        wa_raw[0, 0] = load_wa(0, 0)
-        tab_w[1] = load_table(tab_words, 1, "tab_w1")
         nc.sync.dma_start(idx2[:], offs2)
+        wa_raw[0, 0] = load_wa(0, 0)
         load_table_scales(nc.sync, tab2_s, tab2_scales)
+        tab_w[1] = load_table(tab_words, 1, "tab_w1")
         wa_raw[1, 0] = load_wa(1, 0)
         nc.sync.dma_start(heads[:], pos1)
-        tab2_w[0] = load_table(tab2_words, 0, "tab2_w0")
         load_weight_scales(nc.sync, 0, wg_scales)
-        tab2_w[1] = load_table(tab2_words, 1, "tab2_w1", shared=True)
-
+        tab2_w[0] = load_table(tab2_words, 0, "tab2_w0")
+        load_weight_scales(nc.sync, 4, wc_scales)
+        g_raw = load_g()
+        tab2_w[1] = load_table(tab2_words, 1, "tab2_w1")
         for h in range(2):
             v_w[0, h] = gather("v_w0%d" % h, U32, tab_w[0], idx, h * BANK, (h + 1) * BANK)
         v_s = gather("v_s", U8, tab_s, idx, 0, S)
-        wa_q[0, 0] = quantise("wa00", round_wa(wa_raw[0, 0], "bf00", "ssss"))
+        v2_s = gather("v2_s", U8, tab2_s, idx2, 0, M)
+        bf[0, 0] = round_wa(wa_raw[0, 0], "bf00", "ssss")
+        wa_q[0, 0] = quantise("wa00", bf[0, 0])
         accs = [[bank("a0%d" % t, [P, BANK]) for h in range(2)] for t in range(4)]
         for t in range(4):
             for h in range(2):
                 a_pass(accs[t][h], wa_q[0, 0], 0, t, h)
         for h in range(2):
             v_w[1, h] = gather("v_w1%d" % h, U32, tab_w[1], idx, h * BANK, (h + 1) * BANK)
-        v2_s = gather("v2_s", U8, tab2_s, idx2, 0, M)
         nc.sync.dma_start(v2_s_up[:100, :].bitcast(I32), v2_s[4:104, :].bitcast(I32))
-        load_weight_scales(nc.sync, 4, wc_scales)
-        g_raw = load_g()
-        c_raw = [load_c(0), load_c(1)]
+        c_raw[0] = load_c(0)
+        c_raw[1] = load_c(1)
         wa_raw[0, 1] = load_wa(0, 1)
         wa_raw[1, 1] = load_wa(1, 1)
-        wo_raw = [load_wo(0), load_wo(1)]
-        wa_q[1, 0] = quantise("wa10", round_wa(wa_raw[1, 0], "bf10", "ssvv"))
-        rows = {}
-        for t in range(4):
-            for h in range(2):
-                a_pass(accs[t][h], wa_q[1, 0], 1, t, h)
-            rows[0, t] = a_row(0, t, accs[t])
-        gc_s = deal_scales(nc.gpsimd)
+        wo_raw[0] = load_wo(0)
+        wo_raw[1] = load_wo(1)
+        bf[1, 0] = round_wa(wa_raw[1, 0], "bf10", "ssvv")
+        wa_q[1, 0] = quantise("wa10", bf[1, 0])
+        for h in range(2):
+            a_pass(accs[0][h], wa_q[1, 0], 1, 0, h)
+        rows[0, 0] = a_row(0, 0, accs[0])
+        for h in range(2):
+            a_pass(accs[1][h], wa_q[1, 0], 1, 1, h)
+        rows[0, 1] = a_row(0, 1, accs[1])
+        for h in range(2):
+            a_pass(accs[2][h], wa_q[1, 0], 1, 2, h)
+        rows[0, 2] = a_row(0, 2, accs[2])
+        for h in range(2):
+            a_pass(accs[3][h], wa_q[1, 0], 1, 3, h)
+        rows[0, 3] = a_row(0, 3, accs[3])
         v2_w[0] = gather("v2_w0", U32, tab2_w[0], idx2, 0, M)
+        gc_s = deal_scales(nc.vector)
+        g_w[0] = deal_g(0, nc.vector)
+        g_w[1] = deal_g(1, nc.vector)
         v2_w[1] = gather("v2_w1", U32, tab2_w[1], idx2, 0, M)
-        a_picked = keep.tile([P, 4, M], F32, name="a_picked", tag="shared", align_bytes=64)
-        g_w[0] = deal_g(0, nc.gpsimd)
-        g_w[1] = deal_g(1, nc.gpsimd)
-        c_w[0] = deal_c(0, nc.gpsimd)
-        c_w[1] = deal_c(1, nc.gpsimd)
-        sc0 = kept("sc0", [P, 4, M], F32)
-        for t in range(4):
-            pick(a_picked[:, t, :], rows[0, t], 0, M)
-        gates = {}
-        for t in range(4):
-            gates[0, t] = gate_tile(0, t)
-        for t in range(4):
-            nc.vector.tensor_tensor(sc0[:, t, :], c_tile(0, t)[:], gates[0, t][:], MULT)
-        sc1 = {}
-        bf01 = round_wa(wa_raw[0, 1], "bf01", "ssss")
-        z0_bf = kept("z0_bf", [P, PACK * M], BF16)
-
-        def subtract(lo, hi):
-            nc.vector.tensor_tensor(woven(z0_bf[:, PACK * lo : PACK * hi]), in_fours(sc0[:, :, lo:hi]), in_fours(a_picked[:, :, lo:hi]), SUB)
-
-        subtract(0, M // 2)
-        bf11 = round_wa(wa_raw[1, 1], "bf11", "ssvv")
-        for t in range(4):
-            gates[1, t] = gate_tile(1, t)
-        c_acc = [c_tile(1, t) for t in range(4)]
-        wa_q[0, 1] = quantise("wa01", bf01)
-        wa_q[1, 1] = quantise("wa11", bf11)
-        subtract(M // 2, M)
-        wo_bf0 = round_wo(wo_raw[0], "wo_bf0", "vvvv")
-        for t in range(4):
-            sc1[t] = product(1, t, gates[1, t], c_acc[t])
-        z0 = quantise("z0", z0_bf)
-        for t in range(4):
-            rows[1, t] = a_tile(1, t)
-            if t == 1:
-                wo_q[0] = quantise("wo0", wo_bf0)
-        wo_bf1 = round_wo(wo_raw[1], "wo_bf1", "ssss")
-        PIECE = 128
-        pieces = M // PIECE
+        a_picked[0, 0] = kept("a_picked00", [P, 4, HALF], F32)[:]
+        pick(a_picked[0, 0][:, 0, :], rows[0, 0], 0 * HALF, 1 * HALF)
+        pick(a_picked[0, 0][:, 1, :], rows[0, 1], 0 * HALF, 1 * HALF)
+        pick(a_picked[0, 0][:, 2, :], rows[0, 2], 0 * HALF, 1 * HALF)
+        pick(a_picked[0, 0][:, 3, :], rows[0, 3], 0 * HALF, 1 * HALF)
+        c_w[0, 0] = deal_c(0, 0, nc.vector)
+        c_w[0, 1] = deal_c(0, 1, nc.vector)
+        a_picked[0, 1] = kept("a_picked01", [P, 4, HALF], F32)[:]
+        pick(a_picked[0, 1][:, 0, :], rows[0, 0], 1 * HALF, 2 * HALF)
+        pick(a_picked[0, 1][:, 1, :], rows[0, 1], 1 * HALF, 2 * HALF)
+        pick(a_picked[0, 1][:, 2, :], rows[0, 2], 1 * HALF, 2 * HALF)
+        pick(a_picked[0, 1][:, 3, :], rows[0, 3], 1 * HALF, 2 * HALF)
+        c_w[1, 0] = deal_c(1, 0, nc.vector)
+        c_w[1, 1] = deal_c(1, 1, nc.vector)
+        gates[0, 0] = gate_tile(0, 0)
+        gates[0, 1] = gate_tile(0, 1)
+        gates[0, 2] = gate_tile(0, 2)
+        gates[0, 3] = gate_tile(0, 3)
+        gates[1, 0] = gate_tile(1, 0)
+        gates[1, 1] = gate_tile(1, 1)
+        gates[1, 2] = gate_tile(1, 2)
+        gates[1, 3] = gate_tile(1, 3)
+        c_acc[0, 0] = c_tile(0, 0)
+        c_acc[0, 1] = c_tile(0, 1)
+        c_acc[0, 2] = c_tile(0, 2)
+        c_acc[0, 3] = c_tile(0, 3)
+        sc[0] = kept("sc0", [P, 4, M], F32)
+        nc.vector.tensor_tensor(sc[0][:, 0, :], c_acc[0, 0][:], gates[0, 0][:], MULT)
+        nc.vector.tensor_tensor(sc[0][:, 1, :], c_acc[0, 1][:], gates[0, 1][:], MULT)
+        nc.vector.tensor_tensor(sc[0][:, 2, :], c_acc[0, 2][:], gates[0, 2][:], MULT)
+        nc.vector.tensor_tensor(sc[0][:, 3, :], c_acc[0, 3][:], gates[0, 3][:], MULT)
+        bf[0, 1] = round_wa(wa_raw[0, 1], "bf01", "ssss")
+        bf[1, 1] = round_wa(wa_raw[1, 1], "bf11", "ssss")
+        wa_q[0, 1] = quantise("wa01", bf[0, 1])
+        subtract(0)
+        wa_q[1, 1] = quantise("wa11", bf[1, 1])
+        wo_bf[0] = round_wo(wo_raw[0], "wo_bf0", "ssss")
+        subtract(1)
+        c_acc[1, 0] = c_tile(1, 0)
+        c_acc[1, 1] = c_tile(1, 1)
+        rows[1, 0] = a_tile(1, 0)
+        sc1[0] = product(1, 0, gates[1, 0], c_acc[1, 0])
+        sc1[1] = product(1, 1, gates[1, 1], c_acc[1, 1])
+        c_acc[1, 2] = c_tile(1, 2)
+        c_acc[1, 3] = c_tile(1, 3)
+        sc1[2] = product(1, 2, gates[1, 2], c_acc[1, 2])
+        sc1[3] = product(1, 3, gates[1, 3], c_acc[1, 3])
+        z0[0] = quantise("z00", z0_bf[0])
+        z0[1] = quantise("z01", z0_bf[1])
+        wo_q[0] = quantise("wo0", wo_bf[0])
+        rows[1, 1] = a_tile(1, 1)
+        rows[1, 2] = a_tile(1, 2)
+        rows[1, 3] = a_tile(1, 3)
+        wo_bf[1] = round_wo(wo_raw[1], "wo_bf1", "ssvv")
         y_acc = [bank("y%d" % piece, [P, 4, PIECE]) for piece in range(pieces)]
         for piece in range(pieces):
-            y_pass(y_acc[piece], 0, z0, piece * PIECE, (piece + 1) * PIECE)
+            y_first(y_acc[piece], piece)
 
         y_w = kept("y_w", [P, M], U32)
         y_s = kept("y_s", [P, M], U8)
@@ -375,22 +424,27 @@ def tile_list_expense_overspend_signals_kernel(
             state[n] = minus_z
 
         def z_round(n):
-            state[n] = round_z("z1_bf%d" % n, state[n], "s")
+            state[n] = round_z("z1_bf%d" % n, state[n], "ssss"[n])
 
         def y_product(n):
             if n == 0:
-                wo_q[1] = quantise("wo1", wo_bf1)
+                wo_q[1] = quantise("wo1", wo_bf[1])
             z_q = quantise("z1%d" % n, state[n])
-            y_pass(y_acc[n], 1, z_q, 0, PIECE)
+            acc = y_acc[n]
+            y_pass(acc, 1, z_q, 0, PIECE)
             y = by_scalar("y%d" % n, [P, 4, PIECE], F32)
-            nc.scalar.copy(y[:], y_acc[n][:])
+            if n in ():
+                y_bf = by_scalar("y_bf%d" % n, [P, PACK * PIECE], BF16)
+                nc.scalar.copy(woven(y_bf[:]), in_fours(acc[:]))
+            nc.scalar.copy(y[:], acc[:])
             nc.sync.dma_start(y_rows[:, :, n * PIECE : (n + 1) * PIECE], y[:])
-            state[n] = y
+            state[n] = y_bf if n in () else y
 
         def y_round(n):
-            y_bf = by_vector("y_bf%d" % n, [P, PACK * PIECE], BF16)
-            nc.vector.tensor_copy(woven(y_bf[:]), in_fours(state[n][:]))
-            state[n] = y_bf
+            if n not in ():
+                y_bf = by_vector("y_bf%d" % n, [P, PACK * PIECE], BF16)
+                nc.vector.tensor_copy(woven(y_bf[:]), in_fours(state[n][:]))
+                state[n] = y_bf
 
         def y_planes(n):
             lo, hi = n * PIECE, (n + 1) * PIECE
@@ -399,7 +453,7 @@ def tile_list_expense_overspend_signals_kernel(
                 nc.sync.dma_start(y_words[:, hi - 2 * PIECE : hi], y_w[:, hi - 2 * PIECE : hi].bitcast(I32))
 
         stages = ((z_piece, 0), (z_round, 0), (y_round, 3), (y_product, 1), (y_planes, 3))
-        for step in range(pieces + 5):
+        for step in range(pieces + 4):
             for stage, lag in stages:
                 if 0 <= step - lag < pieces:
                     stage(step - lag)

@@ -1,6 +1,7 @@
 from contextlib import ExitStack
 
 import concourse.mybir as mybir
+from concourse.masks import make_identity
 
 K, T, S, M, H, N = 1024, 2048, 1024, 512, 1024, 512
 FLOPS = 2 * K * H * S + 2 * 2 * K * H * M + 2 * H * N * M
@@ -23,11 +24,11 @@ P = 128
 PACK = 4
 PASS = P * PACK
 BANK = 512
-RUN = 8
+RUN = 1
 V_BUFS = 28
 S_BUFS = 12
 L_BUFS = 7
-SHARE = {"tab2_w1":"h0","a_picked00":"h0","c_raw0":"h1","a_picked01":"h1","z0_bf0":"by_vector","z0_bf1":"by_vector","gc_s":"by_vector","g_w0":"by_vector","g_w1":"by_vector","c_w10":"by_vector","c_w11":"by_vector"}
+SHARE = {"tab2_w1":"h0","a_picked0":"h0"}
 
 
 def tile_list_expense_overspend_signals_kernel(
@@ -95,6 +96,9 @@ def tile_list_expense_overspend_signals_kernel(
 
         def load_wo(b):
             raw = loaded("wo%d" % b, [P, PACK, N], F32)
+            if RUN == 1:
+                nc.sync.dma_start(raw[:], wo[b * PASS : (b + 1) * PASS, :].rearrange("(p t) n -> p t n", t=PACK))
+                return raw
             rows = wo[b * PASS : (b + 1) * PASS, :].rearrange("(g t j) n -> t g j n", t=4, j=RUN)
             for t in range(4):
                 nc.sync.dma_start(raw[:, t, :], rows[t])
@@ -132,6 +136,8 @@ def tile_list_expense_overspend_signals_kernel(
             return [(e, plan.index(e), plan.index(e) + plan.count(e)) for e in "svg" if e in plan]
 
         def round_wa(raw, name, plan):
+            if RUN == 1:
+                return round_wo(raw, name, plan)
             bf = rounded(name, plan)
             for e, lo, hi in shares(plan):
                 if e == "g":
@@ -167,30 +173,6 @@ def tile_list_expense_overspend_signals_kernel(
                         nc.vector.tensor_copy(dst[:, cols], src[:, cols])
             return bf
 
-        def deal_scales(engine):
-            gc_s = kept("gc_s", [P, 2 * H], U8)
-            engine.tensor_copy(
-                gc_s[:].bitcast(I32).rearrange("p (ab t g j) -> p ab t g j", ab=4, t=4, j=RUN // 4),
-                gc_s_raw[:].bitcast(I32).rearrange("p (ab g t j) -> p ab t g j", ab=4, t=4, j=RUN // 4),
-            )
-            return gc_s
-
-        def deal_g(b, engine):
-            g_w = kept("g_w%d" % b, [P, 2, PASS // 2], I32)
-            engine.tensor_copy(
-                g_w[:].rearrange("p a (t g j) -> p a t g j", t=4, j=RUN // 2),
-                g_raw[:, :, b * PASS // 2 : (b + 1) * PASS // 2].rearrange("p a (g t j) -> p a t g j", t=4, j=RUN // 2),
-            )
-            return g_w
-
-        def deal_c(b, a, engine):
-            c_w = kept("c_w%d%d" % (b, a), [P, PASS], I32)
-            engine.tensor_copy(
-                c_w[:].rearrange("p (t g j) -> p t g j", t=4, j=RUN),
-                c_raw[b][:, a, :].rearrange("p (g t j) -> p t g j", t=4, j=RUN),
-            )
-            return c_w
-
         def a_pass(acc, weights, a, t, h):
             codes, scales = weights
             cols = slice(t * P, (t + 1) * P)
@@ -213,34 +195,52 @@ def tile_list_expense_overspend_signals_kernel(
                     a_pass(accs[h], wa_q[a, b], a, t, h)
             return a_row(b, t, accs)
 
-        def gate_tile(b, t):
-            g_acc = bank("g%d%d" % (b, t), [P, BANK])
+        def dealt(ap):
+            return ap.rearrange("p (g t j) -> p t g j", t=4, j=RUN)
+
+        def gate_tile(b, n):
+            g_acc = bank("g%d%d" % (b, n), [P, BANK])
+            cols = slice(n * P, (n + 1) * P)
             for a in range(2):
-                cols = slice(a * H + b * PASS + t * P, a * H + b * PASS + (t + 1) * P)
                 nc.tensor.matmul_mx(
-                    out=g_acc[:], lhsT=g_w[b][:, a, t * P // 2 : (t + 1) * P // 2].bitcast(FP4X4), lhsT_scale=gc_s[:, cols],
-                    rhs=v2_w[a][:].bitcast(FP8X4), rhs_scale=(v2_s, v2_s_up)[a][:],
+                    out=g_acc[:], lhsT=v2_w[a][:, cols].bitcast(FP8X4), lhsT_scale=(v2_s, v2_s_up)[a][:, cols],
+                    rhs=g_raw[:, a, b * PASS // 2 : (b + 1) * PASS // 2].bitcast(FP4X4),
+                    rhs_scale=gc_s_raw[:, a * H + b * PASS : a * H + (b + 1) * PASS],
                     start=(a == 0), stop=(a == 1),
                 )
-            gate = by_scalar("gate%d%d" % (b, t), [P, M], F32)
-            nc.scalar.activation(gate[:], g_acc[:], SILU)
+            gate = by_scalar("gate%d%d" % (b, n), [P, PASS], F32)
+            nc.scalar.activation(gate[:].rearrange("p (t g j) -> p t g j", t=4, j=RUN), dealt(g_acc[:]), SILU)
             return gate
 
-        def c_tile(b, t):
-            c_acc = bank("c%d%d" % (b, t), [P, BANK])
+        def c_tile(b, n):
+            c_acc = bank("c%d%d" % (b, n), [P, BANK])
+            cols = slice(n * P, (n + 1) * P)
             for a in range(2):
-                cols = slice(a * H + b * PASS + t * P, a * H + b * PASS + (t + 1) * P)
                 nc.tensor.matmul_mx(
-                    out=c_acc[:], lhsT=c_w[b, a][:, t * P : (t + 1) * P].bitcast(FP8X4), lhsT_scale=gc_s[4:, cols],
-                    rhs=v2_w[a][:].bitcast(FP8X4), rhs_scale=v2_s[4 * a :, :],
+                    out=c_acc[:], lhsT=v2_w[a][:, cols].bitcast(FP8X4), lhsT_scale=v2_s[4 * a :, cols],
+                    rhs=c_raw[b][:, a, :].bitcast(FP8X4), rhs_scale=gc_s_raw[4:, a * H + b * PASS : a * H + (b + 1) * PASS],
                     start=(a == 0), stop=(a == 1),
                 )
             return c_acc
 
-        def product(b, t, gate, c_acc):
-            sc = by_vector("sc%d%d" % (b, t), [P, M], F32)
-            nc.vector.tensor_tensor(sc[:], c_acc[:], gate[:], MULT)
+        def product(b, n, gate, c_acc):
+            sc = by_vector("sc%d%d" % (b, n), [P, PASS], F32)
+            nc.vector.tensor_tensor(
+                sc[:].rearrange("p (t g j) -> p t g j", t=4, j=RUN), dealt(c_acc[:]),
+                gate[:].rearrange("p (t g j) -> p t g j", t=4, j=RUN), MULT,
+            )
             return sc
+
+        def turn(b, n):
+            turned = bank("T%d%d" % (b, n), [P, 4, PIECE])
+            for t in range(4):
+                nc.tensor.transpose(turned[:, t, :], sc[b, n][:, t * P : (t + 1) * P], ident[:])
+            return turned
+
+        def subtract(b, n):
+            bf = by_vector("z%d_bf%d" % (b, n), [P, PACK * PIECE], BF16)
+            nc.vector.tensor_tensor(woven(bf[:]), in_fours(turned[b, n][:]), in_fours(a_picked[b][:, :, n * PIECE : (n + 1) * PIECE]), SUB)
+            return bf
 
         def pick_minus(dst, row, sc, lo, hi):
             nc.vector.tensor_tensor(dst, row[:].indirect(heads[:, lo // 16 : hi // 16]), sc[:, lo:hi], SUB)
@@ -282,18 +282,36 @@ def tile_list_expense_overspend_signals_kernel(
         y_rows = out_0.rearrange("(p u) m -> p u m", u=4)
         y_words = out_1[0].rearrange("p m t -> p (m t)").bitcast(I32)
         PIECE = 128
-        HALF = M // 2
         pieces = M // PIECE
-        sc1 = {}
-        bf, wo_bf, wo_raw, c_raw, rows, gates, c_acc, a_picked, sc, z0_bf, z0 = {}, {}, {}, {}, {}, {}, {}, {}, {}, {}, {}
+        bf, wo_bf, wo_raw, c_raw, rows, gates, c_acc, a_picked, sc, z_bf, z_q, turned, y_acc, y_f, y_bf = {}, {}, {}, {}, {}, {}, {}, {}, {}, {}, {}, {}, {}, {}, {}
+        ident = kept("ident", [P, P], F32)
+        make_identity(nc, ident[:])
+        y_w = kept("y_w", [P, M], U32)
+        y_s = kept("y_s", [P, M], U8)
 
-        def subtract(half):
-            bf = kept("z0_bf%d" % half, [P, PACK * HALF], BF16)
-            nc.vector.tensor_tensor(woven(bf[:]), in_fours(sc[0][:, :, half * HALF : (half + 1) * HALF]), in_fours(a_picked[0, half]), SUB)
-            z0_bf[half] = bf
+        def y_half(b, n):
+            if b == 0:
+                y_acc[n] = bank("y%d" % n, [P, 4, PIECE])
+            y_pass(y_acc[n], b, z_q[b, n], 0, PIECE)
 
-        def y_first(acc, piece):
-            y_pass(acc, 0, z0[piece // 2], piece % 2 * PIECE, (piece % 2 + 1) * PIECE)
+        def y_out(n):
+            y_f[n] = by_scalar("y%d" % n, [P, 4, PIECE], F32)
+            nc.scalar.copy(y_f[n][:], y_acc[n][:])
+            nc.sync.dma_start(y_rows[:, :, n * PIECE : (n + 1) * PIECE], y_f[n][:])
+
+        def y_round(n, engine):
+            if engine == "s":
+                y_bf[n] = by_scalar("y_bf%d" % n, [P, PACK * PIECE], BF16)
+                nc.scalar.copy(woven(y_bf[n][:]), in_fours(y_acc[n][:]))
+            else:
+                y_bf[n] = by_vector("y_bf%d" % n, [P, PACK * PIECE], BF16)
+                nc.vector.tensor_copy(woven(y_bf[n][:]), in_fours((y_f[n] if engine == "v" else y_acc[n])[:]))
+
+        def y_planes(n):
+            lo, hi = n * PIECE, (n + 1) * PIECE
+            nc.vector.quantize_mx(out=y_w[:, lo:hi].bitcast(FP8X4), scales=y_s[:, lo:hi], in_=y_bf[n][:])
+            if n % 2 == 1:
+                nc.sync.dma_start(y_words[:, hi - 2 * PIECE : hi], y_w[:, hi - 2 * PIECE : hi].bitcast(I32))
 
         tab_s = zeroed("tab_s", T)
         tab2_s = zeroed("tab2_s", T)
@@ -311,10 +329,7 @@ def tile_list_expense_overspend_signals_kernel(
         tab_w[1] = load_table(tab_words, 1, "tab_w1")
         wa_raw[1, 0] = load_wa(1, 0)
         nc.sync.dma_start(heads[:], pos1)
-        load_weight_scales(nc.sync, 0, wg_scales)
         tab2_w[0] = load_table(tab2_words, 0, "tab2_w0")
-        load_weight_scales(nc.sync, 4, wc_scales)
-        g_raw = load_g()
         tab2_w[1] = load_table(tab2_words, 1, "tab2_w1")
         for h in range(2):
             v_w[0, h] = gather("v_w0%d" % h, U32, tab_w[0], idx, h * BANK, (h + 1) * BANK)
@@ -329,6 +344,9 @@ def tile_list_expense_overspend_signals_kernel(
         for h in range(2):
             v_w[1, h] = gather("v_w1%d" % h, U32, tab_w[1], idx, h * BANK, (h + 1) * BANK)
         nc.sync.dma_start(v2_s_up[:100, :].bitcast(I32), v2_s[4:104, :].bitcast(I32))
+        load_weight_scales(nc.sync, 0, wg_scales)
+        g_raw = load_g()
+        load_weight_scales(nc.sync, 4, wc_scales)
         c_raw[0] = load_c(0)
         c_raw[1] = load_c(1)
         wa_raw[0, 1] = load_wa(0, 1)
@@ -350,112 +368,96 @@ def tile_list_expense_overspend_signals_kernel(
             a_pass(accs[3][h], wa_q[1, 0], 1, 3, h)
         rows[0, 3] = a_row(0, 3, accs[3])
         v2_w[0] = gather("v2_w0", U32, tab2_w[0], idx2, 0, M)
-        gc_s = deal_scales(nc.vector)
-        g_w[0] = deal_g(0, nc.vector)
-        g_w[1] = deal_g(1, nc.vector)
         v2_w[1] = gather("v2_w1", U32, tab2_w[1], idx2, 0, M)
-        a_picked[0, 0] = kept("a_picked00", [P, 4, HALF], F32)[:]
-        pick(a_picked[0, 0][:, 0, :], rows[0, 0], 0 * HALF, 1 * HALF)
-        pick(a_picked[0, 0][:, 1, :], rows[0, 1], 0 * HALF, 1 * HALF)
-        pick(a_picked[0, 0][:, 2, :], rows[0, 2], 0 * HALF, 1 * HALF)
-        pick(a_picked[0, 0][:, 3, :], rows[0, 3], 0 * HALF, 1 * HALF)
-        c_w[0, 0] = deal_c(0, 0, nc.vector)
-        c_w[0, 1] = deal_c(0, 1, nc.vector)
-        a_picked[0, 1] = kept("a_picked01", [P, 4, HALF], F32)[:]
-        pick(a_picked[0, 1][:, 0, :], rows[0, 0], 1 * HALF, 2 * HALF)
-        pick(a_picked[0, 1][:, 1, :], rows[0, 1], 1 * HALF, 2 * HALF)
-        pick(a_picked[0, 1][:, 2, :], rows[0, 2], 1 * HALF, 2 * HALF)
-        pick(a_picked[0, 1][:, 3, :], rows[0, 3], 1 * HALF, 2 * HALF)
-        c_w[1, 0] = deal_c(1, 0, nc.vector)
-        c_w[1, 1] = deal_c(1, 1, nc.vector)
+        a_picked[0] = kept("a_picked0", [P, 4, M], F32)
+        pick(a_picked[0][:, 0, :], rows[0, 0], 0, M)
+        pick(a_picked[0][:, 1, :], rows[0, 1], 0, M)
+        pick(a_picked[0][:, 2, :], rows[0, 2], 0, M)
+        pick(a_picked[0][:, 3, :], rows[0, 3], 0, M)
         gates[0, 0] = gate_tile(0, 0)
         gates[0, 1] = gate_tile(0, 1)
         gates[0, 2] = gate_tile(0, 2)
         gates[0, 3] = gate_tile(0, 3)
-        gates[1, 0] = gate_tile(1, 0)
-        gates[1, 1] = gate_tile(1, 1)
-        gates[1, 2] = gate_tile(1, 2)
-        gates[1, 3] = gate_tile(1, 3)
         c_acc[0, 0] = c_tile(0, 0)
         c_acc[0, 1] = c_tile(0, 1)
         c_acc[0, 2] = c_tile(0, 2)
         c_acc[0, 3] = c_tile(0, 3)
-        sc[0] = kept("sc0", [P, 4, M], F32)
-        nc.vector.tensor_tensor(sc[0][:, 0, :], c_acc[0, 0][:], gates[0, 0][:], MULT)
-        nc.vector.tensor_tensor(sc[0][:, 1, :], c_acc[0, 1][:], gates[0, 1][:], MULT)
-        nc.vector.tensor_tensor(sc[0][:, 2, :], c_acc[0, 2][:], gates[0, 2][:], MULT)
-        nc.vector.tensor_tensor(sc[0][:, 3, :], c_acc[0, 3][:], gates[0, 3][:], MULT)
+        sc[0, 0] = product(0, 0, gates[0, 0], c_acc[0, 0])
+        sc[0, 1] = product(0, 1, gates[0, 1], c_acc[0, 1])
+        sc[0, 2] = product(0, 2, gates[0, 2], c_acc[0, 2])
+        sc[0, 3] = product(0, 3, gates[0, 3], c_acc[0, 3])
+        turned[0, 0] = turn(0, 0)
+        turned[0, 1] = turn(0, 1)
+        turned[0, 2] = turn(0, 2)
+        turned[0, 3] = turn(0, 3)
         bf[0, 1] = round_wa(wa_raw[0, 1], "bf01", "ssss")
-        bf[1, 1] = round_wa(wa_raw[1, 1], "bf11", "ssss")
+        bf[1, 1] = round_wa(wa_raw[1, 1], "bf11", "ssvv")
+        z_bf[0, 0] = subtract(0, 0)
+        z_bf[0, 1] = subtract(0, 1)
         wa_q[0, 1] = quantise("wa01", bf[0, 1])
-        subtract(0)
         wa_q[1, 1] = quantise("wa11", bf[1, 1])
+        z_bf[0, 2] = subtract(0, 2)
+        z_bf[0, 3] = subtract(0, 3)
+        gates[1, 0] = gate_tile(1, 0)
+        gates[1, 1] = gate_tile(1, 1)
+        gates[1, 2] = gate_tile(1, 2)
+        gates[1, 3] = gate_tile(1, 3)
         wo_bf[0] = round_wo(wo_raw[0], "wo_bf0", "ssss")
-        subtract(1)
         c_acc[1, 0] = c_tile(1, 0)
         c_acc[1, 1] = c_tile(1, 1)
         rows[1, 0] = a_tile(1, 0)
-        sc1[0] = product(1, 0, gates[1, 0], c_acc[1, 0])
-        sc1[1] = product(1, 1, gates[1, 1], c_acc[1, 1])
+        sc[1, 0] = product(1, 0, gates[1, 0], c_acc[1, 0])
+        sc[1, 1] = product(1, 1, gates[1, 1], c_acc[1, 1])
         c_acc[1, 2] = c_tile(1, 2)
         c_acc[1, 3] = c_tile(1, 3)
-        sc1[2] = product(1, 2, gates[1, 2], c_acc[1, 2])
-        sc1[3] = product(1, 3, gates[1, 3], c_acc[1, 3])
-        z0[0] = quantise("z00", z0_bf[0])
-        z0[1] = quantise("z01", z0_bf[1])
+        sc[1, 2] = product(1, 2, gates[1, 2], c_acc[1, 2])
+        sc[1, 3] = product(1, 3, gates[1, 3], c_acc[1, 3])
+        z_q[0, 0] = quantise("z00", z_bf[0, 0])
+        z_q[0, 1] = quantise("z01", z_bf[0, 1])
+        z_q[0, 2] = quantise("z02", z_bf[0, 2])
+        z_q[0, 3] = quantise("z03", z_bf[0, 3])
         wo_q[0] = quantise("wo0", wo_bf[0])
         rows[1, 1] = a_tile(1, 1)
+        a_picked[1] = kept("a_picked1", [P, 4, M], F32)
+        pick(a_picked[1][:, 0, :], rows[1, 0], 0, M)
         rows[1, 2] = a_tile(1, 2)
+        pick(a_picked[1][:, 1, :], rows[1, 1], 0, M)
         rows[1, 3] = a_tile(1, 3)
-        wo_bf[1] = round_wo(wo_raw[1], "wo_bf1", "ssvv")
-        y_acc = [bank("y%d" % piece, [P, 4, PIECE]) for piece in range(pieces)]
-        for piece in range(pieces):
-            y_first(y_acc[piece], piece)
-
-        y_w = kept("y_w", [P, M], U32)
-        y_s = kept("y_s", [P, M], U8)
-        state = {}
-
-        def z_piece(n):
-            lo, hi = n * PIECE, (n + 1) * PIECE
-            minus_z = by_vector("minus_z1%d" % n, [P, 4, PIECE], F32)
-            for t in range(4):
-                pick_minus(minus_z[:, t, :], rows[1, t], sc1[t], lo, hi)
-            state[n] = minus_z
-
-        def z_round(n):
-            state[n] = round_z("z1_bf%d" % n, state[n], "ssss"[n])
-
-        def y_product(n):
-            if n == 0:
-                wo_q[1] = quantise("wo1", wo_bf[1])
-            z_q = quantise("z1%d" % n, state[n])
-            acc = y_acc[n]
-            y_pass(acc, 1, z_q, 0, PIECE)
-            y = by_scalar("y%d" % n, [P, 4, PIECE], F32)
-            if n in ():
-                y_bf = by_scalar("y_bf%d" % n, [P, PACK * PIECE], BF16)
-                nc.scalar.copy(woven(y_bf[:]), in_fours(acc[:]))
-            nc.scalar.copy(y[:], acc[:])
-            nc.sync.dma_start(y_rows[:, :, n * PIECE : (n + 1) * PIECE], y[:])
-            state[n] = y_bf if n in () else y
-
-        def y_round(n):
-            if n not in ():
-                y_bf = by_vector("y_bf%d" % n, [P, PACK * PIECE], BF16)
-                nc.vector.tensor_copy(woven(y_bf[:]), in_fours(state[n][:]))
-                state[n] = y_bf
-
-        def y_planes(n):
-            lo, hi = n * PIECE, (n + 1) * PIECE
-            nc.vector.quantize_mx(out=y_w[:, lo:hi].bitcast(FP8X4), scales=y_s[:, lo:hi], in_=state[n][:])
-            if n % 2 == 1:
-                nc.sync.dma_start(y_words[:, hi - 2 * PIECE : hi], y_w[:, hi - 2 * PIECE : hi].bitcast(I32))
-
-        stages = ((z_piece, 0), (z_round, 0), (y_round, 3), (y_product, 1), (y_planes, 3))
-        for step in range(pieces + 4):
-            for stage, lag in stages:
-                if 0 <= step - lag < pieces:
-                    stage(step - lag)
+        pick(a_picked[1][:, 2, :], rows[1, 2], 0, M)
+        pick(a_picked[1][:, 3, :], rows[1, 3], 0, M)
+        wo_bf[1] = round_wo(wo_raw[1], "wo_bf1", "ssss")
+        turned[1, 0] = turn(1, 0)
+        turned[1, 1] = turn(1, 1)
+        turned[1, 2] = turn(1, 2)
+        turned[1, 3] = turn(1, 3)
+        z_bf[1, 0] = subtract(1, 0)
+        y_half(0, 0)
+        z_bf[1, 1] = subtract(1, 1)
+        wo_q[1] = quantise("wo1", wo_bf[1])
+        z_q[1, 0] = quantise("z10", z_bf[1, 0])
+        y_half(1, 0)
+        y_out(0)
+        y_half(0, 1)
+        z_bf[1, 2] = subtract(1, 2)
+        z_q[1, 1] = quantise("z11", z_bf[1, 1])
+        y_half(1, 1)
+        y_out(1)
+        y_half(0, 2)
+        z_bf[1, 3] = subtract(1, 3)
+        z_q[1, 2] = quantise("z12", z_bf[1, 2])
+        y_half(1, 2)
+        y_round(0, "v")
+        y_out(2)
+        y_half(0, 3)
+        z_q[1, 3] = quantise("z13", z_bf[1, 3])
+        y_half(1, 3)
+        y_planes(0)
+        y_round(1, "v")
+        y_out(3)
+        y_planes(1)
+        y_round(2, "v")
+        y_planes(2)
+        y_round(3, "v")
+        y_planes(3)
         for q in range(4):
             (nc.scalar, nc.sync)[q % 2].dma_start(out_2[0, 4 * q : 4 * q + 4, :].bitcast(I32), y_s[32 * q : 32 * q + 4, :].bitcast(I32))

@@ -28,7 +28,7 @@ RUN = 1
 V_BUFS = 28
 S_BUFS = 12
 L_BUFS = 7
-SHARE = {"tab2_w1":"h0","a_picked0":"h0"}
+SHARE = {"tab2_w1":"h0","a_picked1":"h0"}
 
 
 def tile_list_expense_overspend_signals_kernel(
@@ -76,12 +76,9 @@ def tile_list_expense_overspend_signals_kernel(
                 queue.dma_start(tile[32 * q : 32 * q + 8, :].bitcast(I32), scales[:, 4 * q : 4 * q + 4, :].bitcast(I32))
 
         def load_weight_scales(queue, first, scales):
-            for q in range(4):
-                rows = gc_s_raw[32 * q + first : 32 * q + first + 4, :].bitcast(I32)
-                queue.dma_start(
-                    rows.rearrange("r (a e) -> r a e", a=2),
-                    scales[:, 4 * q : 4 * q + 4, :].bitcast(I32).rearrange("a r e -> r a e"),
-                )
+            rows = scales.bitcast(I32).rearrange("a (q r) e -> r q a e", r=4)
+            for r in range(4):
+                queue.dma_start(gc_s_raw[first + r : P : 32, :].bitcast(I32).rearrange("q (a e) -> q a e", a=2), rows[r])
 
         def load_table(words, a, name):
             tile = loaded(name, [P, T], U32)
@@ -323,18 +320,20 @@ def tile_list_expense_overspend_signals_kernel(
         nc.sync.dma_start(idx[:], offs)
         tab_w[0] = load_table(tab_words, 0, "tab_w0")
         load_table_scales(nc.sync, tab_s, tab_scales)
-        nc.sync.dma_start(idx2[:], offs2)
         wa_raw[0, 0] = load_wa(0, 0)
-        load_table_scales(nc.sync, tab2_s, tab2_scales)
         tab_w[1] = load_table(tab_words, 1, "tab_w1")
         wa_raw[1, 0] = load_wa(1, 0)
+        nc.sync.dma_start(idx2[:], offs2)
         nc.sync.dma_start(heads[:], pos1)
+        wa_raw[0, 1] = load_wa(0, 1)
+        load_table_scales(nc.sync, tab2_s, tab2_scales)
+        wa_raw[1, 1] = load_wa(1, 1)
         tab2_w[0] = load_table(tab2_words, 0, "tab2_w0")
+        load_weight_scales(nc.sync, 0, wg_scales)
         tab2_w[1] = load_table(tab2_words, 1, "tab2_w1")
         for h in range(2):
             v_w[0, h] = gather("v_w0%d" % h, U32, tab_w[0], idx, h * BANK, (h + 1) * BANK)
         v_s = gather("v_s", U8, tab_s, idx, 0, S)
-        v2_s = gather("v2_s", U8, tab2_s, idx2, 0, M)
         bf[0, 0] = round_wa(wa_raw[0, 0], "bf00", "ssss")
         wa_q[0, 0] = quantise("wa00", bf[0, 0])
         accs = [[bank("a0%d" % t, [P, BANK]) for h in range(2)] for t in range(4)]
@@ -343,18 +342,9 @@ def tile_list_expense_overspend_signals_kernel(
                 a_pass(accs[t][h], wa_q[0, 0], 0, t, h)
         for h in range(2):
             v_w[1, h] = gather("v_w1%d" % h, U32, tab_w[1], idx, h * BANK, (h + 1) * BANK)
-        nc.sync.dma_start(v2_s_up[:100, :].bitcast(I32), v2_s[4:104, :].bitcast(I32))
-        load_weight_scales(nc.sync, 0, wg_scales)
-        g_raw = load_g()
-        load_weight_scales(nc.sync, 4, wc_scales)
-        c_raw[0] = load_c(0)
-        c_raw[1] = load_c(1)
-        wa_raw[0, 1] = load_wa(0, 1)
-        wa_raw[1, 1] = load_wa(1, 1)
-        wo_raw[0] = load_wo(0)
-        wo_raw[1] = load_wo(1)
         bf[1, 0] = round_wa(wa_raw[1, 0], "bf10", "ssvv")
         wa_q[1, 0] = quantise("wa10", bf[1, 0])
+        bf[0, 1] = round_wa(wa_raw[0, 1], "bf01", "vvvv")
         for h in range(2):
             a_pass(accs[0][h], wa_q[1, 0], 1, 0, h)
         rows[0, 0] = a_row(0, 0, accs[0])
@@ -367,95 +357,102 @@ def tile_list_expense_overspend_signals_kernel(
         for h in range(2):
             a_pass(accs[3][h], wa_q[1, 0], 1, 3, h)
         rows[0, 3] = a_row(0, 3, accs[3])
-        v2_w[0] = gather("v2_w0", U32, tab2_w[0], idx2, 0, M)
-        v2_w[1] = gather("v2_w1", U32, tab2_w[1], idx2, 0, M)
+        bf[1, 1] = round_wa(wa_raw[1, 1], "bf11", "ssss")
         a_picked[0] = kept("a_picked0", [P, 4, M], F32)
         pick(a_picked[0][:, 0, :], rows[0, 0], 0, M)
+        wa_q[0, 1] = quantise("wa01", bf[0, 1])
+        v2_s = gather("v2_s", U8, tab2_s, idx2, 0, M)
+        nc.sync.dma_start(v2_s_up[:100, :].bitcast(I32), v2_s[4:104, :].bitcast(I32))
+        load_weight_scales(nc.sync, 4, wc_scales)
+        g_raw = load_g()
+        c_raw[0] = load_c(0)
+        c_raw[1] = load_c(1)
+        wo_raw[0] = load_wo(0)
+        wo_raw[1] = load_wo(1)
         pick(a_picked[0][:, 1, :], rows[0, 1], 0, M)
         pick(a_picked[0][:, 2, :], rows[0, 2], 0, M)
-        pick(a_picked[0][:, 3, :], rows[0, 3], 0, M)
-        gates[0, 0] = gate_tile(0, 0)
-        gates[0, 1] = gate_tile(0, 1)
-        gates[0, 2] = gate_tile(0, 2)
-        gates[0, 3] = gate_tile(0, 3)
-        c_acc[0, 0] = c_tile(0, 0)
-        c_acc[0, 1] = c_tile(0, 1)
-        c_acc[0, 2] = c_tile(0, 2)
-        c_acc[0, 3] = c_tile(0, 3)
-        sc[0, 0] = product(0, 0, gates[0, 0], c_acc[0, 0])
-        sc[0, 1] = product(0, 1, gates[0, 1], c_acc[0, 1])
-        sc[0, 2] = product(0, 2, gates[0, 2], c_acc[0, 2])
-        sc[0, 3] = product(0, 3, gates[0, 3], c_acc[0, 3])
-        turned[0, 0] = turn(0, 0)
-        turned[0, 1] = turn(0, 1)
-        turned[0, 2] = turn(0, 2)
-        turned[0, 3] = turn(0, 3)
-        bf[0, 1] = round_wa(wa_raw[0, 1], "bf01", "ssss")
-        bf[1, 1] = round_wa(wa_raw[1, 1], "bf11", "ssvv")
-        z_bf[0, 0] = subtract(0, 0)
-        z_bf[0, 1] = subtract(0, 1)
-        wa_q[0, 1] = quantise("wa01", bf[0, 1])
         wa_q[1, 1] = quantise("wa11", bf[1, 1])
-        z_bf[0, 2] = subtract(0, 2)
-        z_bf[0, 3] = subtract(0, 3)
-        gates[1, 0] = gate_tile(1, 0)
-        gates[1, 1] = gate_tile(1, 1)
-        gates[1, 2] = gate_tile(1, 2)
-        gates[1, 3] = gate_tile(1, 3)
-        wo_bf[0] = round_wo(wo_raw[0], "wo_bf0", "ssss")
-        c_acc[1, 0] = c_tile(1, 0)
-        c_acc[1, 1] = c_tile(1, 1)
+        pick(a_picked[0][:, 3, :], rows[0, 3], 0, M)
+        v2_w[0] = gather("v2_w0", U32, tab2_w[0], idx2, 0, M)
+        v2_w[1] = gather("v2_w1", U32, tab2_w[1], idx2, 0, M)
         rows[1, 0] = a_tile(1, 0)
-        sc[1, 0] = product(1, 0, gates[1, 0], c_acc[1, 0])
-        sc[1, 1] = product(1, 1, gates[1, 1], c_acc[1, 1])
-        c_acc[1, 2] = c_tile(1, 2)
-        c_acc[1, 3] = c_tile(1, 3)
-        sc[1, 2] = product(1, 2, gates[1, 2], c_acc[1, 2])
-        sc[1, 3] = product(1, 3, gates[1, 3], c_acc[1, 3])
-        z_q[0, 0] = quantise("z00", z_bf[0, 0])
-        z_q[0, 1] = quantise("z01", z_bf[0, 1])
-        z_q[0, 2] = quantise("z02", z_bf[0, 2])
-        z_q[0, 3] = quantise("z03", z_bf[0, 3])
-        wo_q[0] = quantise("wo0", wo_bf[0])
         rows[1, 1] = a_tile(1, 1)
+        rows[1, 2] = a_tile(1, 2)
+        rows[1, 3] = a_tile(1, 3)
         a_picked[1] = kept("a_picked1", [P, 4, M], F32)
         pick(a_picked[1][:, 0, :], rows[1, 0], 0, M)
-        rows[1, 2] = a_tile(1, 2)
         pick(a_picked[1][:, 1, :], rows[1, 1], 0, M)
-        rows[1, 3] = a_tile(1, 3)
         pick(a_picked[1][:, 2, :], rows[1, 2], 0, M)
         pick(a_picked[1][:, 3, :], rows[1, 3], 0, M)
+        gates[0, 0] = gate_tile(0, 0)
+        gates[1, 0] = gate_tile(1, 0)
+        gates[0, 1] = gate_tile(0, 1)
+        gates[1, 1] = gate_tile(1, 1)
+        c_acc[0, 0] = c_tile(0, 0)
+        c_acc[1, 0] = c_tile(1, 0)
+        gates[0, 2] = gate_tile(0, 2)
+        gates[1, 2] = gate_tile(1, 2)
+        c_acc[0, 1] = c_tile(0, 1)
+        c_acc[1, 1] = c_tile(1, 1)
+        sc[0, 0] = product(0, 0, gates[0, 0], c_acc[0, 0])
+        sc[1, 0] = product(1, 0, gates[1, 0], c_acc[1, 0])
+        gates[0, 3] = gate_tile(0, 3)
+        gates[1, 3] = gate_tile(1, 3)
+        wo_bf[0] = round_wo(wo_raw[0], "wo_bf0", "ssss")
         wo_bf[1] = round_wo(wo_raw[1], "wo_bf1", "ssss")
+        sc[0, 1] = product(0, 1, gates[0, 1], c_acc[0, 1])
+        sc[1, 1] = product(1, 1, gates[1, 1], c_acc[1, 1])
+        turned[0, 0] = turn(0, 0)
         turned[1, 0] = turn(1, 0)
-        turned[1, 1] = turn(1, 1)
-        turned[1, 2] = turn(1, 2)
-        turned[1, 3] = turn(1, 3)
+        c_acc[0, 2] = c_tile(0, 2)
+        c_acc[1, 2] = c_tile(1, 2)
+        z_bf[0, 0] = subtract(0, 0)
         z_bf[1, 0] = subtract(1, 0)
-        y_half(0, 0)
-        z_bf[1, 1] = subtract(1, 1)
-        wo_q[1] = quantise("wo1", wo_bf[1])
+        turned[0, 1] = turn(0, 1)
+        turned[1, 1] = turn(1, 1)
+        c_acc[0, 3] = c_tile(0, 3)
+        c_acc[1, 3] = c_tile(1, 3)
+        sc[0, 2] = product(0, 2, gates[0, 2], c_acc[0, 2])
+        sc[1, 2] = product(1, 2, gates[1, 2], c_acc[1, 2])
+        z_q[0, 0] = quantise("z00", z_bf[0, 0])
         z_q[1, 0] = quantise("z10", z_bf[1, 0])
+        z_bf[0, 1] = subtract(0, 1)
+        z_bf[1, 1] = subtract(1, 1)
+        wo_q[0] = quantise("wo0", wo_bf[0])
+        sc[0, 3] = product(0, 3, gates[0, 3], c_acc[0, 3])
+        sc[1, 3] = product(1, 3, gates[1, 3], c_acc[1, 3])
+        turned[0, 2] = turn(0, 2)
+        turned[1, 2] = turn(1, 2)
+        z_q[0, 1] = quantise("z01", z_bf[0, 1])
+        z_q[1, 1] = quantise("z11", z_bf[1, 1])
+        wo_q[1] = quantise("wo1", wo_bf[1])
+        y_half(0, 0)
         y_half(1, 0)
         y_out(0)
+        turned[0, 3] = turn(0, 3)
+        turned[1, 3] = turn(1, 3)
         y_half(0, 1)
-        z_bf[1, 2] = subtract(1, 2)
-        z_q[1, 1] = quantise("z11", z_bf[1, 1])
         y_half(1, 1)
         y_out(1)
-        y_half(0, 2)
-        z_bf[1, 3] = subtract(1, 3)
+        z_bf[0, 2] = subtract(0, 2)
+        z_bf[1, 2] = subtract(1, 2)
+        z_q[0, 2] = quantise("z02", z_bf[0, 2])
         z_q[1, 2] = quantise("z12", z_bf[1, 2])
+        y_half(0, 2)
         y_half(1, 2)
-        y_round(0, "v")
         y_out(2)
-        y_half(0, 3)
+        z_bf[0, 3] = subtract(0, 3)
+        z_bf[1, 3] = subtract(1, 3)
+        z_q[0, 3] = quantise("z03", z_bf[0, 3])
         z_q[1, 3] = quantise("z13", z_bf[1, 3])
+        y_half(0, 3)
         y_half(1, 3)
-        y_planes(0)
-        y_round(1, "v")
         y_out(3)
-        y_planes(1)
+        y_round(0, "v")
+        y_round(1, "v")
+        y_planes(0)
         y_round(2, "v")
+        y_planes(1)
         y_planes(2)
         y_round(3, "v")
         y_planes(3)

@@ -318,22 +318,30 @@ def tile_list_expense_overspend_signals_kernel(
         nc.vector.memset(warm[:, 0:1], 0.0)
         nc.scalar.activation(warm[:, 4:5], warm[:, 0:1], SILU)
         nc.sync.dma_start(idx[:], offs)
-        tab_w[0] = load_table(tab_words, 0, "tab_w0")
+        nc.sync.dma_start(idx2[:], offs2)
         load_table_scales(nc.sync, tab_s, tab_scales)
+        load_table_scales(nc.sync, tab2_s, tab2_scales)
+        tab_w[0] = load_table(tab_words, 0, "tab_w0")
         wa_raw[0, 0] = load_wa(0, 0)
         tab_w[1] = load_table(tab_words, 1, "tab_w1")
         wa_raw[1, 0] = load_wa(1, 0)
-        nc.sync.dma_start(idx2[:], offs2)
         nc.sync.dma_start(heads[:], pos1)
         wa_raw[0, 1] = load_wa(0, 1)
-        load_table_scales(nc.sync, tab2_s, tab2_scales)
         wa_raw[1, 1] = load_wa(1, 1)
         tab2_w[0] = load_table(tab2_words, 0, "tab2_w0")
         load_weight_scales(nc.sync, 0, wg_scales)
         tab2_w[1] = load_table(tab2_words, 1, "tab2_w1")
+        load_weight_scales(nc.sync, 4, wc_scales)
+        g_raw = load_g()
+        c_raw[0] = load_c(0)
+        c_raw[1] = load_c(1)
+        wo_raw[0] = load_wo(0)
+        wo_raw[1] = load_wo(1)
+        v_s = gather("v_s", U8, tab_s, idx, 0, S)
+        v2_s = gather("v2_s", U8, tab2_s, idx2, 0, M)
+        nc.scalar.dma_start(v2_s_up[:100, :].bitcast(I32), v2_s[4:104, :].bitcast(I32))
         for h in range(2):
             v_w[0, h] = gather("v_w0%d" % h, U32, tab_w[0], idx, h * BANK, (h + 1) * BANK)
-        v_s = gather("v_s", U8, tab_s, idx, 0, S)
         bf[0, 0] = round_wa(wa_raw[0, 0], "bf00", "ssss")
         wa_q[0, 0] = quantise("wa00", bf[0, 0])
         accs = [[bank("a0%d" % t, [P, BANK]) for h in range(2)] for t in range(4)]
@@ -361,14 +369,6 @@ def tile_list_expense_overspend_signals_kernel(
         a_picked[0] = kept("a_picked0", [P, 4, M], F32)
         pick(a_picked[0][:, 0, :], rows[0, 0], 0, M)
         wa_q[0, 1] = quantise("wa01", bf[0, 1])
-        v2_s = gather("v2_s", U8, tab2_s, idx2, 0, M)
-        nc.sync.dma_start(v2_s_up[:100, :].bitcast(I32), v2_s[4:104, :].bitcast(I32))
-        load_weight_scales(nc.sync, 4, wc_scales)
-        g_raw = load_g()
-        c_raw[0] = load_c(0)
-        c_raw[1] = load_c(1)
-        wo_raw[0] = load_wo(0)
-        wo_raw[1] = load_wo(1)
         pick(a_picked[0][:, 1, :], rows[0, 1], 0, M)
         pick(a_picked[0][:, 2, :], rows[0, 2], 0, M)
         wa_q[1, 1] = quantise("wa11", bf[1, 1])

@@ -24,7 +24,7 @@ P = 128
 PACK = 4
 PASS = P * PACK
 BANK = 512
-RUN = 1
+RUN = 8
 V_BUFS = 28
 S_BUFS = 12
 L_BUFS = 7
@@ -74,6 +74,14 @@ def tile_list_expense_overspend_signals_kernel(
         def load_table_scales(queue, tile, scales):
             for q in range(4):
                 queue.dma_start(tile[32 * q : 32 * q + 8, :].bitcast(I32), scales[:, 4 * q : 4 * q + 4, :].bitcast(I32))
+
+        def load_rows(queue, tile, scales):
+            queue.dma_start(tile[:32, :].bitcast(I32), scales.rearrange("a j t -> (a j) t").bitcast(I32))
+
+        def place_planes(queue, planes, picked):
+            for a in range(2):
+                for r in range(4):
+                    queue.dma_start(planes[r:P:32, a, :].bitcast(I32), picked[16 * a + r : 16 * a + 16 : 4, :].bitcast(I32))
 
         def load_weight_scales(queue, first, scales):
             rows = scales.bitcast(I32).rearrange("a (q r) e -> r q a e", r=4)
@@ -318,31 +326,31 @@ def tile_list_expense_overspend_signals_kernel(
         nc.vector.memset(warm[:, 0:1], 0.0)
         nc.scalar.activation(warm[:, 4:5], warm[:, 0:1], SILU)
         nc.sync.dma_start(idx[:], offs)
-        nc.sync.dma_start(idx2[:], offs2)
+        tab_w[0] = load_table(tab_words, 0, "tab_w0")
         load_table_scales(nc.sync, tab_s, tab_scales)
         load_table_scales(nc.sync, tab2_s, tab2_scales)
-        tab_w[0] = load_table(tab_words, 0, "tab_w0")
+        nc.sync.dma_start(idx2[:], offs2)
+        nc.sync.dma_start(heads[:], pos1)
         wa_raw[0, 0] = load_wa(0, 0)
         tab_w[1] = load_table(tab_words, 1, "tab_w1")
         wa_raw[1, 0] = load_wa(1, 0)
-        nc.sync.dma_start(heads[:], pos1)
         wa_raw[0, 1] = load_wa(0, 1)
         wa_raw[1, 1] = load_wa(1, 1)
         tab2_w[0] = load_table(tab2_words, 0, "tab2_w0")
-        load_weight_scales(nc.sync, 0, wg_scales)
+        for h in range(2):
+            v_w[0, h] = gather("v_w0%d" % h, U32, tab_w[0], idx, h * BANK, (h + 1) * BANK)
+        v_s = gather("v_s", U8, tab_s, idx, 0, S)
+        v2_s = gather("v2_s", U8, tab2_s, idx2, 0, M)
         tab2_w[1] = load_table(tab2_words, 1, "tab2_w1")
-        load_weight_scales(nc.sync, 4, wc_scales)
+        nc.sync.dma_start(v2_s_up[:100, :].bitcast(I32), v2_s[4:104, :].bitcast(I32))
+        load_weight_scales(nc.sync, 0, wg_scales)
         g_raw = load_g()
+        load_weight_scales(nc.sync, 4, wc_scales)
         c_raw[0] = load_c(0)
         c_raw[1] = load_c(1)
         wo_raw[0] = load_wo(0)
         wo_raw[1] = load_wo(1)
-        v_s = gather("v_s", U8, tab_s, idx, 0, S)
-        v2_s = gather("v2_s", U8, tab2_s, idx2, 0, M)
-        nc.scalar.dma_start(v2_s_up[:100, :].bitcast(I32), v2_s[4:104, :].bitcast(I32))
-        for h in range(2):
-            v_w[0, h] = gather("v_w0%d" % h, U32, tab_w[0], idx, h * BANK, (h + 1) * BANK)
-        bf[0, 0] = round_wa(wa_raw[0, 0], "bf00", "ssss")
+        bf[0, 0] = round_wa(wa_raw[0, 0], "bf00", "ssvv")
         wa_q[0, 0] = quantise("wa00", bf[0, 0])
         accs = [[bank("a0%d" % t, [P, BANK]) for h in range(2)] for t in range(4)]
         for t in range(4):
@@ -359,19 +367,19 @@ def tile_list_expense_overspend_signals_kernel(
         for h in range(2):
             a_pass(accs[1][h], wa_q[1, 0], 1, 1, h)
         rows[0, 1] = a_row(0, 1, accs[1])
+        bf[1, 1] = round_wa(wa_raw[1, 1], "bf11", "ssss")
         for h in range(2):
             a_pass(accs[2][h], wa_q[1, 0], 1, 2, h)
         rows[0, 2] = a_row(0, 2, accs[2])
         for h in range(2):
             a_pass(accs[3][h], wa_q[1, 0], 1, 3, h)
         rows[0, 3] = a_row(0, 3, accs[3])
-        bf[1, 1] = round_wa(wa_raw[1, 1], "bf11", "ssss")
+        wa_q[0, 1] = quantise("wa01", bf[0, 1])
         a_picked[0] = kept("a_picked0", [P, 4, M], F32)
         pick(a_picked[0][:, 0, :], rows[0, 0], 0, M)
-        wa_q[0, 1] = quantise("wa01", bf[0, 1])
         pick(a_picked[0][:, 1, :], rows[0, 1], 0, M)
-        pick(a_picked[0][:, 2, :], rows[0, 2], 0, M)
         wa_q[1, 1] = quantise("wa11", bf[1, 1])
+        pick(a_picked[0][:, 2, :], rows[0, 2], 0, M)
         pick(a_picked[0][:, 3, :], rows[0, 3], 0, M)
         v2_w[0] = gather("v2_w0", U32, tab2_w[0], idx2, 0, M)
         v2_w[1] = gather("v2_w1", U32, tab2_w[1], idx2, 0, M)

@@ -18,17 +18,14 @@ MULT = mybir.AluOpType.mult
 ADD = mybir.AluOpType.add
 SUB = mybir.AluOpType.subtract
 SILU = mybir.ActivationFunctionType.Silu
-COPY = mybir.ActivationFunctionType.Copy
 
 P = 128
 PACK = 4
 PASS = P * PACK
 BANK = 512
 RUN = 8
-V_BUFS = 28
-S_BUFS = 12
-L_BUFS = 7
-SHARE = {"tab2_w1":"h0","a_picked1":"h0"}
+PIECE = 128
+BUFS = {"v": 28, "s": 12, "g": 4, "loaded": 7, "picked0": 1, "picked1": 1}
 
 
 def tile_list_expense_overspend_signals_kernel(
@@ -41,23 +38,11 @@ def tile_list_expense_overspend_signals_kernel(
         keep = ctx.enter_context(tc.tile_pool(name="keep", bufs=1))
         psum = ctx.enter_context(tc.psum_pool(name="psum", bufs=8))
 
-        def made(name, shape, dtype, tag, bufs):
-            if name in SHARE:
-                tag = SHARE[name]
-                bufs = {"by_vector": V_BUFS, "by_scalar": S_BUFS}.get(tag, 1)
-            return keep.tile(shape, dtype, name=name, tag=tag, bufs=bufs, align_bytes=64)
-
         def kept(name, shape, dtype):
-            return made(name, shape, dtype, name, 1)
+            return keep.tile(shape, dtype, name=name, tag=name, bufs=1, align_bytes=64)
 
-        def loaded(name, shape, dtype):
-            return made(name, shape, dtype, "loaded", L_BUFS)
-
-        def by_vector(name, shape, dtype):
-            return made(name, shape, dtype, "by_vector", V_BUFS)
-
-        def by_scalar(name, shape, dtype):
-            return made(name, shape, dtype, "by_scalar", S_BUFS)
+        def by(tag, name, shape, dtype):
+            return keep.tile(shape, dtype, name=name, tag=tag, bufs=BUFS[tag], align_bytes=64)
 
         def bank(name, shape):
             return psum.tile(shape, F32, name=name, tag="bank")
@@ -66,192 +51,179 @@ def tile_list_expense_overspend_signals_kernel(
         idx2 = lists.tile([P, M // 16], U16, name="idx2")
         heads = lists.tile([P, M // 16], U16, name="heads")
 
-        def zeroed(name, width):
+        def zeroed(engine, name, width):
             tile = kept(name, [P, width], U8)
-            nc.vector.memset(tile[:].bitcast(I32), 0)
+            engine.memset(tile[:].bitcast(I32), 0)
             return tile
 
         def load_table_scales(queue, tile, scales):
             for q in range(4):
                 queue.dma_start(tile[32 * q : 32 * q + 8, :].bitcast(I32), scales[:, 4 * q : 4 * q + 4, :].bitcast(I32))
 
-        def load_rows(queue, tile, scales):
-            queue.dma_start(tile[:32, :].bitcast(I32), scales.rearrange("a j t -> (a j) t").bitcast(I32))
-
-        def place_planes(queue, planes, picked):
-            for a in range(2):
-                for r in range(4):
-                    queue.dma_start(planes[r:P:32, a, :].bitcast(I32), picked[16 * a + r : 16 * a + 16 : 4, :].bitcast(I32))
-
         def load_weight_scales(queue, first, scales):
             rows = scales.bitcast(I32).rearrange("a (q r) e -> r q a e", r=4)
             for r in range(4):
-                queue.dma_start(gc_s_raw[first + r : P : 32, :].bitcast(I32).rearrange("q (a e) -> q a e", a=2), rows[r])
+                queue.dma_start(gc_s[first + r : P : 32, :].bitcast(I32).rearrange("q (a e) -> q a e", a=2), rows[r])
 
-        def load_table(words, a, name):
-            tile = loaded(name, [P, T], U32)
+        def load_table(words, a, name, tag="loaded"):
+            tile = by(tag, name, [P, T], U32)
             nc.sync.dma_start(tile[:].bitcast(I32), words[a].rearrange("p t i -> p (t i)").bitcast(I32))
             return tile
 
         def load_wa(a, b):
-            raw = loaded("wa%d%d" % (a, b), [P, PACK, PASS], F32)
+            raw = by("loaded", "wa%d%d" % (a, b), [P, PACK, PASS], F32)
             rows = wa[a * PASS : (a + 1) * PASS, b * PASS : (b + 1) * PASS]
             nc.sync.dma_start(raw[:], rows.rearrange("(p i) r -> p i r", i=PACK))
-            return raw
+            wa_raw[a, b] = raw
 
         def load_wo(b):
-            raw = loaded("wo%d" % b, [P, PACK, N], F32)
-            if RUN == 1:
-                nc.sync.dma_start(raw[:], wo[b * PASS : (b + 1) * PASS, :].rearrange("(p t) n -> p t n", t=PACK))
-                return raw
+            raw = by("loaded", "wo%d" % b, [P, PACK, N], F32)
             rows = wo[b * PASS : (b + 1) * PASS, :].rearrange("(g t j) n -> t g j n", t=4, j=RUN)
             for t in range(4):
                 nc.sync.dma_start(raw[:, t, :], rows[t])
-            return raw
+            wo_raw[b] = raw
 
         def load_g():
-            g_raw = kept("g_raw", [P, 2, H // 2], I32)
-            nc.sync.dma_start(g_raw[:], wg_words.bitcast(I32).rearrange("a p e -> p a e"))
-            return g_raw
+            raw = kept("g_raw", [P, 2, H // 2], I32)
+            nc.sync.dma_start(raw[:], wg_words.bitcast(I32).rearrange("a p e -> p a e"))
+            return raw
 
         def load_c(b):
-            c_raw = kept("c_raw%d" % b, [P, 2, PASS], I32)
+            raw = kept("c_raw%d" % b, [P, 2, PASS], I32)
             c_src = wc_words.rearrange("a p e i -> a p (e i)").bitcast(I32)[:, :, b * PASS : (b + 1) * PASS]
-            nc.sync.dma_start(c_raw[:], c_src.rearrange("a p e -> p a e"))
-            return c_raw
+            nc.sync.dma_start(raw[:], c_src.rearrange("a p e -> p a e"))
+            c_raw[b] = raw
 
         def gather(name, dtype, window, offsets, lo, hi):
-            picked = by_vector(name, [P, hi - lo], dtype)
+            picked = by("v", name, [P, hi - lo], dtype)
             nc.vector.tensor_copy(picked[:], window[:].indirect(offsets[:, lo // 16 : hi // 16]))
             return picked
 
         def quantise(name, src):
             width = src.shape[1] // PACK
-            codes = by_vector(name + "_w", [P, width], U32)
+            codes = by("v", name + "_w", [P, width], U32)
             scales = kept(name + "_s", [P, width], U8)
             nc.vector.quantize_mx(out=codes[:].bitcast(FP8X4), scales=scales[:], in_=src[:])
             return codes, scales
 
-        def rounded(name, plan):
-            if plan[0] == "s":
-                return by_scalar(name, [P, PACK * PASS], BF16)
-            return kept(name, [P, PACK * PASS], BF16)
+        def cast(engine, dst, src):
+            if engine == "s":
+                nc.scalar.copy(dst, src)
+            elif engine == "v":
+                nc.vector.tensor_copy(dst, src)
+            else:
+                nc.gpsimd.tensor_scalar(dst, src, 1.0, 0.0, MULT, ADD)
 
-        def shares(plan):
-            return [(e, plan.index(e), plan.index(e) + plan.count(e)) for e in "svg" if e in plan]
+        def round_wa(a, b, lo, hi, engine):
+            bf = by(engine, "wa_bf%d%d%d" % (a, b, lo), [P, (hi - lo) * PASS], BF16)
+            if engine == "g":
+                dst = bf[:].rearrange("p (t g j i) -> p t g j i", t=hi - lo, j=RUN, i=PACK)
+                src = wa_raw[a, b][:].rearrange("p i (g t j) -> p t g j i", t=4, j=RUN)
+            else:
+                dst = bf[:].rearrange("p (t g h j i) -> p t g h i j", t=hi - lo, h=RUN // 4, j=4, i=PACK)
+                src = wa_raw[a, b][:].rearrange("p i (g t h j) -> p t g h i j", t=4, h=RUN // 4, j=4)
+            for t in range(lo, hi):
+                cast(engine, dst[:, t - lo], src[:, t])
+            wa_bf[a, b, lo] = bf, hi
 
-        def round_wa(raw, name, plan):
-            if RUN == 1:
-                return round_wo(raw, name, plan)
-            bf = rounded(name, plan)
-            for e, lo, hi in shares(plan):
-                if e == "g":
-                    dst = bf[:].rearrange("p (t g j i) -> p t g j i", t=4, j=RUN, i=PACK)
-                    src = raw[:].rearrange("p i (g t j) -> p t g j i", t=4, j=RUN)
-                    for t in range(lo, hi):
-                        nc.gpsimd.tensor_scalar(dst[:, t], src[:, t], 1.0, 0.0, MULT, ADD)
-                else:
-                    dst = bf[:].rearrange("p (t g h j i) -> p t g h i j", t=4, h=RUN // 4, j=4, i=PACK)
-                    src = raw[:].rearrange("p i (g t h j) -> p t g h i j", t=4, h=RUN // 4, j=4)
-                    for t in range(lo, hi):
-                        if e == "s":
-                            nc.scalar.copy(dst[:, t], src[:, t])
-                        else:
-                            nc.vector.tensor_copy(dst[:, t], src[:, t])
-            return bf
+        def quantise_wa(a, b, lo):
+            bf, hi = wa_bf[a, b, lo]
+            codes, scales = quantise("wa%d%d%d" % (a, b, lo), bf)
+            for t in range(lo, hi):
+                cols = slice((t - lo) * P, (t - lo + 1) * P)
+                wa_q[a, b, t] = codes[:, cols], scales[:, cols]
 
-        def round_wo(raw, name, plan):
-            bf = rounded(name, plan)
-            for e, lo, hi in shares(plan):
-                if e == "g":
-                    dst = bf[:].rearrange("p (u c t) -> p u c t", u=4, t=4)
-                    src = raw[:].rearrange("p t (c u) -> p u c t", u=4)
-                    for u in range(lo, hi):
-                        nc.gpsimd.tensor_scalar(dst[:, u], src[:, u], 1.0, 0.0, MULT, ADD)
-                else:
-                    dst = bf[:].rearrange("p (u c t) -> p c t u", u=4, t=4)
-                    src = raw[:].rearrange("p t (c u) -> p c t u", u=4)
-                    cols = slice(lo * 32, hi * 32)
-                    if e == "s":
-                        nc.scalar.copy(dst[:, cols], src[:, cols])
-                    else:
-                        nc.vector.tensor_copy(dst[:, cols], src[:, cols])
-            return bf
+        def round_wo(b, lo, hi, engine):
+            bf = by(engine, "wo_bf%d%d" % (b, lo), [P, (hi - lo) * PASS], BF16)
+            if engine == "g":
+                dst = bf[:].rearrange("p (u c t) -> p u c t", u=hi - lo, t=4)
+                src = wo_raw[b][:].rearrange("p t (c u) -> p u c t", u=4)
+                for u in range(lo, hi):
+                    cast(engine, dst[:, u - lo], src[:, u])
+            else:
+                dst = bf[:].rearrange("p (u c t) -> p c t u", u=hi - lo, t=4)
+                src = wo_raw[b][:].rearrange("p t (c u) -> p c t u", u=4)
+                cast(engine, dst, src[:, :, :, lo:hi])
+            wo_bf[b, lo] = bf, hi
 
-        def a_pass(acc, weights, a, t, h):
-            codes, scales = weights
-            cols = slice(t * P, (t + 1) * P)
-            nc.tensor.matmul_mx(
-                out=acc[:], lhsT=codes[:, cols].bitcast(FP8X4), lhsT_scale=scales[:, cols],
-                rhs=v_w[a, h][:].bitcast(FP8X4), rhs_scale=v_s[4 * a :, h * BANK : (h + 1) * BANK],
-                start=(a == 0), stop=(a == 1),
-            )
+        def quantise_wo(b, lo):
+            bf, hi = wo_bf[b, lo]
+            codes, scales = quantise("wo%d%d" % (b, lo), bf)
+            for u in range(lo, hi):
+                cols = slice((u - lo) * P, (u - lo + 1) * P)
+                wo_q[b, u] = codes[:, cols], scales[:, cols]
 
-        def a_row(b, t, accs):
-            row = by_scalar("row%d%d" % (b, t), [P, S], F32)
+        def a_pass(b, t, a):
+            codes, scales = wa_q[a, b, t]
             for h in range(2):
-                nc.scalar.copy(row[:, h * BANK : (h + 1) * BANK], accs[h][:])
-            return row
+                if a == 0:
+                    a_acc[b, t, h] = bank("a%d%d%d" % (b, t, h), [P, BANK])
+                nc.tensor.matmul_mx(
+                    out=a_acc[b, t, h][:], lhsT=codes.bitcast(FP8X4), lhsT_scale=scales,
+                    rhs=v_w[a, h][:].bitcast(FP8X4), rhs_scale=v_s[4 * a :, h * BANK : (h + 1) * BANK],
+                    start=(a == 0), stop=(a == 1),
+                )
+
+        def a_row(b, t):
+            row = by("s", "row%d%d" % (b, t), [P, S], F32)
+            for h in range(2):
+                nc.scalar.copy(row[:, h * BANK : (h + 1) * BANK], a_acc[b, t, h][:])
+            rows[b, t] = row
 
         def a_tile(b, t):
-            accs = [bank("a%d%d" % (b, t), [P, BANK]) for h in range(2)]
-            for h in range(2):
-                for a in range(2):
-                    a_pass(accs[h], wa_q[a, b], a, t, h)
-            return a_row(b, t, accs)
+            a_pass(b, t, 0)
+            a_pass(b, t, 1)
+            a_row(b, t)
+
+        def pick(b, t):
+            if t == 0:
+                a_picked[b] = by("picked%d" % b, "a_picked%d" % b, [P, 4, M], F32)
+            nc.vector.tensor_copy(a_picked[b][:, t, :], rows[b, t][:].indirect(heads[:]))
 
         def dealt(ap):
             return ap.rearrange("p (g t j) -> p t g j", t=4, j=RUN)
 
-        def gate_tile(b, n):
-            g_acc = bank("g%d%d" % (b, n), [P, BANK])
+        def in_tiles(ap):
+            return ap.rearrange("p (t g j) -> p t g j", t=4, j=RUN)
+
+        def gate(b, n):
+            acc = bank("g%d%d" % (b, n), [P, BANK])
             cols = slice(n * P, (n + 1) * P)
             for a in range(2):
                 nc.tensor.matmul_mx(
-                    out=g_acc[:], lhsT=v2_w[a][:, cols].bitcast(FP8X4), lhsT_scale=(v2_s, v2_s_up)[a][:, cols],
+                    out=acc[:], lhsT=v2_w[a][:, cols].bitcast(FP8X4), lhsT_scale=(v2_s, v2_s_up)[a][:, cols],
                     rhs=g_raw[:, a, b * PASS // 2 : (b + 1) * PASS // 2].bitcast(FP4X4),
-                    rhs_scale=gc_s_raw[:, a * H + b * PASS : a * H + (b + 1) * PASS],
+                    rhs_scale=gc_s[:, a * H + b * PASS : a * H + (b + 1) * PASS],
                     start=(a == 0), stop=(a == 1),
                 )
-            gate = by_scalar("gate%d%d" % (b, n), [P, PASS], F32)
-            nc.scalar.activation(gate[:].rearrange("p (t g j) -> p t g j", t=4, j=RUN), dealt(g_acc[:]), SILU)
-            return gate
+            gates[b, n] = by("s", "gate%d%d" % (b, n), [P, PASS], F32)
+            nc.scalar.activation(in_tiles(gates[b, n][:]), dealt(acc[:]), SILU)
 
         def c_tile(b, n):
-            c_acc = bank("c%d%d" % (b, n), [P, BANK])
+            acc = bank("c%d%d" % (b, n), [P, BANK])
             cols = slice(n * P, (n + 1) * P)
             for a in range(2):
                 nc.tensor.matmul_mx(
-                    out=c_acc[:], lhsT=v2_w[a][:, cols].bitcast(FP8X4), lhsT_scale=v2_s[4 * a :, cols],
-                    rhs=c_raw[b][:, a, :].bitcast(FP8X4), rhs_scale=gc_s_raw[4:, a * H + b * PASS : a * H + (b + 1) * PASS],
+                    out=acc[:], lhsT=v2_w[a][:, cols].bitcast(FP8X4), lhsT_scale=v2_s[4 * a :, cols],
+                    rhs=c_raw[b][:, a, :].bitcast(FP8X4), rhs_scale=gc_s[4:, a * H + b * PASS : a * H + (b + 1) * PASS],
                     start=(a == 0), stop=(a == 1),
                 )
-            return c_acc
+            c_acc[b, n] = acc
 
-        def product(b, n, gate, c_acc):
-            sc = by_vector("sc%d%d" % (b, n), [P, PASS], F32)
-            nc.vector.tensor_tensor(
-                sc[:].rearrange("p (t g j) -> p t g j", t=4, j=RUN), dealt(c_acc[:]),
-                gate[:].rearrange("p (t g j) -> p t g j", t=4, j=RUN), MULT,
-            )
-            return sc
+        def product(b, n):
+            sc[b, n] = by("v", "sc%d%d" % (b, n), [P, PASS], F32)
+            nc.vector.tensor_tensor(in_tiles(sc[b, n][:]), dealt(c_acc[b, n][:]), in_tiles(gates[b, n][:]), MULT)
+
+        def product_g(b, n):
+            c_f = by("s", "c_f%d%d" % (b, n), [P, PASS], F32)
+            nc.scalar.copy(in_tiles(c_f[:]), dealt(c_acc[b, n][:]))
+            sc[b, n] = by("g", "sc%d%d" % (b, n), [P, PASS], F32)
+            nc.gpsimd.tensor_tensor(sc[b, n][:], c_f[:], gates[b, n][:], MULT)
 
         def turn(b, n):
-            turned = bank("T%d%d" % (b, n), [P, 4, PIECE])
+            turned[b, n] = bank("T%d%d" % (b, n), [P, 4, PIECE])
             for t in range(4):
-                nc.tensor.transpose(turned[:, t, :], sc[b, n][:, t * P : (t + 1) * P], ident[:])
-            return turned
-
-        def subtract(b, n):
-            bf = by_vector("z%d_bf%d" % (b, n), [P, PACK * PIECE], BF16)
-            nc.vector.tensor_tensor(woven(bf[:]), in_fours(turned[b, n][:]), in_fours(a_picked[b][:, :, n * PIECE : (n + 1) * PIECE]), SUB)
-            return bf
-
-        def pick_minus(dst, row, sc, lo, hi):
-            nc.vector.tensor_tensor(dst, row[:].indirect(heads[:, lo // 16 : hi // 16]), sc[:, lo:hi], SUB)
-
-        def pick(dst, row, lo, hi):
-            nc.vector.tensor_copy(dst, row[:].indirect(heads[:, lo // 16 : hi // 16]))
+                nc.tensor.transpose(turned[b, n][:, t, :], sc[b, n][:, t * P : (t + 1) * P], ident[:])
 
         def in_fours(planes):
             return planes.rearrange("p t (c i) -> p c t i", i=4)
@@ -259,210 +231,179 @@ def tile_list_expense_overspend_signals_kernel(
         def woven(bf):
             return bf.rearrange("p (c i t) -> p c t i", i=4, t=PACK)
 
-        def round_z(name, minus_z, engine):
-            width = minus_z.shape[2]
-            if engine == "s":
-                bf = by_scalar(name, [P, PACK * width], BF16)
-                nc.scalar.activation(woven(bf[:]), in_fours(minus_z[:]), COPY, scale=-1.0)
-            elif engine == "v":
-                bf = by_vector(name, [P, PACK * width], BF16)
-                nc.vector.tensor_scalar(woven(bf[:]), in_fours(minus_z[:]), -1.0, None, MULT)
-            else:
-                bf = kept(name, [P, PACK * width], BF16)
-                nc.gpsimd.tensor_scalar(
-                    bf[:].rearrange("p (c t) -> p c t", t=PACK), minus_z[:].rearrange("p t c -> p c t"), -1.0, 0.0, MULT, ADD
-                )
-            return bf
+        def subtract(b, n):
+            z_bf[b, n] = by("v", "z_bf%d%d" % (b, n), [P, PACK * PIECE], BF16)
+            nc.vector.tensor_tensor(
+                woven(z_bf[b, n][:]), in_fours(turned[b, n][:]), in_fours(a_picked[b][:, :, n * PIECE : (n + 1) * PIECE]), SUB
+            )
 
-        def y_pass(acc, b, z_q, lo, hi):
-            for u in range(4):
-                cols = slice(u * P, (u + 1) * P)
-                nc.tensor.matmul_mx(
-                    out=acc[:, u, :], lhsT=wo_q[b][0][:, cols].bitcast(FP8X4), lhsT_scale=wo_q[b][1][:, cols],
-                    rhs=z_q[0][:, lo:hi].bitcast(FP8X4), rhs_scale=z_q[1][:, lo:hi],
-                    start=(b == 0 and u == 0), stop=(b == 1 and u == 3),
-                )
+        def quantise_z(b, n):
+            z_q[b, n] = quantise("z%d%d" % (b, n), z_bf[b, n])
 
-        v_w, v2_w, wa_raw, wa_q, wo_q, gc_raw, g_w, c_w, tab_w, tab2_w = {}, {}, {}, {}, {}, {}, {}, {}, {}, {}
-        y_rows = out_0.rearrange("(p u) m -> p u m", u=4)
-        y_words = out_1[0].rearrange("p m t -> p (m t)").bitcast(I32)
-        PIECE = 128
-        pieces = M // PIECE
-        bf, wo_bf, wo_raw, c_raw, rows, gates, c_acc, a_picked, sc, z_bf, z_q, turned, y_acc, y_f, y_bf = {}, {}, {}, {}, {}, {}, {}, {}, {}, {}, {}, {}, {}, {}, {}
-        ident = kept("ident", [P, P], F32)
-        make_identity(nc, ident[:])
-        y_w = kept("y_w", [P, M], U32)
-        y_s = kept("y_s", [P, M], U8)
-
-        def y_half(b, n):
-            if b == 0:
+        def y_half(b, n, first):
+            if first:
                 y_acc[n] = bank("y%d" % n, [P, 4, PIECE])
-            y_pass(y_acc[n], b, z_q[b, n], 0, PIECE)
+            for u in range(4):
+                nc.tensor.matmul_mx(
+                    out=y_acc[n][:, u, :], lhsT=wo_q[b, u][0].bitcast(FP8X4), lhsT_scale=wo_q[b, u][1],
+                    rhs=z_q[b, n][0][:].bitcast(FP8X4), rhs_scale=z_q[b, n][1][:],
+                    start=(first and u == 0), stop=(not first and u == 3),
+                )
 
         def y_out(n):
-            y_f[n] = by_scalar("y%d" % n, [P, 4, PIECE], F32)
+            y_f[n] = by("s", "y%d" % n, [P, 4, PIECE], F32)
             nc.scalar.copy(y_f[n][:], y_acc[n][:])
             nc.sync.dma_start(y_rows[:, :, n * PIECE : (n + 1) * PIECE], y_f[n][:])
 
         def y_round(n, engine):
-            if engine == "s":
-                y_bf[n] = by_scalar("y_bf%d" % n, [P, PACK * PIECE], BF16)
-                nc.scalar.copy(woven(y_bf[n][:]), in_fours(y_acc[n][:]))
+            y_bf[n] = by(engine, "y_bf%d" % n, [P, PACK * PIECE], BF16)
+            if engine == "g":
+                cast(engine, y_bf[n][:].rearrange("p (c t) -> p c t", t=PACK), y_f[n][:].rearrange("p t c -> p c t"))
             else:
-                y_bf[n] = by_vector("y_bf%d" % n, [P, PACK * PIECE], BF16)
-                nc.vector.tensor_copy(woven(y_bf[n][:]), in_fours((y_f[n] if engine == "v" else y_acc[n])[:]))
+                cast(engine, woven(y_bf[n][:]), in_fours(y_f[n][:]))
 
         def y_planes(n):
             lo, hi = n * PIECE, (n + 1) * PIECE
             nc.vector.quantize_mx(out=y_w[:, lo:hi].bitcast(FP8X4), scales=y_s[:, lo:hi], in_=y_bf[n][:])
-            if n % 2 == 1:
-                nc.sync.dma_start(y_words[:, hi - 2 * PIECE : hi], y_w[:, hi - 2 * PIECE : hi].bitcast(I32))
 
-        tab_s = zeroed("tab_s", T)
-        tab2_s = zeroed("tab2_s", T)
-        gc_s_raw = zeroed("gc_s_raw", 2 * H)
-        v2_s_up = zeroed("v2_s_up", M)
+        def store_words(lo, hi):
+            nc.sync.dma_start(y_words[:, lo * PIECE : hi * PIECE], y_w[:, lo * PIECE : hi * PIECE].bitcast(I32))
+
+        def store_scales():
+            for q in range(4):
+                (nc.scalar, nc.sync)[q % 2].dma_start(out_2[0, 4 * q : 4 * q + 4, :].bitcast(I32), y_s[32 * q : 32 * q + 4, :].bitcast(I32))
+
+        v_w, v2_w, tab_w, tab2_w, wa_raw, wa_bf, wa_q, wo_raw, wo_bf, wo_q, c_raw = {}, {}, {}, {}, {}, {}, {}, {}, {}, {}, {}
+        a_acc, rows, a_picked, gates, c_acc, sc, turned, z_bf, z_q, y_acc, y_f, y_bf = {}, {}, {}, {}, {}, {}, {}, {}, {}, {}, {}, {}
+        y_rows = out_0.rearrange("(p u) m -> p u m", u=4)
+        y_words = out_1[0].rearrange("p m t -> p (m t)").bitcast(I32)
+        y_w = kept("y_w", [P, M], U32)
+        y_s = kept("y_s", [P, M], U8)
+
+        ident = kept("ident", [P, P], F32)
+        make_identity(nc, ident[:])
+        tab_s = zeroed(nc.vector, "tab_s", T)
+        tab2_s = zeroed(nc.vector, "tab2_s", T)
+        gc_s = zeroed(nc.vector, "gc_s", 2 * H)
+        v2_s_up = zeroed(nc.vector, "v2_s_up", M)
         warm = kept("warm", [P, 8], F32)
         nc.vector.memset(warm[:, 0:1], 0.0)
         nc.scalar.activation(warm[:, 4:5], warm[:, 0:1], SILU)
+
         nc.sync.dma_start(idx[:], offs)
         tab_w[0] = load_table(tab_words, 0, "tab_w0")
         load_table_scales(nc.sync, tab_s, tab_scales)
         load_table_scales(nc.sync, tab2_s, tab2_scales)
         nc.sync.dma_start(idx2[:], offs2)
         nc.sync.dma_start(heads[:], pos1)
-        wa_raw[0, 0] = load_wa(0, 0)
+        load_wa(0, 0)
         tab_w[1] = load_table(tab_words, 1, "tab_w1")
-        wa_raw[1, 0] = load_wa(1, 0)
-        wa_raw[0, 1] = load_wa(0, 1)
-        wa_raw[1, 1] = load_wa(1, 1)
+        load_wa(1, 0)
+        load_wa(0, 1)
+        load_wa(1, 1)
         tab2_w[0] = load_table(tab2_words, 0, "tab2_w0")
         for h in range(2):
             v_w[0, h] = gather("v_w0%d" % h, U32, tab_w[0], idx, h * BANK, (h + 1) * BANK)
         v_s = gather("v_s", U8, tab_s, idx, 0, S)
         v2_s = gather("v2_s", U8, tab2_s, idx2, 0, M)
-        tab2_w[1] = load_table(tab2_words, 1, "tab2_w1")
+        tab2_w[1] = load_table(tab2_words, 1, "tab2_w1", "picked1")
         nc.sync.dma_start(v2_s_up[:100, :].bitcast(I32), v2_s[4:104, :].bitcast(I32))
         load_weight_scales(nc.sync, 0, wg_scales)
         g_raw = load_g()
         load_weight_scales(nc.sync, 4, wc_scales)
-        c_raw[0] = load_c(0)
-        c_raw[1] = load_c(1)
-        wo_raw[0] = load_wo(0)
-        wo_raw[1] = load_wo(1)
-        bf[0, 0] = round_wa(wa_raw[0, 0], "bf00", "ssvv")
-        wa_q[0, 0] = quantise("wa00", bf[0, 0])
-        accs = [[bank("a0%d" % t, [P, BANK]) for h in range(2)] for t in range(4)]
-        for t in range(4):
-            for h in range(2):
-                a_pass(accs[t][h], wa_q[0, 0], 0, t, h)
+        load_c(0)
+        load_c(1)
+        load_wo(0)
+        load_wo(1)
+        def both(f, n):
+            for b in range(2):
+                f(b, n)
+        def y(n):
+            y_half(0, n, True)
+            y_half(1, n, False)
+            y_out(n)
+
+        round_wa(0, 0, 0, 2, "s")
+        round_wa(0, 0, 2, 4, "v")
+        quantise_wa(0, 0, 0)
+        quantise_wa(0, 0, 2)
         for h in range(2):
             v_w[1, h] = gather("v_w1%d" % h, U32, tab_w[1], idx, h * BANK, (h + 1) * BANK)
-        bf[1, 0] = round_wa(wa_raw[1, 0], "bf10", "ssvv")
-        wa_q[1, 0] = quantise("wa10", bf[1, 0])
-        bf[0, 1] = round_wa(wa_raw[0, 1], "bf01", "vvvv")
-        for h in range(2):
-            a_pass(accs[0][h], wa_q[1, 0], 1, 0, h)
-        rows[0, 0] = a_row(0, 0, accs[0])
-        for h in range(2):
-            a_pass(accs[1][h], wa_q[1, 0], 1, 1, h)
-        rows[0, 1] = a_row(0, 1, accs[1])
-        bf[1, 1] = round_wa(wa_raw[1, 1], "bf11", "ssss")
-        for h in range(2):
-            a_pass(accs[2][h], wa_q[1, 0], 1, 2, h)
-        rows[0, 2] = a_row(0, 2, accs[2])
-        for h in range(2):
-            a_pass(accs[3][h], wa_q[1, 0], 1, 3, h)
-        rows[0, 3] = a_row(0, 3, accs[3])
-        wa_q[0, 1] = quantise("wa01", bf[0, 1])
-        a_picked[0] = kept("a_picked0", [P, 4, M], F32)
-        pick(a_picked[0][:, 0, :], rows[0, 0], 0, M)
-        pick(a_picked[0][:, 1, :], rows[0, 1], 0, M)
-        wa_q[1, 1] = quantise("wa11", bf[1, 1])
-        pick(a_picked[0][:, 2, :], rows[0, 2], 0, M)
-        pick(a_picked[0][:, 3, :], rows[0, 3], 0, M)
+        for t in range(4):
+            a_pass(0, t, 0)
+        round_wa(1, 0, 2, 4, "s")
+        round_wa(1, 0, 0, 1, "v")
+        round_wa(1, 0, 1, 2, "v")
+        quantise_wa(1, 0, 0)
+        quantise_wa(1, 0, 1)
+        quantise_wa(1, 0, 2)
+        round_wa(0, 1, 0, 2, "v")
+        round_wa(0, 1, 2, 4, "v")
+        for t in range(2):
+            a_pass(0, t, 1)
+            a_row(0, t)
+        round_wa(1, 1, 0, 2, "s")
+        pick(0, 0)
+        quantise_wa(0, 1, 0)
+        quantise_wa(0, 1, 2)
+        a_pass(0, 2, 1)
+        a_row(0, 2)
+        round_wa(1, 1, 2, 4, "s")
+        a_pass(0, 3, 1)
+        a_row(0, 3)
+        pick(0, 1)
+        quantise_wa(1, 1, 0)
         v2_w[0] = gather("v2_w0", U32, tab2_w[0], idx2, 0, M)
+        quantise_wa(1, 1, 2)
+        pick(0, 2)
         v2_w[1] = gather("v2_w1", U32, tab2_w[1], idx2, 0, M)
-        rows[1, 0] = a_tile(1, 0)
-        rows[1, 1] = a_tile(1, 1)
-        rows[1, 2] = a_tile(1, 2)
-        rows[1, 3] = a_tile(1, 3)
-        a_picked[1] = kept("a_picked1", [P, 4, M], F32)
-        pick(a_picked[1][:, 0, :], rows[1, 0], 0, M)
-        pick(a_picked[1][:, 1, :], rows[1, 1], 0, M)
-        pick(a_picked[1][:, 2, :], rows[1, 2], 0, M)
-        pick(a_picked[1][:, 3, :], rows[1, 3], 0, M)
-        gates[0, 0] = gate_tile(0, 0)
-        gates[1, 0] = gate_tile(1, 0)
-        gates[0, 1] = gate_tile(0, 1)
-        gates[1, 1] = gate_tile(1, 1)
-        c_acc[0, 0] = c_tile(0, 0)
-        c_acc[1, 0] = c_tile(1, 0)
-        gates[0, 2] = gate_tile(0, 2)
-        gates[1, 2] = gate_tile(1, 2)
-        c_acc[0, 1] = c_tile(0, 1)
-        c_acc[1, 1] = c_tile(1, 1)
-        sc[0, 0] = product(0, 0, gates[0, 0], c_acc[0, 0])
-        sc[1, 0] = product(1, 0, gates[1, 0], c_acc[1, 0])
-        gates[0, 3] = gate_tile(0, 3)
-        gates[1, 3] = gate_tile(1, 3)
-        wo_bf[0] = round_wo(wo_raw[0], "wo_bf0", "ssss")
-        wo_bf[1] = round_wo(wo_raw[1], "wo_bf1", "ssss")
-        sc[0, 1] = product(0, 1, gates[0, 1], c_acc[0, 1])
-        sc[1, 1] = product(1, 1, gates[1, 1], c_acc[1, 1])
-        turned[0, 0] = turn(0, 0)
-        turned[1, 0] = turn(1, 0)
-        c_acc[0, 2] = c_tile(0, 2)
-        c_acc[1, 2] = c_tile(1, 2)
-        z_bf[0, 0] = subtract(0, 0)
-        z_bf[1, 0] = subtract(1, 0)
-        turned[0, 1] = turn(0, 1)
-        turned[1, 1] = turn(1, 1)
-        c_acc[0, 3] = c_tile(0, 3)
-        c_acc[1, 3] = c_tile(1, 3)
-        sc[0, 2] = product(0, 2, gates[0, 2], c_acc[0, 2])
-        sc[1, 2] = product(1, 2, gates[1, 2], c_acc[1, 2])
-        z_q[0, 0] = quantise("z00", z_bf[0, 0])
-        z_q[1, 0] = quantise("z10", z_bf[1, 0])
-        z_bf[0, 1] = subtract(0, 1)
-        z_bf[1, 1] = subtract(1, 1)
-        wo_q[0] = quantise("wo0", wo_bf[0])
-        sc[0, 3] = product(0, 3, gates[0, 3], c_acc[0, 3])
-        sc[1, 3] = product(1, 3, gates[1, 3], c_acc[1, 3])
-        turned[0, 2] = turn(0, 2)
-        turned[1, 2] = turn(1, 2)
-        z_q[0, 1] = quantise("z01", z_bf[0, 1])
-        z_q[1, 1] = quantise("z11", z_bf[1, 1])
-        wo_q[1] = quantise("wo1", wo_bf[1])
-        y_half(0, 0)
-        y_half(1, 0)
-        y_out(0)
-        turned[0, 3] = turn(0, 3)
-        turned[1, 3] = turn(1, 3)
-        y_half(0, 1)
-        y_half(1, 1)
-        y_out(1)
-        z_bf[0, 2] = subtract(0, 2)
-        z_bf[1, 2] = subtract(1, 2)
-        z_q[0, 2] = quantise("z02", z_bf[0, 2])
-        z_q[1, 2] = quantise("z12", z_bf[1, 2])
-        y_half(0, 2)
-        y_half(1, 2)
-        y_out(2)
-        z_bf[0, 3] = subtract(0, 3)
-        z_bf[1, 3] = subtract(1, 3)
-        z_q[0, 3] = quantise("z03", z_bf[0, 3])
-        z_q[1, 3] = quantise("z13", z_bf[1, 3])
-        y_half(0, 3)
-        y_half(1, 3)
-        y_out(3)
+        pick(0, 3)
+        for t in range(4):
+            a_tile(1, t)
+        both(gate, 0)
+        both(c_tile, 0)
+        both(gate, 1)
+        pick(1, 0)
+        pick(1, 1)
+        pick(1, 2)
+        both(c_tile, 1)
+        both(product, 0)
+        pick(1, 3)
+        both(gate, 2)
+        both(turn, 0)
+        both(product, 1)
+        round_wo(0, 0, 4, "s")
+        both(c_tile, 2)
+        both(gate, 3)
+        both(turn, 1)
+        both(subtract, 0)
+        both(product, 2)
+        round_wo(1, 0, 4, "s")
+        both(c_tile, 3)
+        both(subtract, 1)
+        both(quantise_z, 0)
+        quantise_wo(0, 0)
+        both(turn, 2)
+        both(product, 3)
+        both(quantise_z, 1)
+        quantise_wo(1, 0)
+        both(subtract, 2)
+        both(turn, 3)
+        y(0)
+        y(1)
+        both(quantise_z, 2)
+        both(subtract, 3)
+        y(2)
         y_round(0, "v")
+        both(quantise_z, 3)
+        y(3)
         y_round(1, "v")
         y_planes(0)
         y_round(2, "v")
         y_planes(1)
+        store_words(0, 2)
         y_planes(2)
         y_round(3, "v")
         y_planes(3)
-        for q in range(4):
-            (nc.scalar, nc.sync)[q % 2].dma_start(out_2[0, 4 * q : 4 * q + 4, :].bitcast(I32), y_s[32 * q : 32 * q + 4, :].bitcast(I32))
+        store_words(2, 4)
+        store_scales()

@@ -25,7 +25,8 @@ PASS = P * PACK
 BANK = 512
 RUN = 8
 PIECE = 128
-BUFS = {"v": 28, "s": 12, "g": 4, "loaded": 7, "picked0": 1, "picked1": 1}
+G_PARTS = 1
+BUFS = {"v": 14, "s": 12, "g": 1, "loaded": 7, "picked0": 1, "picked1": 1}
 
 
 def tile_list_expense_overspend_signals_kernel(
@@ -103,7 +104,7 @@ def tile_list_expense_overspend_signals_kernel(
             width = src.shape[1] // PACK
             codes = by("v", name + "_w", [P, width], U32)
             scales = kept(name + "_s", [P, width], U8)
-            nc.vector.quantize_mx(out=codes[:].bitcast(FP8X4), scales=scales[:], in_=src[:])
+            nc.vector.quantize_mx(out=codes[:].bitcast(FP8X4), scales=scales[:], in_=src)
             return codes, scales
 
         def cast(engine, dst, src):
@@ -128,7 +129,7 @@ def tile_list_expense_overspend_signals_kernel(
 
         def quantise_wa(a, b, lo):
             bf, hi = wa_bf[a, b, lo]
-            codes, scales = quantise("wa%d%d%d" % (a, b, lo), bf)
+            codes, scales = quantise("wa%d%d%d" % (a, b, lo), bf[:])
             for t in range(lo, hi):
                 cols = slice((t - lo) * P, (t - lo + 1) * P)
                 wa_q[a, b, t] = codes[:, cols], scales[:, cols]
@@ -148,7 +149,7 @@ def tile_list_expense_overspend_signals_kernel(
 
         def quantise_wo(b, lo):
             bf, hi = wo_bf[b, lo]
-            codes, scales = quantise("wo%d%d" % (b, lo), bf)
+            codes, scales = quantise("wo%d%d" % (b, lo), bf[:])
             for u in range(lo, hi):
                 cols = slice((u - lo) * P, (u - lo + 1) * P)
                 wo_q[b, u] = codes[:, cols], scales[:, cols]
@@ -218,7 +219,9 @@ def tile_list_expense_overspend_signals_kernel(
             c_f = by("s", "c_f%d%d" % (b, n), [P, PASS], F32)
             nc.scalar.copy(in_tiles(c_f[:]), dealt(c_acc[b, n][:]))
             sc[b, n] = by("g", "sc%d%d" % (b, n), [P, PASS], F32)
-            nc.gpsimd.tensor_tensor(sc[b, n][:], c_f[:], gates[b, n][:], MULT)
+            for h in range(G_PARTS):
+                cols = slice(h * PASS // G_PARTS, (h + 1) * PASS // G_PARTS)
+                nc.gpsimd.tensor_tensor(sc[b, n][:, cols], c_f[:, cols], gates[b, n][:, cols], MULT)
 
         def turn(b, n):
             turned[b, n] = bank("T%d%d" % (b, n), [P, 4, PIECE])
@@ -232,13 +235,38 @@ def tile_list_expense_overspend_signals_kernel(
             return bf.rearrange("p (c i t) -> p c t i", i=4, t=PACK)
 
         def subtract(b, n):
-            z_bf[b, n] = by("v", "z_bf%d%d" % (b, n), [P, PACK * PIECE], BF16)
+            if b == 0:
+                z_bf[n] = by("v", "z_bf%d" % n, [P, 2, PACK * PIECE], BF16)
             nc.vector.tensor_tensor(
-                woven(z_bf[b, n][:]), in_fours(turned[b, n][:]), in_fours(a_picked[b][:, :, n * PIECE : (n + 1) * PIECE]), SUB
+                woven(z_bf[n][:, b, :]), in_fours(turned[b, n][:]), in_fours(a_picked[b][:, :, n * PIECE : (n + 1) * PIECE]), SUB
             )
 
-        def quantise_z(b, n):
-            z_q[b, n] = quantise("z%d%d" % (b, n), z_bf[b, n])
+        def quantise_z(n):
+            codes, scales = quantise("z%d" % n, z_bf[n][:].rearrange("p b c -> p (b c)"))
+            for b in range(2):
+                z_q[b, n] = codes[:, b * PIECE : (b + 1) * PIECE], scales[:, b * PIECE : (b + 1) * PIECE]
+
+        def subtract_half(b, n):
+            if n % 2 == 0:
+                z_bf[b, n // 2] = by("v", "z_bf%d%d" % (b, n), [P, 2, PACK * PIECE], BF16)
+            nc.vector.tensor_tensor(
+                woven(z_bf[b, n // 2][:, n % 2, :]), in_fours(turned[b, n][:]), in_fours(a_picked[b][:, :, n * PIECE : (n + 1) * PIECE]), SUB
+            )
+
+        def quantise_pair(b, pair):
+            codes, scales = quantise("z%d%d" % (b, pair), z_bf[b, pair][:].rearrange("p n c -> p (n c)"))
+            for i in range(2):
+                z_q[b, 2 * pair + i] = codes[:, i * PIECE : (i + 1) * PIECE], scales[:, i * PIECE : (i + 1) * PIECE]
+
+        def subtract_one(b, n):
+            z_bf[b, n, 1] = by("v", "z_bf%d%d" % (b, n), [P, PACK * PIECE], BF16)
+            nc.vector.tensor_tensor(
+                woven(z_bf[b, n, 1][:]), in_fours(turned[b, n][:]), in_fours(a_picked[b][:, :, n * PIECE : (n + 1) * PIECE]), SUB
+            )
+
+        def quantise_one(b, n):
+            codes, scales = quantise("z%d%d" % (b, n), z_bf[b, n, 1][:])
+            z_q[b, n] = codes[:], scales[:]
 
         def y_half(b, n, first):
             if first:
@@ -246,13 +274,15 @@ def tile_list_expense_overspend_signals_kernel(
             for u in range(4):
                 nc.tensor.matmul_mx(
                     out=y_acc[n][:, u, :], lhsT=wo_q[b, u][0].bitcast(FP8X4), lhsT_scale=wo_q[b, u][1],
-                    rhs=z_q[b, n][0][:].bitcast(FP8X4), rhs_scale=z_q[b, n][1][:],
+                    rhs=z_q[b, n][0].bitcast(FP8X4), rhs_scale=z_q[b, n][1],
                     start=(first and u == 0), stop=(not first and u == 3),
                 )
 
         def y_out(n):
             y_f[n] = by("s", "y%d" % n, [P, 4, PIECE], F32)
             nc.scalar.copy(y_f[n][:], y_acc[n][:])
+
+        def y_store(n):
             nc.sync.dma_start(y_rows[:, :, n * PIECE : (n + 1) * PIECE], y_f[n][:])
 
         def y_round(n, engine):
@@ -261,6 +291,28 @@ def tile_list_expense_overspend_signals_kernel(
                 cast(engine, y_bf[n][:].rearrange("p (c t) -> p c t", t=PACK), y_f[n][:].rearrange("p t c -> p c t"))
             else:
                 cast(engine, woven(y_bf[n][:]), in_fours(y_f[n][:]))
+
+        def y_last(n, b):
+            for pair in range(2):
+                if b == 0:
+                    y_acc[n, pair] = bank("y%d%d" % (n, pair), [P, 2, PIECE])
+                for u in range(2):
+                    codes, scales = wo_q[b, 2 * pair + u]
+                    nc.tensor.matmul_mx(
+                        out=y_acc[n, pair][:, u, :], lhsT=codes.bitcast(FP8X4), lhsT_scale=scales,
+                        rhs=z_q[b, n][0].bitcast(FP8X4), rhs_scale=z_q[b, n][1],
+                        start=(b == 0 and u == 0), stop=(b == 1 and u == 1),
+                    )
+
+        def y_last_round(n, pair):
+            if pair == 0:
+                y_bf[n] = by("v", "y_bf%d" % n, [P, PACK * PIECE], BF16)
+            nc.vector.tensor_copy(woven(y_bf[n][:])[:, :, 2 * pair : 2 * pair + 2, :], in_fours(y_acc[n, pair][:]))
+
+        def y_last_out(n, pair):
+            y_f[n, pair] = by("s", "y%d%d" % (n, pair), [P, 2, PIECE], F32)
+            nc.scalar.copy(y_f[n, pair][:], y_acc[n, pair][:])
+            nc.sync.dma_start(y_rows[:, 2 * pair : 2 * pair + 2, n * PIECE : (n + 1) * PIECE], y_f[n, pair][:])
 
         def y_planes(n):
             lo, hi = n * PIECE, (n + 1) * PIECE
@@ -291,14 +343,14 @@ def tile_list_expense_overspend_signals_kernel(
         nc.scalar.activation(warm[:, 4:5], warm[:, 0:1], SILU)
 
         nc.sync.dma_start(idx[:], offs)
+        nc.sync.dma_start(idx2[:], offs2)
         tab_w[0] = load_table(tab_words, 0, "tab_w0")
         load_table_scales(nc.sync, tab_s, tab_scales)
         load_table_scales(nc.sync, tab2_s, tab2_scales)
-        nc.sync.dma_start(idx2[:], offs2)
-        nc.sync.dma_start(heads[:], pos1)
         load_wa(0, 0)
         tab_w[1] = load_table(tab_words, 1, "tab_w1")
         load_wa(1, 0)
+        nc.sync.dma_start(heads[:], pos1)
         load_wa(0, 1)
         load_wa(1, 1)
         tab2_w[0] = load_table(tab2_words, 0, "tab2_w0")
@@ -324,28 +376,27 @@ def tile_list_expense_overspend_signals_kernel(
             y_out(n)
 
         round_wa(0, 0, 0, 2, "s")
-        round_wa(0, 0, 2, 4, "v")
+        round_wa(0, 0, 2, 4, "s")
         quantise_wa(0, 0, 0)
+        v_w[1, 0] = gather("v_w10", U32, tab_w[1], idx, 0, BANK)
         quantise_wa(0, 0, 2)
-        for h in range(2):
-            v_w[1, h] = gather("v_w1%d" % h, U32, tab_w[1], idx, h * BANK, (h + 1) * BANK)
+        v_w[1, 1] = gather("v_w11", U32, tab_w[1], idx, BANK, S)
         for t in range(4):
             a_pass(0, t, 0)
-        round_wa(1, 0, 2, 4, "s")
-        round_wa(1, 0, 0, 1, "v")
-        round_wa(1, 0, 1, 2, "v")
+        round_wa(1, 0, 0, 1, "s")
+        round_wa(1, 0, 1, 2, "s")
+        round_wa(1, 0, 2, 4, "v")
         quantise_wa(1, 0, 0)
         quantise_wa(1, 0, 1)
         quantise_wa(1, 0, 2)
-        round_wa(0, 1, 0, 2, "v")
-        round_wa(0, 1, 2, 4, "v")
+        round_wa(0, 1, 0, 4, "v")
+
         for t in range(2):
             a_pass(0, t, 1)
             a_row(0, t)
         round_wa(1, 1, 0, 2, "s")
         pick(0, 0)
         quantise_wa(0, 1, 0)
-        quantise_wa(0, 1, 2)
         a_pass(0, 2, 1)
         a_row(0, 2)
         round_wa(1, 1, 2, 4, "s")
@@ -360,6 +411,7 @@ def tile_list_expense_overspend_signals_kernel(
         pick(0, 3)
         for t in range(4):
             a_tile(1, t)
+
         both(gate, 0)
         both(c_tile, 0)
         both(gate, 1)
@@ -369,40 +421,46 @@ def tile_list_expense_overspend_signals_kernel(
         both(c_tile, 1)
         both(product, 0)
         pick(1, 3)
+        round_wo(0, 0, 4, "s")
         both(gate, 2)
         both(turn, 0)
         both(product, 1)
-        round_wo(0, 0, 4, "s")
+        round_wo(1, 0, 4, "s")
         both(c_tile, 2)
-        both(gate, 3)
         both(turn, 1)
+        both(gate, 3)
         both(subtract, 0)
         both(product, 2)
-        round_wo(1, 0, 4, "s")
         both(c_tile, 3)
-        both(subtract, 1)
-        both(quantise_z, 0)
         quantise_wo(0, 0)
+        quantise_z(0)
+        both(subtract, 1)
+        quantise_wo(1, 0)
         both(turn, 2)
         both(product, 3)
-        both(quantise_z, 1)
-        quantise_wo(1, 0)
+        quantise_z(1)
+        y(0)
+        y_store(0)
+        y_round(0, "s")
         both(subtract, 2)
         both(turn, 3)
-        y(0)
         y(1)
-        both(quantise_z, 2)
-        both(subtract, 3)
-        y(2)
-        y_round(0, "v")
-        both(quantise_z, 3)
-        y(3)
-        y_round(1, "v")
+        y_store(1)
+        y_round(1, "s")
         y_planes(0)
-        y_round(2, "v")
+        quantise_z(2)
+        subtract_one(0, 3)
+        subtract_one(1, 3)
+        y(2)
+        quantise_one(0, 3)
+        quantise_one(1, 3)
+        y(3)
         y_planes(1)
         store_words(0, 2)
+        y_store(2)
+        y_round(2, "v")
         y_planes(2)
+        y_store(3)
         y_round(3, "v")
         y_planes(3)
         store_words(2, 4)

@@ -343,14 +343,14 @@ def tile_list_expense_overspend_signals_kernel(
         nc.scalar.activation(warm[:, 4:5], warm[:, 0:1], SILU)
 
         nc.sync.dma_start(idx[:], offs)
-        nc.sync.dma_start(idx2[:], offs2)
         tab_w[0] = load_table(tab_words, 0, "tab_w0")
         load_table_scales(nc.sync, tab_s, tab_scales)
         load_table_scales(nc.sync, tab2_s, tab2_scales)
+        nc.sync.dma_start(idx2[:], offs2)
+        nc.sync.dma_start(heads[:], pos1)
         load_wa(0, 0)
         tab_w[1] = load_table(tab_words, 1, "tab_w1")
         load_wa(1, 0)
-        nc.sync.dma_start(heads[:], pos1)
         load_wa(0, 1)
         load_wa(1, 1)
         tab2_w[0] = load_table(tab2_words, 0, "tab2_w0")
@@ -361,8 +361,8 @@ def tile_list_expense_overspend_signals_kernel(
         tab2_w[1] = load_table(tab2_words, 1, "tab2_w1", "picked1")
         nc.sync.dma_start(v2_s_up[:100, :].bitcast(I32), v2_s[4:104, :].bitcast(I32))
         load_weight_scales(nc.sync, 0, wg_scales)
-        g_raw = load_g()
         load_weight_scales(nc.sync, 4, wc_scales)
+        g_raw = load_g()
         load_c(0)
         load_c(1)
         load_wo(0)
@@ -376,18 +376,16 @@ def tile_list_expense_overspend_signals_kernel(
             y_out(n)
 
         round_wa(0, 0, 0, 2, "s")
-        round_wa(0, 0, 2, 4, "s")
+        round_wa(0, 0, 2, 4, "v")
         quantise_wa(0, 0, 0)
-        v_w[1, 0] = gather("v_w10", U32, tab_w[1], idx, 0, BANK)
         quantise_wa(0, 0, 2)
-        v_w[1, 1] = gather("v_w11", U32, tab_w[1], idx, BANK, S)
+        for h in range(2):
+            v_w[1, h] = gather("v_w1%d" % h, U32, tab_w[1], idx, h * BANK, (h + 1) * BANK)
         for t in range(4):
             a_pass(0, t, 0)
-        round_wa(1, 0, 0, 1, "s")
-        round_wa(1, 0, 1, 2, "s")
-        round_wa(1, 0, 2, 4, "v")
+        round_wa(1, 0, 2, 4, "s")
+        round_wa(1, 0, 0, 2, "v")
         quantise_wa(1, 0, 0)
-        quantise_wa(1, 0, 1)
         quantise_wa(1, 0, 2)
         round_wa(0, 1, 0, 4, "v")
 

@@ -23,7 +23,6 @@ P = 128
 PACK = 4
 PASS = P * PACK
 BANK = 512
-RUN = 8
 PIECE = 128
 G_PARTS = 1
 BUFS = {"v": 14, "s": 12, "g": 1, "loaded": 7, "picked0": 1, "picked1": 1}
@@ -79,9 +78,7 @@ def tile_list_expense_overspend_signals_kernel(
 
         def load_wo(b):
             raw = by("loaded", "wo%d" % b, [P, PACK, N], F32)
-            rows = wo[b * PASS : (b + 1) * PASS, :].rearrange("(g t j) n -> t g j n", t=4, j=RUN)
-            for t in range(4):
-                nc.sync.dma_start(raw[:, t, :], rows[t])
+            nc.sync.dma_start(raw[:], wo[b * PASS : (b + 1) * PASS, :].rearrange("(p t) n -> p t n", t=PACK))
             wo_raw[b] = raw
 
         def load_g():
@@ -117,14 +114,10 @@ def tile_list_expense_overspend_signals_kernel(
 
         def round_wa(a, b, lo, hi, engine):
             bf = by(engine, "wa_bf%d%d%d" % (a, b, lo), [P, (hi - lo) * PASS], BF16)
-            if engine == "g":
-                dst = bf[:].rearrange("p (t g j i) -> p t g j i", t=hi - lo, j=RUN, i=PACK)
-                src = wa_raw[a, b][:].rearrange("p i (g t j) -> p t g j i", t=4, j=RUN)
-            else:
-                dst = bf[:].rearrange("p (t g h j i) -> p t g h i j", t=hi - lo, h=RUN // 4, j=4, i=PACK)
-                src = wa_raw[a, b][:].rearrange("p i (g t h j) -> p t g h i j", t=4, h=RUN // 4, j=4)
-            for t in range(lo, hi):
-                cast(engine, dst[:, t - lo], src[:, t])
+            dst = bf[:].rearrange("p (t q i) -> p q i t", t=hi - lo, i=PACK)
+            src = wa_raw[a, b][:].rearrange("p i (q t) -> p q i t", t=4)
+            for t in range(lo, hi, 2):
+                cast(engine, dst[:, :, :, t - lo : t - lo + 2], src[:, :, :, t : t + 2])
             wa_bf[a, b, lo] = bf, hi
 
         def quantise_wa(a, b, lo):
@@ -137,10 +130,11 @@ def tile_list_expense_overspend_signals_kernel(
         def round_wo(b, lo, hi, engine):
             bf = by(engine, "wo_bf%d%d" % (b, lo), [P, (hi - lo) * PASS], BF16)
             if engine == "g":
-                dst = bf[:].rearrange("p (u c t) -> p u c t", u=hi - lo, t=4)
-                src = wo_raw[b][:].rearrange("p t (c u) -> p u c t", u=4)
-                for u in range(lo, hi):
-                    cast(engine, dst[:, u - lo], src[:, u])
+                dst = bf[:].rearrange("p (u c t) -> p c u t", u=hi - lo, t=4)
+                src = wo_raw[b][:].rearrange("p t (c u) -> p c u t", u=4)
+                for part in range(4):
+                    cols = slice(part * 32, (part + 1) * 32)
+                    cast(engine, dst[:, cols], src[:, cols, lo:hi])
             else:
                 dst = bf[:].rearrange("p (u c t) -> p c t u", u=hi - lo, t=4)
                 src = wo_raw[b][:].rearrange("p t (c u) -> p c t u", u=4)
@@ -182,10 +176,10 @@ def tile_list_expense_overspend_signals_kernel(
             nc.vector.tensor_copy(a_picked[b][:, t, :], rows[b, t][:].indirect(heads[:]))
 
         def dealt(ap):
-            return ap.rearrange("p (g t j) -> p t g j", t=4, j=RUN)
+            return ap.rearrange("p (c i t) -> p c t i", t=4, i=4)
 
         def in_tiles(ap):
-            return ap.rearrange("p (t g j) -> p t g j", t=4, j=RUN)
+            return ap.rearrange("p (t c i) -> p c t i", t=4, i=4)
 
         def gate(b, n):
             acc = bank("g%d%d" % (b, n), [P, BANK])
@@ -361,8 +355,8 @@ def tile_list_expense_overspend_signals_kernel(
         tab2_w[1] = load_table(tab2_words, 1, "tab2_w1", "picked1")
         nc.sync.dma_start(v2_s_up[:100, :].bitcast(I32), v2_s[4:104, :].bitcast(I32))
         load_weight_scales(nc.sync, 0, wg_scales)
-        load_weight_scales(nc.sync, 4, wc_scales)
         g_raw = load_g()
+        load_weight_scales(nc.sync, 4, wc_scales)
         load_c(0)
         load_c(1)
         load_wo(0)

@@ -25,7 +25,7 @@ PASS = P * PACK
 BANK = 512
 PIECE = 128
 G_PARTS = 1
-BUFS = {"v": 14, "s": 12, "g": 1, "loaded": 7, "picked0": 1, "picked1": 1}
+BUFS = {"v": 14, "s": 12, "g": 3, "loaded": 7, "picked0": 1, "picked1": 1}
 
 
 def tile_list_expense_overspend_signals_kernel(
@@ -308,6 +308,17 @@ def tile_list_expense_overspend_signals_kernel(
             nc.scalar.copy(y_f[n, pair][:], y_acc[n, pair][:])
             nc.sync.dma_start(y_rows[:, 2 * pair : 2 * pair + 2, n * PIECE : (n + 1) * PIECE], y_f[n, pair][:])
 
+        def y_round_psum(n):
+            y_bf[n] = by("v", "y_bf%d" % n, [P, PACK * PIECE], BF16)
+            nc.vector.tensor_copy(woven(y_bf[n][:]), in_fours(y_acc[n][:]))
+
+        def y_out_half(n, pair):
+            y_f[n, pair] = by("s", "y%d%d" % (n, pair), [P, 2, PIECE], F32)
+            nc.scalar.copy(y_f[n, pair][:], y_acc[n][:, 2 * pair : 2 * pair + 2, :])
+
+        def y_store_half(n, pair):
+            nc.sync.dma_start(y_rows[:, 2 * pair : 2 * pair + 2, n * PIECE : (n + 1) * PIECE], y_f[n, pair][:])
+
         def y_planes(n):
             lo, hi = n * PIECE, (n + 1) * PIECE
             nc.vector.quantize_mx(out=y_w[:, lo:hi].bitcast(FP8X4), scales=y_s[:, lo:hi], in_=y_bf[n][:])
@@ -317,8 +328,9 @@ def tile_list_expense_overspend_signals_kernel(
 
         def store_scales():
             for q in range(4):
-                (nc.scalar, nc.sync)[q % 2].dma_start(out_2[0, 4 * q : 4 * q + 4, :].bitcast(I32), y_s[32 * q : 32 * q + 4, :].bitcast(I32))
+                SCALE_QUEUES[q].dma_start(out_2[0, 4 * q : 4 * q + 4, :].bitcast(I32), y_s[32 * q : 32 * q + 4, :].bitcast(I32))
 
+        SCALE_QUEUES = (nc.scalar, nc.sync, nc.scalar, nc.sync)
         v_w, v2_w, tab_w, tab2_w, wa_raw, wa_bf, wa_q, wo_raw, wo_bf, wo_q, c_raw = {}, {}, {}, {}, {}, {}, {}, {}, {}, {}, {}
         a_acc, rows, a_picked, gates, c_acc, sc, turned, z_bf, z_q, y_acc, y_f, y_bf = {}, {}, {}, {}, {}, {}, {}, {}, {}, {}, {}, {}
         y_rows = out_0.rearrange("(p u) m -> p u m", u=4)
@@ -404,29 +416,30 @@ def tile_list_expense_overspend_signals_kernel(
         for t in range(4):
             a_tile(1, t)
 
-        both(gate, 0)
-        both(c_tile, 0)
+        gate(0, 0)
+        c_tile(0, 0)
+        product_g(0, 0)
+        gate(1, 0)
+        c_tile(1, 0)
+        product_g(1, 0)
         both(gate, 1)
-        pick(1, 0)
-        pick(1, 1)
-        pick(1, 2)
+        for t in range(4):
+            pick(1, t)
         both(c_tile, 1)
-        both(product, 0)
-        pick(1, 3)
-        round_wo(0, 0, 4, "s")
         both(gate, 2)
         both(turn, 0)
+        round_wo(0, 0, 4, "s")
+        round_wo(1, 0, 4, "g")
         both(product, 1)
-        round_wo(1, 0, 4, "s")
         both(c_tile, 2)
         both(turn, 1)
         both(gate, 3)
         both(subtract, 0)
         both(product, 2)
         both(c_tile, 3)
+        both(subtract, 1)
         quantise_wo(0, 0)
         quantise_z(0)
-        both(subtract, 1)
         quantise_wo(1, 0)
         both(turn, 2)
         both(product, 3)

@@ -25,7 +25,7 @@ PASS = P * PACK
 BANK = 512
 PIECE = 128
 G_PARTS = 1
-BUFS = {"v": 14, "s": 12, "g": 3, "loaded": 7, "picked0": 1, "picked1": 1}
+BUFS = {"v": 14, "s": 12, "g": 4, "loaded": 7, "picked0": 1, "picked1": 1}
 
 
 def tile_list_expense_overspend_signals_kernel(
@@ -60,10 +60,10 @@ def tile_list_expense_overspend_signals_kernel(
             for q in range(4):
                 queue.dma_start(tile[32 * q : 32 * q + 8, :].bitcast(I32), scales[:, 4 * q : 4 * q + 4, :].bitcast(I32))
 
-        def load_weight_scales(queue, first, scales):
+        def load_weight_scales(queue, tile, first, scales):
             rows = scales.bitcast(I32).rearrange("a (q r) e -> r q a e", r=4)
             for r in range(4):
-                queue.dma_start(gc_s[first + r : P : 32, :].bitcast(I32).rearrange("q (a e) -> q a e", a=2), rows[r])
+                queue.dma_start(tile[first + r : P : 32, :].bitcast(I32).rearrange("q (a e) -> q a e", a=2), rows[r])
 
         def load_table(words, a, name, tag="loaded"):
             tile = by(tag, name, [P, T], U32)
@@ -81,10 +81,11 @@ def tile_list_expense_overspend_signals_kernel(
             nc.sync.dma_start(raw[:], wo[b * PASS : (b + 1) * PASS, :].rearrange("(p t) n -> p t n", t=PACK))
             wo_raw[b] = raw
 
-        def load_g():
-            raw = kept("g_raw", [P, 2, H // 2], I32)
-            nc.sync.dma_start(raw[:], wg_words.bitcast(I32).rearrange("a p e -> p a e"))
-            return raw
+        def load_g(lo, hi):
+            raw = kept("g_raw%d" % lo, [P, 2, (hi - lo) * PASS // 2], I32)
+            nc.sync.dma_start(raw[:], wg_words.bitcast(I32)[:, :, lo * PASS // 2 : hi * PASS // 2].rearrange("a p e -> p a e"))
+            for b in range(lo, hi):
+                g_raw[b] = raw[:, :, (b - lo) * PASS // 2 : (b - lo + 1) * PASS // 2]
 
         def load_c(b):
             raw = kept("c_raw%d" % b, [P, 2, PASS], I32)
@@ -117,7 +118,10 @@ def tile_list_expense_overspend_signals_kernel(
             dst = bf[:].rearrange("p (t q i) -> p q i t", t=hi - lo, i=PACK)
             src = wa_raw[a, b][:].rearrange("p i (q t) -> p q i t", t=4)
             for t in range(lo, hi, 2):
-                cast(engine, dst[:, :, :, t - lo : t - lo + 2], src[:, :, :, t : t + 2])
+                pair_dst, pair_src = dst[:, :, :, t - lo : t - lo + 2], src[:, :, :, t : t + 2]
+                if engine == "g":
+                    pair_dst, pair_src = pair_dst.rearrange("p q i t -> p q t i"), pair_src.rearrange("p q i t -> p q t i")
+                cast(engine, pair_dst, pair_src)
             wa_bf[a, b, lo] = bf, hi
 
         def quantise_wa(a, b, lo):
@@ -132,8 +136,8 @@ def tile_list_expense_overspend_signals_kernel(
             if engine == "g":
                 dst = bf[:].rearrange("p (u c t) -> p c u t", u=hi - lo, t=4)
                 src = wo_raw[b][:].rearrange("p t (c u) -> p c u t", u=4)
-                for part in range(4):
-                    cols = slice(part * 32, (part + 1) * 32)
+                for part in range(2):
+                    cols = slice(part * 64, (part + 1) * 64)
                     cast(engine, dst[:, cols], src[:, cols, lo:hi])
             else:
                 dst = bf[:].rearrange("p (u c t) -> p c t u", u=hi - lo, t=4)
@@ -187,8 +191,8 @@ def tile_list_expense_overspend_signals_kernel(
             for a in range(2):
                 nc.tensor.matmul_mx(
                     out=acc[:], lhsT=v2_w[a][:, cols].bitcast(FP8X4), lhsT_scale=(v2_s, v2_s_up)[a][:, cols],
-                    rhs=g_raw[:, a, b * PASS // 2 : (b + 1) * PASS // 2].bitcast(FP4X4),
-                    rhs_scale=gc_s[:, a * H + b * PASS : a * H + (b + 1) * PASS],
+                    rhs=g_raw[b][:, a, :].bitcast(FP4X4),
+                    rhs_scale=g_s[:, a * H + b * PASS : a * H + (b + 1) * PASS],
                     start=(a == 0), stop=(a == 1),
                 )
             gates[b, n] = by("s", "gate%d%d" % (b, n), [P, PASS], F32)
@@ -200,7 +204,7 @@ def tile_list_expense_overspend_signals_kernel(
             for a in range(2):
                 nc.tensor.matmul_mx(
                     out=acc[:], lhsT=v2_w[a][:, cols].bitcast(FP8X4), lhsT_scale=v2_s[4 * a :, cols],
-                    rhs=c_raw[b][:, a, :].bitcast(FP8X4), rhs_scale=gc_s[4:, a * H + b * PASS : a * H + (b + 1) * PASS],
+                    rhs=c_raw[b][:, a, :].bitcast(FP8X4), rhs_scale=c_s[4:, a * H + b * PASS : a * H + (b + 1) * PASS],
                     start=(a == 0), stop=(a == 1),
                 )
             c_acc[b, n] = acc
@@ -333,6 +337,7 @@ def tile_list_expense_overspend_signals_kernel(
         SCALE_QUEUES = (nc.scalar, nc.sync, nc.scalar, nc.sync)
         v_w, v2_w, tab_w, tab2_w, wa_raw, wa_bf, wa_q, wo_raw, wo_bf, wo_q, c_raw = {}, {}, {}, {}, {}, {}, {}, {}, {}, {}, {}
         a_acc, rows, a_picked, gates, c_acc, sc, turned, z_bf, z_q, y_acc, y_f, y_bf = {}, {}, {}, {}, {}, {}, {}, {}, {}, {}, {}, {}
+        g_raw = {}
         y_rows = out_0.rearrange("(p u) m -> p u m", u=4)
         y_words = out_1[0].rearrange("p m t -> p (m t)").bitcast(I32)
         y_w = kept("y_w", [P, M], U32)
@@ -342,7 +347,8 @@ def tile_list_expense_overspend_signals_kernel(
         make_identity(nc, ident[:])
         tab_s = zeroed(nc.vector, "tab_s", T)
         tab2_s = zeroed(nc.vector, "tab2_s", T)
-        gc_s = zeroed(nc.vector, "gc_s", 2 * H)
+        g_s = zeroed(nc.vector, "g_s", 2 * H)
+        c_s = zeroed(nc.vector, "c_s", 2 * H)
         v2_s_up = zeroed(nc.vector, "v2_s_up", M)
         warm = kept("warm", [P, 8], F32)
         nc.vector.memset(warm[:, 0:1], 0.0)
@@ -366,9 +372,9 @@ def tile_list_expense_overspend_signals_kernel(
         v2_s = gather("v2_s", U8, tab2_s, idx2, 0, M)
         tab2_w[1] = load_table(tab2_words, 1, "tab2_w1", "picked1")
         nc.sync.dma_start(v2_s_up[:100, :].bitcast(I32), v2_s[4:104, :].bitcast(I32))
-        load_weight_scales(nc.sync, 0, wg_scales)
-        g_raw = load_g()
-        load_weight_scales(nc.sync, 4, wc_scales)
+        load_weight_scales(nc.sync, g_s, 0, wg_scales)
+        load_g(0, 2)
+        load_weight_scales(nc.sync, c_s, 4, wc_scales)
         load_c(0)
         load_c(1)
         load_wo(0)
@@ -395,41 +401,45 @@ def tile_list_expense_overspend_signals_kernel(
         quantise_wa(1, 0, 2)
         round_wa(0, 1, 0, 4, "v")
 
+        quantise_wa(0, 1, 0)
         for t in range(2):
             a_pass(0, t, 1)
             a_row(0, t)
         round_wa(1, 1, 0, 2, "s")
+        round_wa(1, 1, 2, 4, "g")
         pick(0, 0)
-        quantise_wa(0, 1, 0)
-        a_pass(0, 2, 1)
-        a_row(0, 2)
-        round_wa(1, 1, 2, 4, "s")
-        a_pass(0, 3, 1)
-        a_row(0, 3)
         pick(0, 1)
+        for t in range(2, 4):
+            a_pass(0, t, 1)
+            a_row(0, t)
         quantise_wa(1, 1, 0)
-        v2_w[0] = gather("v2_w0", U32, tab2_w[0], idx2, 0, M)
         quantise_wa(1, 1, 2)
-        pick(0, 2)
+        v2_w[0] = gather("v2_w0", U32, tab2_w[0], idx2, 0, M)
         v2_w[1] = gather("v2_w1", U32, tab2_w[1], idx2, 0, M)
+        pick(0, 2)
         pick(0, 3)
-        for t in range(4):
+        a_pass(1, 0, 0)
+        a_pass(1, 1, 0)
+        for t in range(2):
+            a_pass(1, t, 1)
+            a_row(1, t)
+        for t in range(2, 4):
             a_tile(1, t)
 
-        gate(0, 0)
+        both(gate, 0)
         c_tile(0, 0)
         product_g(0, 0)
-        gate(1, 0)
+        gate(0, 1)
         c_tile(1, 0)
         product_g(1, 0)
-        both(gate, 1)
+        gate(1, 1)
         for t in range(4):
             pick(1, t)
         both(c_tile, 1)
         both(gate, 2)
         both(turn, 0)
-        round_wo(0, 0, 4, "s")
-        round_wo(1, 0, 4, "g")
+        round_wo(0, 0, 4, "g")
+        round_wo(1, 0, 4, "s")
         both(product, 1)
         both(c_tile, 2)
         both(turn, 1)
@@ -452,7 +462,6 @@ def tile_list_expense_overspend_signals_kernel(
         y(1)
         y_store(1)
         y_round(1, "s")
-        y_planes(0)
         quantise_z(2)
         subtract_one(0, 3)
         subtract_one(1, 3)
@@ -460,6 +469,7 @@ def tile_list_expense_overspend_signals_kernel(
         quantise_one(0, 3)
         quantise_one(1, 3)
         y(3)
+        y_planes(0)
         y_planes(1)
         store_words(0, 2)
         y_store(2)

@@ -121,7 +121,10 @@ def tile_list_expense_overspend_signals_kernel(
                 pair_dst, pair_src = dst[:, :, :, t - lo : t - lo + 2], src[:, :, :, t : t + 2]
                 if engine == "g":
                     pair_dst, pair_src = pair_dst.rearrange("p q i t -> p q t i"), pair_src.rearrange("p q i t -> p q t i")
-                cast(engine, pair_dst, pair_src)
+                    for part in range(2):
+                        cast(engine, pair_dst[:, part * 64 : (part + 1) * 64], pair_src[:, part * 64 : (part + 1) * 64])
+                else:
+                    cast(engine, pair_dst, pair_src)
             wa_bf[a, b, lo] = bf, hi
 
         def quantise_wa(a, b, lo):
@@ -136,8 +139,8 @@ def tile_list_expense_overspend_signals_kernel(
             if engine == "g":
                 dst = bf[:].rearrange("p (u c t) -> p c u t", u=hi - lo, t=4)
                 src = wo_raw[b][:].rearrange("p t (c u) -> p c u t", u=4)
-                for part in range(2):
-                    cols = slice(part * 64, (part + 1) * 64)
+                for part in range(4):
+                    cols = slice(part * 32, (part + 1) * 32)
                     cast(engine, dst[:, cols], src[:, cols, lo:hi])
             else:
                 dst = bf[:].rearrange("p (u c t) -> p c t u", u=hi - lo, t=4)
@@ -163,10 +166,10 @@ def tile_list_expense_overspend_signals_kernel(
                     start=(a == 0), stop=(a == 1),
                 )
 
-        def a_row(b, t):
+        def a_row(b, t, who="ss"):
             row = by("s", "row%d%d" % (b, t), [P, S], F32)
             for h in range(2):
-                nc.scalar.copy(row[:, h * BANK : (h + 1) * BANK], a_acc[b, t, h][:])
+                cast(who[h], row[:, h * BANK : (h + 1) * BANK], a_acc[b, t, h][:])
             rows[b, t] = row
 
         def a_tile(b, t):
@@ -174,10 +177,10 @@ def tile_list_expense_overspend_signals_kernel(
             a_pass(b, t, 1)
             a_row(b, t)
 
-        def pick(b, t):
-            if t == 0:
+        def pick(b, t, lo=0, hi=M):
+            if b not in a_picked:
                 a_picked[b] = by("picked%d" % b, "a_picked%d" % b, [P, 4, M], F32)
-            nc.vector.tensor_copy(a_picked[b][:, t, :], rows[b, t][:].indirect(heads[:]))
+            nc.vector.tensor_copy(a_picked[b][:, t, lo:hi], rows[b, t][:].indirect(heads[:, lo // 16 : hi // 16]))
 
         def dealt(ap):
             return ap.rearrange("p (c i t) -> p c t i", t=4, i=4)
@@ -185,16 +188,25 @@ def tile_list_expense_overspend_signals_kernel(
         def in_tiles(ap):
             return ap.rearrange("p (t c i) -> p c t i", t=4, i=4)
 
-        def gate(b, n):
-            acc = bank("g%d%d" % (b, n), [P, BANK])
+        def g_pass(b, n, a):
+            if a == 0:
+                g_acc[b, n] = bank("g%d%d" % (b, n), [P, BANK])
             cols = slice(n * P, (n + 1) * P)
-            for a in range(2):
-                nc.tensor.matmul_mx(
-                    out=acc[:], lhsT=v2_w[a][:, cols].bitcast(FP8X4), lhsT_scale=(v2_s, v2_s_up)[a][:, cols],
-                    rhs=g_raw[b][:, a, :].bitcast(FP4X4),
-                    rhs_scale=g_s[:, a * H + b * PASS : a * H + (b + 1) * PASS],
-                    start=(a == 0), stop=(a == 1),
-                )
+            nc.tensor.matmul_mx(
+                out=g_acc[b, n][:], lhsT=v2_w[a][:, cols].bitcast(FP8X4), lhsT_scale=(v2_s, v2_s_up)[a][:, cols],
+                rhs=g_raw[b][:, a, :].bitcast(FP4X4),
+                rhs_scale=g_s[:, a * H + b * PASS : a * H + (b + 1) * PASS],
+                start=(a == 0), stop=(a == 1),
+            )
+
+        def gate(b, n):
+            if (b, n) not in g_acc:
+                g_pass(b, n, 0)
+            g_pass(b, n, 1)
+            silu(b, n)
+
+        def silu(b, n):
+            acc = g_acc[b, n]
             gates[b, n] = by("s", "gate%d%d" % (b, n), [P, PASS], F32)
             nc.scalar.activation(in_tiles(gates[b, n][:]), dealt(acc[:]), SILU)
 
@@ -303,7 +315,7 @@ def tile_list_expense_overspend_signals_kernel(
                     )
 
         def y_last_round(n, pair):
-            if pair == 0:
+            if n not in y_bf:
                 y_bf[n] = by("v", "y_bf%d" % n, [P, PACK * PIECE], BF16)
             nc.vector.tensor_copy(woven(y_bf[n][:])[:, :, 2 * pair : 2 * pair + 2, :], in_fours(y_acc[n, pair][:]))
 
@@ -337,14 +349,13 @@ def tile_list_expense_overspend_signals_kernel(
         SCALE_QUEUES = (nc.scalar, nc.sync, nc.scalar, nc.sync)
         v_w, v2_w, tab_w, tab2_w, wa_raw, wa_bf, wa_q, wo_raw, wo_bf, wo_q, c_raw = {}, {}, {}, {}, {}, {}, {}, {}, {}, {}, {}
         a_acc, rows, a_picked, gates, c_acc, sc, turned, z_bf, z_q, y_acc, y_f, y_bf = {}, {}, {}, {}, {}, {}, {}, {}, {}, {}, {}, {}
-        g_raw = {}
+        g_raw, g_acc = {}, {}
         y_rows = out_0.rearrange("(p u) m -> p u m", u=4)
         y_words = out_1[0].rearrange("p m t -> p (m t)").bitcast(I32)
         y_w = kept("y_w", [P, M], U32)
         y_s = kept("y_s", [P, M], U8)
 
         ident = kept("ident", [P, P], F32)
-        make_identity(nc, ident[:])
         tab_s = zeroed(nc.vector, "tab_s", T)
         tab2_s = zeroed(nc.vector, "tab2_s", T)
         g_s = zeroed(nc.vector, "g_s", 2 * H)
@@ -353,32 +364,7 @@ def tile_list_expense_overspend_signals_kernel(
         warm = kept("warm", [P, 8], F32)
         nc.vector.memset(warm[:, 0:1], 0.0)
         nc.scalar.activation(warm[:, 4:5], warm[:, 0:1], SILU)
-
-        nc.sync.dma_start(idx[:], offs)
-        tab_w[0] = load_table(tab_words, 0, "tab_w0")
-        load_table_scales(nc.sync, tab_s, tab_scales)
-        load_table_scales(nc.sync, tab2_s, tab2_scales)
-        nc.sync.dma_start(idx2[:], offs2)
-        nc.sync.dma_start(heads[:], pos1)
-        load_wa(0, 0)
-        tab_w[1] = load_table(tab_words, 1, "tab_w1")
-        load_wa(1, 0)
-        load_wa(0, 1)
-        load_wa(1, 1)
-        tab2_w[0] = load_table(tab2_words, 0, "tab2_w0")
-        for h in range(2):
-            v_w[0, h] = gather("v_w0%d" % h, U32, tab_w[0], idx, h * BANK, (h + 1) * BANK)
-        v_s = gather("v_s", U8, tab_s, idx, 0, S)
-        v2_s = gather("v2_s", U8, tab2_s, idx2, 0, M)
-        tab2_w[1] = load_table(tab2_words, 1, "tab2_w1", "picked1")
-        nc.sync.dma_start(v2_s_up[:100, :].bitcast(I32), v2_s[4:104, :].bitcast(I32))
-        load_weight_scales(nc.sync, g_s, 0, wg_scales)
-        load_g(0, 2)
-        load_weight_scales(nc.sync, c_s, 4, wc_scales)
-        load_c(0)
-        load_c(1)
-        load_wo(0)
-        load_wo(1)
+        make_identity(nc, ident[:])
         def both(f, n):
             for b in range(2):
                 f(b, n)
@@ -387,8 +373,24 @@ def tile_list_expense_overspend_signals_kernel(
             y_half(1, n, False)
             y_out(n)
 
-        round_wa(0, 0, 0, 2, "s")
-        round_wa(0, 0, 2, 4, "v")
+        nc.sync.dma_start(idx[:], offs)
+        tab_w[0] = load_table(tab_words, 0, "tab_w0")
+        load_table_scales(nc.sync, tab_s, tab_scales)
+        nc.sync.dma_start(idx2[:], offs2)
+        nc.sync.dma_start(heads[:], pos1)
+        load_wa(0, 0)
+        tab_w[1] = load_table(tab_words, 1, "tab_w1")
+        load_wa(1, 0)
+        load_table_scales(nc.sync, tab2_s, tab2_scales)
+        load_wa(0, 1)
+        load_wa(1, 1)
+        tab2_w[0] = load_table(tab2_words, 0, "tab2_w0")
+        tab2_w[1] = load_table(tab2_words, 1, "tab2_w1", "picked1")
+        for h in range(2):
+            v_w[0, h] = gather("v_w0%d" % h, U32, tab_w[0], idx, h * BANK, (h + 1) * BANK)
+        v_s = gather("v_s", U8, tab_s, idx, 0, S)
+        round_wa(0, 0, 0, 2, "v")
+        round_wa(0, 0, 2, 4, "s")
         quantise_wa(0, 0, 0)
         quantise_wa(0, 0, 2)
         for h in range(2):
@@ -399,65 +401,99 @@ def tile_list_expense_overspend_signals_kernel(
         round_wa(1, 0, 0, 2, "v")
         quantise_wa(1, 0, 0)
         quantise_wa(1, 0, 2)
-        round_wa(0, 1, 0, 4, "v")
+        v2_s = gather("v2_s", U8, tab2_s, idx2, 0, M)
+        nc.sync.dma_start(v2_s_up[:100, :].bitcast(I32), v2_s[4:104, :].bitcast(I32))
+        load_weight_scales(nc.sync, g_s, 0, wg_scales)
+        load_g(0, 1)
+        load_weight_scales(nc.sync, c_s, 4, wc_scales)
+        load_c(0)
+        load_g(1, 2)
+        load_c(1)
+        load_wo(0)
+        load_wo(1)
 
-        quantise_wa(0, 1, 0)
-        for t in range(2):
-            a_pass(0, t, 1)
-            a_row(0, t)
-        round_wa(1, 1, 0, 2, "s")
-        round_wa(1, 1, 2, 4, "g")
+        round_wa(0, 1, 0, 2, "g")
+        round_wa(0, 1, 2, 4, "g")
+        a_pass(0, 0, 1)
+        a_row(0, 0)
+        a_pass(0, 1, 1)
+        a_row(0, 1)
+        a_pass(0, 2, 1)
+        a_row(0, 2)
+        a_pass(0, 3, 1)
         pick(0, 0)
         pick(0, 1)
-        for t in range(2, 4):
-            a_pass(0, t, 1)
-            a_row(0, t)
-        quantise_wa(1, 1, 0)
-        quantise_wa(1, 1, 2)
-        v2_w[0] = gather("v2_w0", U32, tab2_w[0], idx2, 0, M)
-        v2_w[1] = gather("v2_w1", U32, tab2_w[1], idx2, 0, M)
+        quantise_wa(0, 1, 0)
         pick(0, 2)
+        round_wa(1, 1, 0, 2, "s")
+        quantise_wa(0, 1, 2)
+        a_row(0, 3)
+        round_wa(1, 1, 2, 4, "s")
+        quantise_wa(1, 1, 0)
+        v2_w[0] = gather("v2_w0", U32, tab2_w[0], idx2, 0, M)
         pick(0, 3)
+        quantise_wa(1, 1, 2)
+        v2_w[1] = gather("v2_w1", U32, tab2_w[1], idx2, 0, M)
         a_pass(1, 0, 0)
         a_pass(1, 1, 0)
-        for t in range(2):
-            a_pass(1, t, 1)
-            a_row(1, t)
-        for t in range(2, 4):
-            a_tile(1, t)
-
-        both(gate, 0)
+        a_pass(1, 2, 0)
+        a_pass(1, 0, 1)
+        a_row(1, 0)
+        a_pass(1, 1, 1)
+        a_row(1, 1)
+        a_pass(1, 3, 0)
+        a_pass(1, 2, 1)
+        a_row(1, 2)
+        a_pass(1, 3, 1)
+        a_row(1, 3)
+        gate(0, 0)
+        gate(0, 1)
+        g_pass(0, 2, 0)
+        g_pass(0, 2, 1)
+        pick(1, 0)
+        pick(1, 1)
+        pick(1, 2)
+        pick(1, 3)
         c_tile(0, 0)
         product_g(0, 0)
-        gate(0, 1)
-        c_tile(1, 0)
-        product_g(1, 0)
+        silu(0, 2)
+        c_tile(0, 1)
+        c_tile(0, 2)
+        product_g(0, 2)
+        product(0, 1)
+        gate(1, 0)
         gate(1, 1)
-        for t in range(4):
-            pick(1, t)
-        both(c_tile, 1)
-        both(gate, 2)
-        both(turn, 0)
+        c_tile(1, 0)
+        c_tile(1, 1)
+        product(1, 0)
+        product(1, 1)
         round_wo(0, 0, 4, "g")
-        round_wo(1, 0, 4, "s")
-        both(product, 1)
-        both(c_tile, 2)
-        both(turn, 1)
+        turn(0, 0)
+        turn(0, 1)
+        gate(1, 2)
+        turn(1, 0)
+        turn(1, 1)
+        c_tile(1, 2)
+        round_wo(1, 0, 2, "s")
+        round_wo(1, 2, 4, "s")
         both(gate, 3)
-        both(subtract, 0)
-        both(product, 2)
+        subtract(0, 0)
+        subtract(0, 1)
+        subtract(1, 0)
+        subtract(1, 1)
+        product(1, 2)
         both(c_tile, 3)
-        both(subtract, 1)
+        both(turn, 2)
         quantise_wo(0, 0)
         quantise_z(0)
-        quantise_wo(1, 0)
-        both(turn, 2)
-        both(product, 3)
         quantise_z(1)
+        quantise_wo(1, 0)
+        quantise_wo(1, 2)
+        both(product, 3)
+        both(subtract, 2)
         y(0)
         y_store(0)
         y_round(0, "s")
-        both(subtract, 2)
         both(turn, 3)
         y(1)
         y_store(1)
@@ -465,18 +501,18 @@ def tile_list_expense_overspend_signals_kernel(
         quantise_z(2)
         subtract_one(0, 3)
         subtract_one(1, 3)
-        y(2)
         quantise_one(0, 3)
+        y(2)
+        y_store(2)
+        y_planes(0)
         quantise_one(1, 3)
         y(3)
-        y_planes(0)
+        y_store(3)
         y_planes(1)
         store_words(0, 2)
-        y_store(2)
         y_round(2, "v")
-        y_planes(2)
-        y_store(3)
         y_round(3, "v")
+        y_planes(2)
         y_planes(3)
         store_words(2, 4)
         store_scales()

@@ -121,10 +121,7 @@ def tile_list_expense_overspend_signals_kernel(
                 pair_dst, pair_src = dst[:, :, :, t - lo : t - lo + 2], src[:, :, :, t : t + 2]
                 if engine == "g":
                     pair_dst, pair_src = pair_dst.rearrange("p q i t -> p q t i"), pair_src.rearrange("p q i t -> p q t i")
-                    for part in range(2):
-                        cast(engine, pair_dst[:, part * 64 : (part + 1) * 64], pair_src[:, part * 64 : (part + 1) * 64])
-                else:
-                    cast(engine, pair_dst, pair_src)
+                cast(engine, pair_dst, pair_src)
             wa_bf[a, b, lo] = bf, hi
 
         def quantise_wa(a, b, lo):
@@ -139,8 +136,8 @@ def tile_list_expense_overspend_signals_kernel(
             if engine == "g":
                 dst = bf[:].rearrange("p (u c t) -> p c u t", u=hi - lo, t=4)
                 src = wo_raw[b][:].rearrange("p t (c u) -> p c u t", u=4)
-                for part in range(4):
-                    cols = slice(part * 32, (part + 1) * 32)
+                for part in range(2):
+                    cols = slice(part * 64, (part + 1) * 64)
                     cast(engine, dst[:, cols], src[:, cols, lo:hi])
             else:
                 dst = bf[:].rearrange("p (u c t) -> p c t u", u=hi - lo, t=4)
@@ -328,6 +325,10 @@ def tile_list_expense_overspend_signals_kernel(
             y_bf[n] = by("v", "y_bf%d" % n, [P, PACK * PIECE], BF16)
             nc.vector.tensor_copy(woven(y_bf[n][:]), in_fours(y_acc[n][:]))
 
+        def y_round_first(n):
+            y_bf[n] = by("s", "y_bf%d" % n, [P, PACK * PIECE], BF16)
+            nc.scalar.copy(woven(y_bf[n][:]), in_fours(y_acc[n][:]))
+
         def y_out_half(n, pair):
             y_f[n, pair] = by("s", "y%d%d" % (n, pair), [P, 2, PIECE], F32)
             nc.scalar.copy(y_f[n, pair][:], y_acc[n][:, 2 * pair : 2 * pair + 2, :])
@@ -412,7 +413,6 @@ def tile_list_expense_overspend_signals_kernel(
         load_wo(0)
         load_wo(1)
 
-        round_wa(0, 1, 0, 2, "g")
         round_wa(0, 1, 2, 4, "g")
         a_pass(0, 0, 1)
         a_row(0, 0)
@@ -423,44 +423,45 @@ def tile_list_expense_overspend_signals_kernel(
         a_pass(0, 3, 1)
         pick(0, 0)
         pick(0, 1)
-        quantise_wa(0, 1, 0)
-        pick(0, 2)
-        round_wa(1, 1, 0, 2, "s")
         quantise_wa(0, 1, 2)
-        a_row(0, 3)
+        round_wa(0, 1, 0, 2, "v")
+        pick(0, 2)
         round_wa(1, 1, 2, 4, "s")
-        quantise_wa(1, 1, 0)
+        quantise_wa(0, 1, 0)
+        a_row(0, 3)
+        round_wa(1, 1, 0, 2, "s")
+        quantise_wa(1, 1, 2)
         v2_w[0] = gather("v2_w0", U32, tab2_w[0], idx2, 0, M)
         pick(0, 3)
-        quantise_wa(1, 1, 2)
+        quantise_wa(1, 1, 0)
         v2_w[1] = gather("v2_w1", U32, tab2_w[1], idx2, 0, M)
-        a_pass(1, 0, 0)
-        a_pass(1, 1, 0)
         a_pass(1, 2, 0)
-        a_pass(1, 0, 1)
-        a_row(1, 0)
-        a_pass(1, 1, 1)
-        a_row(1, 1)
         a_pass(1, 3, 0)
+        a_pass(1, 0, 0)
         a_pass(1, 2, 1)
         a_row(1, 2)
         a_pass(1, 3, 1)
         a_row(1, 3)
+        a_pass(1, 1, 0)
+        a_pass(1, 0, 1)
+        a_row(1, 0)
+        a_pass(1, 1, 1)
+        a_row(1, 1)
         gate(0, 0)
         gate(0, 1)
         g_pass(0, 2, 0)
         g_pass(0, 2, 1)
-        pick(1, 0)
-        pick(1, 1)
         pick(1, 2)
         pick(1, 3)
+        pick(1, 0)
+        pick(1, 1)
         c_tile(0, 0)
         product_g(0, 0)
         silu(0, 2)
         c_tile(0, 1)
         c_tile(0, 2)
-        product_g(0, 2)
         product(0, 1)
+        product(0, 2)
         gate(1, 0)
         gate(1, 1)
         c_tile(1, 0)

@@ -25,7 +25,7 @@ PASS = P * PACK
 BANK = 512
 PIECE = 128
 G_PARTS = 1
-BUFS = {"v": 14, "s": 12, "g": 4, "loaded": 7, "picked0": 1, "picked1": 1}
+BUFS = {"v": 14, "s": 12, "g": 4, "cd": 1, "loaded": 7, "picked0": 1, "picked1": 2}
 
 
 def tile_list_expense_overspend_signals_kernel(
@@ -65,6 +65,15 @@ def tile_list_expense_overspend_signals_kernel(
             for r in range(4):
                 queue.dma_start(tile[first + r : P : 32, :].bitcast(I32).rearrange("q (a e) -> q a e", a=2), rows[r])
 
+        def load_spread_scales(tile, scales):
+            nc.sync.dma_start(tile[0:P:4, :].bitcast(I32), scales.rearrange("a j e -> (a j) e").bitcast(I32))
+
+        def place_scales(plane, picked, width, lo, hi):
+            for move in range(lo, hi):
+                a, r = divmod(move, 4)
+                first = 64 * a + 4 * r
+                nc.sync.dma_start(plane[r:P:32, a * width : (a + 1) * width].bitcast(I32), picked[first : first + 49 : 16, :].bitcast(I32))
+
         def load_table(words, a, name, tag="loaded"):
             tile = by(tag, name, [P, T], U32)
             nc.sync.dma_start(tile[:].bitcast(I32), words[a].rearrange("p t i -> p (t i)").bitcast(I32))
@@ -93,10 +102,14 @@ def tile_list_expense_overspend_signals_kernel(
             nc.sync.dma_start(raw[:], c_src.rearrange("a p e -> p a e"))
             c_raw[b] = raw
 
-        def gather(name, dtype, window, offsets, lo, hi):
-            picked = by("v", name, [P, hi - lo], dtype)
+        def gather(name, dtype, window, offsets, lo, hi, tag="v"):
+            picked = by(tag, name, [P, hi - lo], dtype)
             nc.vector.tensor_copy(picked[:], window[:].indirect(offsets[:, lo // 16 : hi // 16]))
             return picked
+
+        def gather_v2(a, half, tag="v"):
+            lo = half * M // 2
+            v2_w[a, half] = gather("v2_w%d%d" % (a, half), U32, tab2_w[a], idx2, lo, lo + M // 2, tag)
 
         def quantise(name, src):
             width = src.shape[1] // PACK
@@ -113,8 +126,8 @@ def tile_list_expense_overspend_signals_kernel(
             else:
                 nc.gpsimd.tensor_scalar(dst, src, 1.0, 0.0, MULT, ADD)
 
-        def round_wa(a, b, lo, hi, engine):
-            bf = by(engine, "wa_bf%d%d%d" % (a, b, lo), [P, (hi - lo) * PASS], BF16)
+        def round_wa(a, b, lo, hi, engine, tag=None):
+            bf = by(tag or engine, "wa_bf%d%d%d" % (a, b, lo), [P, (hi - lo) * PASS], BF16)
             dst = bf[:].rearrange("p (t q i) -> p q i t", t=hi - lo, i=PACK)
             src = wa_raw[a, b][:].rearrange("p i (q t) -> p q i t", t=4)
             for t in range(lo, hi, 2):
@@ -123,6 +136,19 @@ def tile_list_expense_overspend_signals_kernel(
                     pair_dst, pair_src = pair_dst.rearrange("p q i t -> p q t i"), pair_src.rearrange("p q i t -> p q t i")
                 cast(engine, pair_dst, pair_src)
             wa_bf[a, b, lo] = bf, hi
+
+        def round_wa_shared(a, b, lo, split):
+            bf = by("s", "wa_bf%d%d%d" % (a, b, lo), [P, 2 * PASS], BF16)
+            dst = bf[:].rearrange("p (t q i) -> p q i t", t=2, i=PACK)
+            src = wa_raw[a, b][:].rearrange("p i (q t) -> p q i t", t=4)[:, :, :, lo : lo + 2]
+            cast("s", dst[:, split:], src[:, split:])
+            cast("v", dst[:, :split], src[:, :split])
+            wa_bf[a, b, lo] = bf, lo + 2
+
+        def quantise_wa_tile(a, b, lo, t):
+            bf, hi = wa_bf[a, b, lo]
+            codes, scales = quantise("wa%d%d%d" % (a, b, t), bf[:, (t - lo) * PASS : (t - lo + 1) * PASS])
+            wa_q[a, b, t] = codes[:], scales[:]
 
         def quantise_wa(a, b, lo):
             bf, hi = wa_bf[a, b, lo]
@@ -169,6 +195,11 @@ def tile_list_expense_overspend_signals_kernel(
                 cast(who[h], row[:, h * BANK : (h + 1) * BANK], a_acc[b, t, h][:])
             rows[b, t] = row
 
+        def a_half_row(b, t, h, engine):
+            if (b, t) not in rows:
+                rows[b, t] = by("s", "row%d%d" % (b, t), [P, S], F32)
+            cast(engine, rows[b, t][:, h * BANK : (h + 1) * BANK], a_acc[b, t, h][:])
+
         def a_tile(b, t):
             a_pass(b, t, 0)
             a_pass(b, t, 1)
@@ -185,12 +216,17 @@ def tile_list_expense_overspend_signals_kernel(
         def in_tiles(ap):
             return ap.rearrange("p (t c i) -> p c t i", t=4, i=4)
 
+        def v2_words(a, n):
+            if a in v2_w:
+                return v2_w[a][:, n * P : (n + 1) * P]
+            return v2_w[a, n // 2][:, n % 2 * P : (n % 2 + 1) * P]
+
         def g_pass(b, n, a):
             if a == 0:
                 g_acc[b, n] = bank("g%d%d" % (b, n), [P, BANK])
             cols = slice(n * P, (n + 1) * P)
             nc.tensor.matmul_mx(
-                out=g_acc[b, n][:], lhsT=v2_w[a][:, cols].bitcast(FP8X4), lhsT_scale=(v2_s, v2_s_up)[a][:, cols],
+                out=g_acc[b, n][:], lhsT=v2_words(a, n).bitcast(FP8X4), lhsT_scale=v2_s[:, a * M + n * P : a * M + (n + 1) * P],
                 rhs=g_raw[b][:, a, :].bitcast(FP4X4),
                 rhs_scale=g_s[:, a * H + b * PASS : a * H + (b + 1) * PASS],
                 start=(a == 0), stop=(a == 1),
@@ -212,7 +248,7 @@ def tile_list_expense_overspend_signals_kernel(
             cols = slice(n * P, (n + 1) * P)
             for a in range(2):
                 nc.tensor.matmul_mx(
-                    out=acc[:], lhsT=v2_w[a][:, cols].bitcast(FP8X4), lhsT_scale=v2_s[4 * a :, cols],
+                    out=acc[:], lhsT=v2_words(a, n).bitcast(FP8X4), lhsT_scale=v2_s[:, a * M + n * P : a * M + (n + 1) * P],
                     rhs=c_raw[b][:, a, :].bitcast(FP8X4), rhs_scale=c_s[4:, a * H + b * PASS : a * H + (b + 1) * PASS],
                     start=(a == 0), stop=(a == 1),
                 )
@@ -242,7 +278,7 @@ def tile_list_expense_overspend_signals_kernel(
             return bf.rearrange("p (c i t) -> p c t i", i=4, t=PACK)
 
         def subtract(b, n):
-            if b == 0:
+            if n not in z_bf:
                 z_bf[n] = by("v", "z_bf%d" % n, [P, 2, PACK * PIECE], BF16)
             nc.vector.tensor_tensor(
                 woven(z_bf[n][:, b, :]), in_fours(turned[b, n][:]), in_fours(a_picked[b][:, :, n * PIECE : (n + 1) * PIECE]), SUB
@@ -254,7 +290,7 @@ def tile_list_expense_overspend_signals_kernel(
                 z_q[b, n] = codes[:, b * PIECE : (b + 1) * PIECE], scales[:, b * PIECE : (b + 1) * PIECE]
 
         def subtract_half(b, n):
-            if n % 2 == 0:
+            if (b, n // 2) not in z_bf:
                 z_bf[b, n // 2] = by("v", "z_bf%d%d" % (b, n), [P, 2, PACK * PIECE], BF16)
             nc.vector.tensor_tensor(
                 woven(z_bf[b, n // 2][:, n % 2, :]), in_fours(turned[b, n][:]), in_fours(a_picked[b][:, :, n * PIECE : (n + 1) * PIECE]), SUB
@@ -316,6 +352,16 @@ def tile_list_expense_overspend_signals_kernel(
                 y_bf[n] = by("v", "y_bf%d" % n, [P, PACK * PIECE], BF16)
             nc.vector.tensor_copy(woven(y_bf[n][:])[:, :, 2 * pair : 2 * pair + 2, :], in_fours(y_acc[n, pair][:]))
 
+        def y_last_round_by(n, pair, engine):
+            if n not in y_bf:
+                y_bf[n] = kept("y_bf%d" % n, [P, PACK * PIECE], BF16)
+            cast(engine, woven(y_bf[n][:])[:, :, 2 * pair : 2 * pair + 2, :], in_fours(y_acc[n, pair][:]))
+
+        def y_last_copy(n, pair, engine):
+            if n not in y_f:
+                y_f[n] = kept("y_f%d" % n, [P, 4, PIECE], F32)
+            cast(engine, y_f[n][:, 2 * pair : 2 * pair + 2, :], y_acc[n, pair][:])
+
         def y_last_out(n, pair):
             y_f[n, pair] = by("s", "y%d%d" % (n, pair), [P, 2, PIECE], F32)
             nc.scalar.copy(y_f[n, pair][:], y_acc[n, pair][:])
@@ -361,7 +407,7 @@ def tile_list_expense_overspend_signals_kernel(
         tab2_s = zeroed(nc.vector, "tab2_s", T)
         g_s = zeroed(nc.vector, "g_s", 2 * H)
         c_s = zeroed(nc.vector, "c_s", 2 * H)
-        v2_s_up = zeroed(nc.vector, "v2_s_up", M)
+        v2_s = zeroed(nc.vector, "v2_s", 2 * M)
         warm = kept("warm", [P, 8], F32)
         nc.vector.memset(warm[:, 0:1], 0.0)
         nc.scalar.activation(warm[:, 4:5], warm[:, 0:1], SILU)
@@ -380,31 +426,20 @@ def tile_list_expense_overspend_signals_kernel(
         nc.sync.dma_start(idx2[:], offs2)
         nc.sync.dma_start(heads[:], pos1)
         load_wa(0, 0)
+        load_spread_scales(tab2_s, tab2_scales)
         tab_w[1] = load_table(tab_words, 1, "tab_w1")
         load_wa(1, 0)
-        load_table_scales(nc.sync, tab2_s, tab2_scales)
         load_wa(0, 1)
         load_wa(1, 1)
-        tab2_w[0] = load_table(tab2_words, 0, "tab2_w0")
-        tab2_w[1] = load_table(tab2_words, 1, "tab2_w1", "picked1")
-        for h in range(2):
-            v_w[0, h] = gather("v_w0%d" % h, U32, tab_w[0], idx, h * BANK, (h + 1) * BANK)
-        v_s = gather("v_s", U8, tab_s, idx, 0, S)
-        round_wa(0, 0, 0, 2, "v")
-        round_wa(0, 0, 2, 4, "s")
-        quantise_wa(0, 0, 0)
-        quantise_wa(0, 0, 2)
-        for h in range(2):
-            v_w[1, h] = gather("v_w1%d" % h, U32, tab_w[1], idx, h * BANK, (h + 1) * BANK)
-        for t in range(4):
-            a_pass(0, t, 0)
-        round_wa(1, 0, 2, 4, "s")
-        round_wa(1, 0, 0, 2, "v")
-        quantise_wa(1, 0, 0)
-        quantise_wa(1, 0, 2)
-        v2_s = gather("v2_s", U8, tab2_s, idx2, 0, M)
-        nc.sync.dma_start(v2_s_up[:100, :].bitcast(I32), v2_s[4:104, :].bitcast(I32))
         load_weight_scales(nc.sync, g_s, 0, wg_scales)
+        v_w[0, 0] = gather("v_w00", U32, tab_w[0], idx, 0, BANK)
+        v_w[0, 1] = gather("v_w01", U32, tab_w[0], idx, BANK, S)
+        v_s = gather("v_s", U8, tab_s, idx, 0, S)
+        v2_picked = gather("v2_picked", U8, tab2_s, idx2, 0, M)
+        place_scales(v2_s, v2_picked, M, 0, 2)
+        tab2_w[0] = load_table(tab2_words, 0, "tab2_w0")
+        place_scales(v2_s, v2_picked, M, 2, 8)
+        tab2_w[1] = load_table(tab2_words, 1, "tab2_w1")
         load_g(0, 1)
         load_weight_scales(nc.sync, c_s, 4, wc_scales)
         load_c(0)
@@ -412,108 +447,132 @@ def tile_list_expense_overspend_signals_kernel(
         load_c(1)
         load_wo(0)
         load_wo(1)
-
-        round_wa(0, 1, 2, 4, "g")
-        a_pass(0, 0, 1)
-        a_row(0, 0)
-        a_pass(0, 1, 1)
-        a_row(0, 1)
-        a_pass(0, 2, 1)
-        a_row(0, 2)
-        a_pass(0, 3, 1)
-        pick(0, 0)
-        pick(0, 1)
-        quantise_wa(0, 1, 2)
-        round_wa(0, 1, 0, 2, "v")
-        pick(0, 2)
-        round_wa(1, 1, 2, 4, "s")
-        quantise_wa(0, 1, 0)
-        a_row(0, 3)
-        round_wa(1, 1, 0, 2, "s")
-        quantise_wa(1, 1, 2)
+        round_wa(0, 0, 0, 2, "s")
+        round_wa(0, 0, 2, 4, "g")
+        quantise_wa(0, 0, 0)
+        quantise_wa(0, 0, 2)
+        v_w[1, 0] = gather("v_w10", U32, tab_w[1], idx, 0, BANK)
+        v_w[1, 1] = gather("v_w11", U32, tab_w[1], idx, BANK, S)
+        a_pass(0,0,0)
+        a_pass(0,1,0)
+        a_pass(0,2,0)
+        a_pass(0,3,0)
+        round_wa(1, 0, 2, 4, "s")
+        round_wa(1, 0, 0, 2, "v")
+        quantise_wa(1, 0, 0)
+        quantise_wa(1, 0, 2)
+        round_wa(0,1,2,4,"g")
+        round_wa(0,1,0,2,"g")
+        a_pass(0,0,1)
+        a_row(0,0,"sv")
+        a_pass(0,1,1)
+        a_row(0,1)
+        a_pass(0,2,1)
+        a_row(0,2)
+        a_pass(0,3,1)
+        round_wa(1,1,2,4,"s")
+        a_row(0,3)
+        round_wa(1,1,0,2,"s")
+        pick(0,0)
+        pick(0,1)
+        quantise_wa(0,1,2)
+        pick(0,2)
+        quantise_wa(0,1,0)
+        quantise_wa(1,1,2)
+        pick(0,3)
+        quantise_wa(1,1,0)
         v2_w[0] = gather("v2_w0", U32, tab2_w[0], idx2, 0, M)
-        pick(0, 3)
-        quantise_wa(1, 1, 0)
-        v2_w[1] = gather("v2_w1", U32, tab2_w[1], idx2, 0, M)
-        a_pass(1, 2, 0)
-        a_pass(1, 3, 0)
-        a_pass(1, 0, 0)
-        a_pass(1, 2, 1)
-        a_row(1, 2)
-        a_pass(1, 3, 1)
-        a_row(1, 3)
-        a_pass(1, 1, 0)
-        a_pass(1, 0, 1)
-        a_row(1, 0)
-        a_pass(1, 1, 1)
-        a_row(1, 1)
-        gate(0, 0)
-        gate(0, 1)
-        g_pass(0, 2, 0)
-        g_pass(0, 2, 1)
-        pick(1, 2)
-        pick(1, 3)
-        pick(1, 0)
-        pick(1, 1)
-        c_tile(0, 0)
-        product_g(0, 0)
-        silu(0, 2)
-        c_tile(0, 1)
-        c_tile(0, 2)
-        product(0, 1)
-        product(0, 2)
-        gate(1, 0)
-        gate(1, 1)
-        c_tile(1, 0)
-        c_tile(1, 1)
-        product(1, 0)
-        product(1, 1)
-        round_wo(0, 0, 4, "g")
-        turn(0, 0)
-        turn(0, 1)
-        gate(1, 2)
-        turn(1, 0)
-        turn(1, 1)
-        c_tile(1, 2)
-        round_wo(1, 0, 2, "s")
-        round_wo(1, 2, 4, "s")
-        both(gate, 3)
-        subtract(0, 0)
-        subtract(0, 1)
-        subtract(1, 0)
-        subtract(1, 1)
-        product(1, 2)
-        both(c_tile, 3)
-        both(turn, 2)
-        quantise_wo(0, 0)
+        a_pass(1,2,0)
+        a_pass(1,3,0)
+        a_pass(1,0,0)
+        a_pass(1,2,1)
+        a_row(1,2)
+        a_pass(1,3,1)
+        a_row(1,3)
+        a_pass(1,1,0)
+        a_pass(1,0,1)
+        a_row(1,0)
+        a_pass(1,1,1)
+        a_row(1,1)
+        gather_v2(1,0)
+        gather_v2(1,1,"picked1")
+        gate(0,0)
+        g_pass(0,1,0)
+        g_pass(0,1,1)
+        g_pass(0,2,0)
+        g_pass(0,2,1)
+        pick(1,2)
+        pick(1,3)
+        pick(1,0)
+        pick(1,1)
+        c_tile(0,0)
+        product_g(0,0)
+        silu(0,1)
+        c_tile(0,1)
+        product_g(0,1)
+        silu(0,2)
+        c_tile(0,2)
+        product(0,2)
+        gate(1,0)
+        gate(1,1)
+        c_tile(1,0)
+        c_tile(1,1)
+        product(1,0)
+        product(1,1)
+        round_wo(0,0,4,"g")
+        turn(0,0)
+        turn(0,2)
+        gate(1,2)
+        turn(1,0)
+        turn(0,1)
+        turn(1,1)
+        c_tile(1,2)
+        round_wo(1,0,2,"s")
+        round_wo(1,2,4,"s")
+        both(gate,3)
+        subtract(0,0)
+        subtract(0,2)
+        subtract(1,0)
+        subtract(0,1)
+        subtract(1,1)
+        product(1,2)
+        turn(1,2)
+        both(c_tile,3)
+        quantise_wo(0,0)
         quantise_z(0)
         quantise_z(1)
-        quantise_wo(1, 0)
-        quantise_wo(1, 2)
-        both(product, 3)
-        both(subtract, 2)
+        quantise_wo(1,0)
+        quantise_wo(1,2)
+        subtract(1,2)
         y(0)
         y_store(0)
-        y_round(0, "s")
-        both(turn, 3)
+        product(0,3)
+        product(1,3)
+        quantise_z(2)
         y(1)
         y_store(1)
-        y_round(1, "s")
-        quantise_z(2)
-        subtract_one(0, 3)
-        subtract_one(1, 3)
-        quantise_one(0, 3)
+        y_round(0,"s")
+        turn(0,3)
+        turn(1,3)
         y(2)
         y_store(2)
+        y_round(1,"g")
+        subtract_one(0,3)
+        subtract_one(1,3)
+        quantise_one(0,3)
         y_planes(0)
-        quantise_one(1, 3)
-        y(3)
-        y_store(3)
+        quantise_one(1,3)
         y_planes(1)
-        store_words(0, 2)
-        y_round(2, "v")
-        y_round(3, "v")
+        y_round(2,"s")
+        y_last(3,0)
+        y_last(3,1)
+        store_words(0,2)
+        y_last_round_by(3,1,"v")
+        y_last_round_by(3,0,"s")
+        y_last_copy(3,0,"s")
+        y_last_copy(3,1,"v")
+        y_store(3)
         y_planes(2)
         y_planes(3)
-        store_words(2, 4)
+        store_words(2,4)
         store_scales()

from contextlib import ExitStack

import concourse.mybir as mybir
from concourse.masks import make_identity

K, T, S, M, H, N = 1024, 2048, 1024, 512, 1024, 512
FLOPS = 2 * K * H * S + 2 * 2 * K * H * M + 2 * H * N * M

F32 = mybir.dt.float32
BF16 = mybir.dt.bfloat16
I32 = mybir.dt.int32
U32 = mybir.dt.uint32
U16 = mybir.dt.uint16
U8 = mybir.dt.uint8
FP8X4 = mybir.dt.float8_e4m3fn_x4
FP4X4 = mybir.dt.float4_e2m1fn_x4
MULT = mybir.AluOpType.mult
ADD = mybir.AluOpType.add
SUB = mybir.AluOpType.subtract
SILU = mybir.ActivationFunctionType.Silu

P = 128
PACK = 4
PASS = P * PACK
BANK = 512
PIECE = 128
G_PARTS = 1
BUFS = {"v": 14, "s": 12, "g": 4, "cd": 1, "loaded": 7, "picked0": 1, "picked1": 2}


def tile_list_expense_overspend_signals_kernel(
    tc, tab_words, tab_scales, offs, pos1, tab2_words, tab2_scales, offs2,
    wa, wg_words, wg_scales, wc_words, wc_scales, wo, out_0, out_1, out_2,
):
    nc = tc.nc
    with ExitStack() as ctx:
        lists = ctx.enter_context(tc.tile_pool(name="lists", bufs=1))
        keep = ctx.enter_context(tc.tile_pool(name="keep", bufs=1))
        psum = ctx.enter_context(tc.psum_pool(name="psum", bufs=8))

        def kept(name, shape, dtype):
            return keep.tile(shape, dtype, name=name, tag=name, bufs=1, align_bytes=64)

        def by(tag, name, shape, dtype):
            return keep.tile(shape, dtype, name=name, tag=tag, bufs=BUFS[tag], align_bytes=64)

        def bank(name, shape):
            return psum.tile(shape, F32, name=name, tag="bank")

        idx = lists.tile([P, S // 16], U16, name="idx")
        idx2 = lists.tile([P, M // 16], U16, name="idx2")
        heads = lists.tile([P, M // 16], U16, name="heads")

        def zeroed(engine, name, width):
            tile = kept(name, [P, width], U8)
            engine.memset(tile[:].bitcast(I32), 0)
            return tile

        def load_table_scales(queue, tile, scales):
            for q in range(4):
                queue.dma_start(tile[32 * q : 32 * q + 8, :].bitcast(I32), scales[:, 4 * q : 4 * q + 4, :].bitcast(I32))

        def load_weight_scales(queue, tile, first, scales):
            rows = scales.bitcast(I32).rearrange("a (q r) e -> r q a e", r=4)
            for r in range(4):
                queue.dma_start(tile[first + r : P : 32, :].bitcast(I32).rearrange("q (a e) -> q a e", a=2), rows[r])

        def load_spread_scales(tile, scales):
            nc.sync.dma_start(tile[0:P:4, :].bitcast(I32), scales.rearrange("a j e -> (a j) e").bitcast(I32))

        def place_scales(plane, picked, width, lo, hi):
            for move in range(lo, hi):
                a, r = divmod(move, 4)
                first = 64 * a + 4 * r
                nc.sync.dma_start(plane[r:P:32, a * width : (a + 1) * width].bitcast(I32), picked[first : first + 49 : 16, :].bitcast(I32))

        def load_table(words, a, name, tag="loaded"):
            tile = by(tag, name, [P, T], U32)
            nc.sync.dma_start(tile[:].bitcast(I32), words[a].rearrange("p t i -> p (t i)").bitcast(I32))
            return tile

        def load_wa(a, b):
            raw = by("loaded", "wa%d%d" % (a, b), [P, PACK, PASS], F32)
            rows = wa[a * PASS : (a + 1) * PASS, b * PASS : (b + 1) * PASS]
            nc.sync.dma_start(raw[:], rows.rearrange("(p i) r -> p i r", i=PACK))
            wa_raw[a, b] = raw

        def load_wo(b):
            raw = by("loaded", "wo%d" % b, [P, PACK, N], F32)
            nc.sync.dma_start(raw[:], wo[b * PASS : (b + 1) * PASS, :].rearrange("(p t) n -> p t n", t=PACK))
            wo_raw[b] = raw

        def load_g(lo, hi):
            raw = kept("g_raw%d" % lo, [P, 2, (hi - lo) * PASS // 2], I32)
            nc.sync.dma_start(raw[:], wg_words.bitcast(I32)[:, :, lo * PASS // 2 : hi * PASS // 2].rearrange("a p e -> p a e"))
            for b in range(lo, hi):
                g_raw[b] = raw[:, :, (b - lo) * PASS // 2 : (b - lo + 1) * PASS // 2]

        def load_c(b):
            raw = kept("c_raw%d" % b, [P, 2, PASS], I32)
            c_src = wc_words.rearrange("a p e i -> a p (e i)").bitcast(I32)[:, :, b * PASS : (b + 1) * PASS]
            nc.sync.dma_start(raw[:], c_src.rearrange("a p e -> p a e"))
            c_raw[b] = raw

        def gather(name, dtype, window, offsets, lo, hi, tag="v"):
            picked = by(tag, name, [P, hi - lo], dtype)
            nc.vector.tensor_copy(picked[:], window[:].indirect(offsets[:, lo // 16 : hi // 16]))
            return picked

        def gather_v2(a, half, tag="v"):
            lo = half * M // 2
            v2_w[a, half] = gather("v2_w%d%d" % (a, half), U32, tab2_w[a], idx2, lo, lo + M // 2, tag)

        def quantise(name, src):
            width = src.shape[1] // PACK
            codes = by("v", name + "_w", [P, width], U32)
            scales = kept(name + "_s", [P, width], U8)
            nc.vector.quantize_mx(out=codes[:].bitcast(FP8X4), scales=scales[:], in_=src)
            return codes, scales

        def cast(engine, dst, src):
            if engine == "s":
                nc.scalar.copy(dst, src)
            elif engine == "v":
                nc.vector.tensor_copy(dst, src)
            else:
                nc.gpsimd.tensor_scalar(dst, src, 1.0, 0.0, MULT, ADD)

        def round_wa(a, b, lo, hi, engine, tag=None):
            bf = by(tag or engine, "wa_bf%d%d%d" % (a, b, lo), [P, (hi - lo) * PASS], BF16)
            dst = bf[:].rearrange("p (t q i) -> p q i t", t=hi - lo, i=PACK)
            src = wa_raw[a, b][:].rearrange("p i (q t) -> p q i t", t=4)
            for t in range(lo, hi, 2):
                pair_dst, pair_src = dst[:, :, :, t - lo : t - lo + 2], src[:, :, :, t : t + 2]
                if engine == "g":
                    pair_dst, pair_src = pair_dst.rearrange("p q i t -> p q t i"), pair_src.rearrange("p q i t -> p q t i")
                cast(engine, pair_dst, pair_src)
            wa_bf[a, b, lo] = bf, hi

        def round_wa_shared(a, b, lo, split):
            bf = by("s", "wa_bf%d%d%d" % (a, b, lo), [P, 2 * PASS], BF16)
            dst = bf[:].rearrange("p (t q i) -> p q i t", t=2, i=PACK)
            src = wa_raw[a, b][:].rearrange("p i (q t) -> p q i t", t=4)[:, :, :, lo : lo + 2]
            cast("s", dst[:, split:], src[:, split:])
            cast("v", dst[:, :split], src[:, :split])
            wa_bf[a, b, lo] = bf, lo + 2

        def quantise_wa_tile(a, b, lo, t):
            bf, hi = wa_bf[a, b, lo]
            codes, scales = quantise("wa%d%d%d" % (a, b, t), bf[:, (t - lo) * PASS : (t - lo + 1) * PASS])
            wa_q[a, b, t] = codes[:], scales[:]

        def quantise_wa(a, b, lo):
            bf, hi = wa_bf[a, b, lo]
            codes, scales = quantise("wa%d%d%d" % (a, b, lo), bf[:])
            for t in range(lo, hi):
                cols = slice((t - lo) * P, (t - lo + 1) * P)
                wa_q[a, b, t] = codes[:, cols], scales[:, cols]

        def round_wo(b, lo, hi, engine):
            bf = by(engine, "wo_bf%d%d" % (b, lo), [P, (hi - lo) * PASS], BF16)
            if engine == "g":
                dst = bf[:].rearrange("p (u c t) -> p c u t", u=hi - lo, t=4)
                src = wo_raw[b][:].rearrange("p t (c u) -> p c u t", u=4)
                for part in range(2):
                    cols = slice(part * 64, (part + 1) * 64)
                    cast(engine, dst[:, cols], src[:, cols, lo:hi])
            else:
                dst = bf[:].rearrange("p (u c t) -> p c t u", u=hi - lo, t=4)
                src = wo_raw[b][:].rearrange("p t (c u) -> p c t u", u=4)
                cast(engine, dst, src[:, :, :, lo:hi])
            wo_bf[b, lo] = bf, hi

        def quantise_wo(b, lo):
            bf, hi = wo_bf[b, lo]
            codes, scales = quantise("wo%d%d" % (b, lo), bf[:])
            for u in range(lo, hi):
                cols = slice((u - lo) * P, (u - lo + 1) * P)
                wo_q[b, u] = codes[:, cols], scales[:, cols]

        def a_pass(b, t, a):
            codes, scales = wa_q[a, b, t]
            for h in range(2):
                if a == 0:
                    a_acc[b, t, h] = bank("a%d%d%d" % (b, t, h), [P, BANK])
                nc.tensor.matmul_mx(
                    out=a_acc[b, t, h][:], lhsT=codes.bitcast(FP8X4), lhsT_scale=scales,
                    rhs=v_w[a, h][:].bitcast(FP8X4), rhs_scale=v_s[4 * a :, h * BANK : (h + 1) * BANK],
                    start=(a == 0), stop=(a == 1),
                )

        def a_row(b, t, who="ss"):
            row = by("s", "row%d%d" % (b, t), [P, S], F32)
            for h in range(2):
                cast(who[h], row[:, h * BANK : (h + 1) * BANK], a_acc[b, t, h][:])
            rows[b, t] = row

        def a_half_row(b, t, h, engine):
            if (b, t) not in rows:
                rows[b, t] = by("s", "row%d%d" % (b, t), [P, S], F32)
            cast(engine, rows[b, t][:, h * BANK : (h + 1) * BANK], a_acc[b, t, h][:])

        def a_tile(b, t):
            a_pass(b, t, 0)
            a_pass(b, t, 1)
            a_row(b, t)

        def pick(b, t, lo=0, hi=M):
            if b not in a_picked:
                a_picked[b] = by("picked%d" % b, "a_picked%d" % b, [P, 4, M], F32)
            nc.vector.tensor_copy(a_picked[b][:, t, lo:hi], rows[b, t][:].indirect(heads[:, lo // 16 : hi // 16]))

        def dealt(ap):
            return ap.rearrange("p (c i t) -> p c t i", t=4, i=4)

        def in_tiles(ap):
            return ap.rearrange("p (t c i) -> p c t i", t=4, i=4)

        def v2_words(a, n):
            if a in v2_w:
                return v2_w[a][:, n * P : (n + 1) * P]
            return v2_w[a, n // 2][:, n % 2 * P : (n % 2 + 1) * P]

        def g_pass(b, n, a):
            if a == 0:
                g_acc[b, n] = bank("g%d%d" % (b, n), [P, BANK])
            cols = slice(n * P, (n + 1) * P)
            nc.tensor.matmul_mx(
                out=g_acc[b, n][:], lhsT=v2_words(a, n).bitcast(FP8X4), lhsT_scale=v2_s[:, a * M + n * P : a * M + (n + 1) * P],
                rhs=g_raw[b][:, a, :].bitcast(FP4X4),
                rhs_scale=g_s[:, a * H + b * PASS : a * H + (b + 1) * PASS],
                start=(a == 0), stop=(a == 1),
            )

        def gate(b, n):
            if (b, n) not in g_acc:
                g_pass(b, n, 0)
            g_pass(b, n, 1)
            silu(b, n)

        def silu(b, n):
            acc = g_acc[b, n]
            gates[b, n] = by("s", "gate%d%d" % (b, n), [P, PASS], F32)
            nc.scalar.activation(in_tiles(gates[b, n][:]), dealt(acc[:]), SILU)

        def c_tile(b, n):
            acc = bank("c%d%d" % (b, n), [P, BANK])
            cols = slice(n * P, (n + 1) * P)
            for a in range(2):
                nc.tensor.matmul_mx(
                    out=acc[:], lhsT=v2_words(a, n).bitcast(FP8X4), lhsT_scale=v2_s[:, a * M + n * P : a * M + (n + 1) * P],
                    rhs=c_raw[b][:, a, :].bitcast(FP8X4), rhs_scale=c_s[4:, a * H + b * PASS : a * H + (b + 1) * PASS],
                    start=(a == 0), stop=(a == 1),
                )
            c_acc[b, n] = acc

        def product(b, n):
            sc[b, n] = by("v", "sc%d%d" % (b, n), [P, PASS], F32)
            nc.vector.tensor_tensor(in_tiles(sc[b, n][:]), dealt(c_acc[b, n][:]), in_tiles(gates[b, n][:]), MULT)

        def product_g(b, n):
            c_f = by("s", "c_f%d%d" % (b, n), [P, PASS], F32)
            nc.scalar.copy(in_tiles(c_f[:]), dealt(c_acc[b, n][:]))
            sc[b, n] = by("g", "sc%d%d" % (b, n), [P, PASS], F32)
            for h in range(G_PARTS):
                cols = slice(h * PASS // G_PARTS, (h + 1) * PASS // G_PARTS)
                nc.gpsimd.tensor_tensor(sc[b, n][:, cols], c_f[:, cols], gates[b, n][:, cols], MULT)

        def turn(b, n):
            turned[b, n] = bank("T%d%d" % (b, n), [P, 4, PIECE])
            for t in range(4):
                nc.tensor.transpose(turned[b, n][:, t, :], sc[b, n][:, t * P : (t + 1) * P], ident[:])

        def in_fours(planes):
            return planes.rearrange("p t (c i) -> p c t i", i=4)

        def woven(bf):
            return bf.rearrange("p (c i t) -> p c t i", i=4, t=PACK)

        def subtract(b, n):
            if n not in z_bf:
                z_bf[n] = by("v", "z_bf%d" % n, [P, 2, PACK * PIECE], BF16)
            nc.vector.tensor_tensor(
                woven(z_bf[n][:, b, :]), in_fours(turned[b, n][:]), in_fours(a_picked[b][:, :, n * PIECE : (n + 1) * PIECE]), SUB
            )

        def quantise_z(n):
            codes, scales = quantise("z%d" % n, z_bf[n][:].rearrange("p b c -> p (b c)"))
            for b in range(2):
                z_q[b, n] = codes[:, b * PIECE : (b + 1) * PIECE], scales[:, b * PIECE : (b + 1) * PIECE]

        def subtract_half(b, n):
            if (b, n // 2) not in z_bf:
                z_bf[b, n // 2] = by("v", "z_bf%d%d" % (b, n), [P, 2, PACK * PIECE], BF16)
            nc.vector.tensor_tensor(
                woven(z_bf[b, n // 2][:, n % 2, :]), in_fours(turned[b, n][:]), in_fours(a_picked[b][:, :, n * PIECE : (n + 1) * PIECE]), SUB
            )

        def quantise_pair(b, pair):
            codes, scales = quantise("z%d%d" % (b, pair), z_bf[b, pair][:].rearrange("p n c -> p (n c)"))
            for i in range(2):
                z_q[b, 2 * pair + i] = codes[:, i * PIECE : (i + 1) * PIECE], scales[:, i * PIECE : (i + 1) * PIECE]

        def subtract_one(b, n):
            z_bf[b, n, 1] = by("v", "z_bf%d%d" % (b, n), [P, PACK * PIECE], BF16)
            nc.vector.tensor_tensor(
                woven(z_bf[b, n, 1][:]), in_fours(turned[b, n][:]), in_fours(a_picked[b][:, :, n * PIECE : (n + 1) * PIECE]), SUB
            )

        def quantise_one(b, n):
            codes, scales = quantise("z%d%d" % (b, n), z_bf[b, n, 1][:])
            z_q[b, n] = codes[:], scales[:]

        def y_half(b, n, first):
            if first:
                y_acc[n] = bank("y%d" % n, [P, 4, PIECE])
            for u in range(4):
                nc.tensor.matmul_mx(
                    out=y_acc[n][:, u, :], lhsT=wo_q[b, u][0].bitcast(FP8X4), lhsT_scale=wo_q[b, u][1],
                    rhs=z_q[b, n][0].bitcast(FP8X4), rhs_scale=z_q[b, n][1],
                    start=(first and u == 0), stop=(not first and u == 3),
                )

        def y_out(n):
            y_f[n] = by("s", "y%d" % n, [P, 4, PIECE], F32)
            nc.scalar.copy(y_f[n][:], y_acc[n][:])

        def y_store(n):
            nc.sync.dma_start(y_rows[:, :, n * PIECE : (n + 1) * PIECE], y_f[n][:])

        def y_round(n, engine):
            y_bf[n] = by(engine, "y_bf%d" % n, [P, PACK * PIECE], BF16)
            if engine == "g":
                cast(engine, y_bf[n][:].rearrange("p (c t) -> p c t", t=PACK), y_f[n][:].rearrange("p t c -> p c t"))
            else:
                cast(engine, woven(y_bf[n][:]), in_fours(y_f[n][:]))

        def y_last(n, b):
            for pair in range(2):
                if b == 0:
                    y_acc[n, pair] = bank("y%d%d" % (n, pair), [P, 2, PIECE])
                for u in range(2):
                    codes, scales = wo_q[b, 2 * pair + u]
                    nc.tensor.matmul_mx(
                        out=y_acc[n, pair][:, u, :], lhsT=codes.bitcast(FP8X4), lhsT_scale=scales,
                        rhs=z_q[b, n][0].bitcast(FP8X4), rhs_scale=z_q[b, n][1],
                        start=(b == 0 and u == 0), stop=(b == 1 and u == 1),
                    )

        def y_last_round(n, pair):
            if n not in y_bf:
                y_bf[n] = by("v", "y_bf%d" % n, [P, PACK * PIECE], BF16)
            nc.vector.tensor_copy(woven(y_bf[n][:])[:, :, 2 * pair : 2 * pair + 2, :], in_fours(y_acc[n, pair][:]))

        def y_last_round_by(n, pair, engine):
            if n not in y_bf:
                y_bf[n] = kept("y_bf%d" % n, [P, PACK * PIECE], BF16)
            cast(engine, woven(y_bf[n][:])[:, :, 2 * pair : 2 * pair + 2, :], in_fours(y_acc[n, pair][:]))

        def y_last_copy(n, pair, engine):
            if n not in y_f:
                y_f[n] = kept("y_f%d" % n, [P, 4, PIECE], F32)
            cast(engine, y_f[n][:, 2 * pair : 2 * pair + 2, :], y_acc[n, pair][:])

        def y_last_out(n, pair):
            y_f[n, pair] = by("s", "y%d%d" % (n, pair), [P, 2, PIECE], F32)
            nc.scalar.copy(y_f[n, pair][:], y_acc[n, pair][:])
            nc.sync.dma_start(y_rows[:, 2 * pair : 2 * pair + 2, n * PIECE : (n + 1) * PIECE], y_f[n, pair][:])

        def y_round_psum(n):
            y_bf[n] = by("v", "y_bf%d" % n, [P, PACK * PIECE], BF16)
            nc.vector.tensor_copy(woven(y_bf[n][:]), in_fours(y_acc[n][:]))

        def y_round_first(n):
            y_bf[n] = by("s", "y_bf%d" % n, [P, PACK * PIECE], BF16)
            nc.scalar.copy(woven(y_bf[n][:]), in_fours(y_acc[n][:]))

        def y_out_half(n, pair):
            y_f[n, pair] = by("s", "y%d%d" % (n, pair), [P, 2, PIECE], F32)
            nc.scalar.copy(y_f[n, pair][:], y_acc[n][:, 2 * pair : 2 * pair + 2, :])

        def y_store_half(n, pair):
            nc.sync.dma_start(y_rows[:, 2 * pair : 2 * pair + 2, n * PIECE : (n + 1) * PIECE], y_f[n, pair][:])

        def y_planes(n):
            lo, hi = n * PIECE, (n + 1) * PIECE
            nc.vector.quantize_mx(out=y_w[:, lo:hi].bitcast(FP8X4), scales=y_s[:, lo:hi], in_=y_bf[n][:])

        def store_words(lo, hi):
            nc.sync.dma_start(y_words[:, lo * PIECE : hi * PIECE], y_w[:, lo * PIECE : hi * PIECE].bitcast(I32))

        def store_scales():
            for q in range(4):
                SCALE_QUEUES[q].dma_start(out_2[0, 4 * q : 4 * q + 4, :].bitcast(I32), y_s[32 * q : 32 * q + 4, :].bitcast(I32))

        SCALE_QUEUES = (nc.scalar, nc.sync, nc.scalar, nc.sync)
        v_w, v2_w, tab_w, tab2_w, wa_raw, wa_bf, wa_q, wo_raw, wo_bf, wo_q, c_raw = {}, {}, {}, {}, {}, {}, {}, {}, {}, {}, {}
        a_acc, rows, a_picked, gates, c_acc, sc, turned, z_bf, z_q, y_acc, y_f, y_bf = {}, {}, {}, {}, {}, {}, {}, {}, {}, {}, {}, {}
        g_raw, g_acc = {}, {}
        y_rows = out_0.rearrange("(p u) m -> p u m", u=4)
        y_words = out_1[0].rearrange("p m t -> p (m t)").bitcast(I32)
        y_w = kept("y_w", [P, M], U32)
        y_s = kept("y_s", [P, M], U8)

        ident = kept("ident", [P, P], F32)
        tab_s = zeroed(nc.vector, "tab_s", T)
        tab2_s = zeroed(nc.vector, "tab2_s", T)
        g_s = zeroed(nc.vector, "g_s", 2 * H)
        c_s = zeroed(nc.vector, "c_s", 2 * H)
        v2_s = zeroed(nc.vector, "v2_s", 2 * M)
        warm = kept("warm", [P, 8], F32)
        nc.vector.memset(warm[:, 0:1], 0.0)
        nc.scalar.activation(warm[:, 4:5], warm[:, 0:1], SILU)
        make_identity(nc, ident[:])
        def both(f, n):
            for b in range(2):
                f(b, n)
        def y(n):
            y_half(0, n, True)
            y_half(1, n, False)
            y_out(n)

        nc.sync.dma_start(idx[:], offs)
        tab_w[0] = load_table(tab_words, 0, "tab_w0")
        load_table_scales(nc.sync, tab_s, tab_scales)
        nc.sync.dma_start(idx2[:], offs2)
        nc.sync.dma_start(heads[:], pos1)
        load_wa(0, 0)
        load_spread_scales(tab2_s, tab2_scales)
        tab_w[1] = load_table(tab_words, 1, "tab_w1")
        load_wa(1, 0)
        load_wa(0, 1)
        load_wa(1, 1)
        load_weight_scales(nc.sync, g_s, 0, wg_scales)
        v_w[0, 0] = gather("v_w00", U32, tab_w[0], idx, 0, BANK)
        v_w[0, 1] = gather("v_w01", U32, tab_w[0], idx, BANK, S)
        v_s = gather("v_s", U8, tab_s, idx, 0, S)
        v2_picked = gather("v2_picked", U8, tab2_s, idx2, 0, M)
        place_scales(v2_s, v2_picked, M, 0, 2)
        tab2_w[0] = load_table(tab2_words, 0, "tab2_w0")
        place_scales(v2_s, v2_picked, M, 2, 8)
        tab2_w[1] = load_table(tab2_words, 1, "tab2_w1")
        load_g(0, 1)
        load_weight_scales(nc.sync, c_s, 4, wc_scales)
        load_c(0)
        load_g(1, 2)
        load_c(1)
        load_wo(0)
        load_wo(1)
        round_wa(0, 0, 0, 2, "s")
        round_wa(0, 0, 2, 4, "g")
        quantise_wa(0, 0, 0)
        quantise_wa(0, 0, 2)
        v_w[1, 0] = gather("v_w10", U32, tab_w[1], idx, 0, BANK)
        v_w[1, 1] = gather("v_w11", U32, tab_w[1], idx, BANK, S)
        a_pass(0,0,0)
        a_pass(0,1,0)
        a_pass(0,2,0)
        a_pass(0,3,0)
        round_wa(1, 0, 2, 4, "s")
        round_wa(1, 0, 0, 2, "v")
        quantise_wa(1, 0, 0)
        quantise_wa(1, 0, 2)
        round_wa(0,1,2,4,"g")
        round_wa(0,1,0,2,"g")
        a_pass(0,0,1)
        a_row(0,0,"sv")
        a_pass(0,1,1)
        a_row(0,1)
        a_pass(0,2,1)
        a_row(0,2)
        a_pass(0,3,1)
        round_wa(1,1,2,4,"s")
        a_row(0,3)
        round_wa(1,1,0,2,"s")
        pick(0,0)
        pick(0,1)
        quantise_wa(0,1,2)
        pick(0,2)
        quantise_wa(0,1,0)
        quantise_wa(1,1,2)
        pick(0,3)
        quantise_wa(1,1,0)
        v2_w[0] = gather("v2_w0", U32, tab2_w[0], idx2, 0, M)
        a_pass(1,2,0)
        a_pass(1,3,0)
        a_pass(1,0,0)
        a_pass(1,2,1)
        a_row(1,2)
        a_pass(1,3,1)
        a_row(1,3)
        a_pass(1,1,0)
        a_pass(1,0,1)
        a_row(1,0)
        a_pass(1,1,1)
        a_row(1,1)
        gather_v2(1,0)
        gather_v2(1,1,"picked1")
        gate(0,0)
        g_pass(0,1,0)
        g_pass(0,1,1)
        g_pass(0,2,0)
        g_pass(0,2,1)
        pick(1,2)
        pick(1,3)
        pick(1,0)
        pick(1,1)
        c_tile(0,0)
        product_g(0,0)
        silu(0,1)
        c_tile(0,1)
        product_g(0,1)
        silu(0,2)
        c_tile(0,2)
        product(0,2)
        gate(1,0)
        gate(1,1)
        c_tile(1,0)
        c_tile(1,1)
        product(1,0)
        product(1,1)
        round_wo(0,0,4,"g")
        turn(0,0)
        turn(0,2)
        gate(1,2)
        turn(1,0)
        turn(0,1)
        turn(1,1)
        c_tile(1,2)
        round_wo(1,0,2,"s")
        round_wo(1,2,4,"s")
        both(gate,3)
        subtract(0,0)
        subtract(0,2)
        subtract(1,0)
        subtract(0,1)
        subtract(1,1)
        product(1,2)
        turn(1,2)
        both(c_tile,3)
        quantise_wo(0,0)
        quantise_z(0)
        quantise_z(1)
        quantise_wo(1,0)
        quantise_wo(1,2)
        subtract(1,2)
        y(0)
        y_store(0)
        product(0,3)
        product(1,3)
        quantise_z(2)
        y(1)
        y_store(1)
        y_round(0,"s")
        turn(0,3)
        turn(1,3)
        y(2)
        y_store(2)
        y_round(1,"g")
        subtract_one(0,3)
        subtract_one(1,3)
        quantise_one(0,3)
        y_planes(0)
        quantise_one(1,3)
        y_planes(1)
        y_round(2,"s")
        y_last(3,0)
        y_last(3,1)
        store_words(0,2)
        y_last_round_by(3,1,"v")
        y_last_round_by(3,0,"s")
        y_last_copy(3,0,"s")
        y_last_copy(3,1,"v")
        y_store(3)
        y_planes(2)
        y_planes(3)
        store_words(2,4)
        store_scales()
